import numpy as np, ml_dtypes
CORES = [16,32,48,64,80]
N = 5
BF = ml_dtypes.bfloat16
def gentries(a):
    return np.ascontiguousarray(a.reshape(8, 16, -1).transpose(0, 2, 1)).reshape(8, -1)
def gtable(e):
    e = np.asarray(e); return np.ascontiguousarray(e.reshape(8, -1, 16).transpose(0, 2, 1)).reshape(128, -1).astype(np.int32)
S, LEN, RO = 768, 18, 3
W = N * S
FARTHEST = 2 ** 23
def parts(rng):
    own = S * np.arange(N)[:, None, None, None] + np.arange(S)[None, None, :, None]
    sc = np.exp2(3 + (np.log2(W) - 3.5) * rng.random((N, 8, 1, 16)))
    rf = (own + np.rint(sc * rng.standard_normal((N, 8, S, 16))).astype(np.int64)) % W
    hi = rng.integers(40, 256, (N, 8, 16, 1)); sz = 16 + (rng.random((N, 8, 16, S)) * (hi - 15)).astype(np.int64)
    lim = 135 * sc * np.where(sc > S // 2, 8, 1) * np.exp2(2 * rng.random((N, 8, 1, 16))) * (0.8 + 0.4 * rng.random((N, 8, 16, 16)))
    return np.minimum(sz, 255), rf, np.minimum(lim.astype(np.int64), FARTHEST)
def kinds(rng, fold, decoy, chain, strange):
    u = rng.random((N, 8, S)); k = np.where(u < fold, rng.integers(1, RO + 1, u.shape), 0); lo = fold
    for share, c in ((decoy, RO + 1), (chain, RO + 2), (strange, RO + 3)):
        k = np.where((u >= lo) & (u < lo + share), c, k); lo = lo + share
    k[..., S - RO:] = np.argsort(rng.random((N, 8, RO)), axis=-1) + 1; k[..., 0] = 0
    return k
def weave(rng, rf, kind, first=False):
    n = np.arange(S)
    def earlier(ok):
        order = np.argsort(~ok, axis=-1, kind="stable"); cnt = np.add.accumulate(ok.astype(np.int64), axis=-1) - ok
        j = np.minimum((rng.random(ok.shape) * cnt).astype(np.int64), np.maximum(cnt - 1, 0))
        return np.where(cnt > 0, np.take_along_axis(order, j, -1), n)
    def of(a, i): return np.take_along_axis(a, i[..., None], 2)
    rf = rf.copy(); m = (kind >= 1) & (kind <= RO); dec = kind == RO + 1
    root = np.zeros(kind.shape, np.int64) if first else earlier(kind == 0)
    cd = np.where(m | dec | (kind == RO + 3), root, n)
    cdw = (cd + S * np.arange(N)[:, None, None]).transpose(1, 0, 2).reshape(8, W)
    pos = np.ascontiguousarray(np.argsort(rng.random((N, 8, S, 16)), axis=-1)[..., :RO - 1]); x = np.zeros((N, 8, S, RO - 1), np.int64)
    for g in range(8):
        flat = kind[:, g].reshape(-1)
        for l in range(1, RO): x[:, g, :, l - 1] = rng.choice(np.flatnonzero(flat == l), (N, S))
    y = cdw[np.arange(8)[None, :, None, None], x]
    flip = rng.random(x.shape) < 0.4; x, y = np.where(flip, y, x), np.where(flip, x, y)
    np.put_along_axis(rf, pos, np.where((kind == 0)[..., None], y, np.take_along_axis(rf, pos, -1)), -1)
    base, bp, bx = of(rf, cd), of(pos, cd), of(x, cd)
    for l in range(1, RO):
        use = m & ((kind == l + 1) | ((kind > l + 1) & (rng.random(kind.shape) < 0.5))); p = bp[..., l - 1:l]
        np.put_along_axis(base, p, np.where(use[..., None], bx[..., l - 1:l], np.take_along_axis(base, p, -1)), -1)
    p = bp[..., :1]; v = np.take_along_axis(base, p, -1)
    np.put_along_axis(base, p, np.where(dec[..., None], (v // S + 1) % N * S, v), -1)
    rf = np.where((m | dec)[..., None], base, rf)
    c2 = earlier(m); ch = (kind == RO + 2) & (c2 != n)
    cd = np.where(ch, c2, cd); rl = of(rf, cd); pl = of(bp, cd)[..., :1]
    late = ch & (np.take_along_axis(kind, cd, -1) == 1) & (rng.random(kind.shape) < 0.6)
    np.put_along_axis(rl, pl, np.where(late[..., None], of(bx, cd)[..., :1], np.take_along_axis(rl, pl, -1)), -1)
    return np.where(ch[..., None], rl, rf), cd
def pack(sz, rf, cd, rch):
    return {"sz": np.ascontiguousarray(sz.reshape(N, 128, S)).astype(np.int32), "rf": np.ascontiguousarray(rf.transpose(0, 1, 3, 2)).reshape(N, 128, S).astype(np.int32),
            "cd": np.stack([gtable(a) for a in cd]), "rch": np.ascontiguousarray(rch.reshape(N, 128, 16)).astype(np.int32)}
def half():
    return (np.arange(N)[:, None] + np.arange(8)[None, :]) % 2 == 0
def setup_inputs(rng):
    sz, rf, rch = parts(rng); rf, cd = weave(rng, rf, kinds(rng, 0.24, 0.06, 0.06, 0.04))
    return pack(sz, rf, cd, rch)
def setup_inputs_spread(rng):
    sz, rf, rch = parts(rng)
    sz = 16 + (240 * np.power(rng.random((N, 8, 16, S)), np.exp2(rng.integers(-2, 4, (N, 8, 1, S))))).astype(np.int64)
    rch = np.exp2(4 + 18 * rng.random((N, 8, 1, 16)) + 3 * rng.random((N, 8, 16, 16))).astype(np.int64)
    rf, cd = weave(rng, rf, kinds(rng, 0.2, 0.08, 0.08, 0.08))
    return pack(np.minimum(sz, 255), rf, cd, np.minimum(rch, FARTHEST))
def setup_inputs_ends(rng):
    sz = np.where(rng.random((N, 8, 16, S)) < 0.5, 16, 255); sz[:, :, [1, 15]] = 255; sz[:, :, [0, 14]] = 16
    k = kinds(rng, 0.05, 0.08, 0.0, 0.55); k[:, 1::2, S - 1] = 0
    for g in range(0, 8, 2): k[N - 1, g, S - 1] = 1 + (g >> 1) % (RO - 1)
    m = 2 ** 20 // (S * (252 + 9 * LEN))
    many = (2 ** 20 / (S * m * (1 - np.mean(k == 1))) - 255) / LEN
    few = np.floor(many * np.arange(8 * N + 1)).astype(np.int64); few = 16 - (few[1:] - few[:-1]).reshape(N, 8, 1, 1)
    o = rng.random((N, 8, 1, 16)); o[..., 0] = -1; o[..., 15] = 2; o[:N - m, ::2, :, 15] = -1
    late = np.argsort(np.argsort(o, axis=-1), axis=-1) < few
    zero = rng.random((N, 8, 16, 16)) < 0.5; zero[:, :, np.arange(16), np.arange(16)] = True
    rch = np.where(late | ~zero, FARTHEST, 0)
    away = np.where(2 * np.arange(N) < N, W - 1, 0)[:, None, None, None]
    rf = np.where(rng.random((N, 8, S, 16)) < 0.5, 0, W - 1); rf = np.where(late & (rng.random(rf.shape) < 0.8), away, rf)
    rf, cd = weave(rng, rf, k, True)
    n = np.arange(S); own = S * np.arange(N)[:, None, None] + n
    fold = (cd != n) & np.all(rf == np.take_along_axis(rf, cd[..., None], 2), axis=-1)
    cnt = np.add.reduce(((rf != own[..., None]) & ~late).astype(np.int64), axis=-1)
    ln = np.where(fold, 0, 255 + LEN * cnt).reshape(-1); at = np.add.accumulate(ln) - ln
    gone = fold.reshape(-1).copy(); free = (((k == 0) | (k > RO)) & ~fold).reshape(-1); less = 0; last = 0
    for q in range(N - m):
        for g in range(8):
            ks = np.flatnonzero(late[q, g, 0]); ws = rng.permutation(1 + np.flatnonzero(k[q, g, 1:S // 4] == RO + 3))
            for i in range(2):
                vs = rng.permutation(np.arange((1 + i) * S // 4, (2 + i) * S // 4 - 12)); vs = vs[k[q, g, vs] == RO + 3]
                if i == 0: vs = vs[at[(q * 8 + g) * S + vs] % 2 == 1]
                if len(vs) == 0 or len(ws) < 2: continue
                v, w = int(vs[0]), int(ws[i])
                want = int(at[(q * 8 + g) * S + v]) + FARTHEST + i * int(rng.integers(0, 2)) + less
                u = int(np.searchsorted(at, want)); b = u % S
                if u // S != (q + m) * 8 + g or b < 8 or b >= S - 8 or u - 8 < last: continue
                cuts = [j for j in range(u - 1, u - 7, -1) if not gone[j]][:3]
                if len(cuts) < 3 or not (free[u] and free[u + 1]): continue
                rest = int(at[u]) - want; less += rest
                for j in cuts:
                    cut = min(rest, 239); rest -= cut
                    sz[j // (8 * S), j // S % 8, [1, 15], j % S] -= cut
                to = (q + m) * S + b
                if i == 0:
                    cd[q + m, g, b] = 0; cd[q + m, g, b + 1] = b; rf[q + m, g, [b, b + 1]] = rf[q + m, g, 0]
                    gone[u] = True; gone[u + 1] = True; less += int(ln[u] + ln[u + 1]); to += 1
                last = u + 1
                kk = int(ks[-1]) if i == 0 else int(rng.choice(ks)); p = int(rng.choice(np.flatnonzero(~late[q, g, 0])))
                x = int(rng.choice(np.flatnonzero(fold[:, g].reshape(-1)))); y = x // S * S + int(cd[x // S, g, x % S])
                rf[q, g, w] = rf[q, g, v]; rf[q, g, [w, v], kk] = to
                rf[q, g, w, p], rf[q, g, v, p] = (y, x) if rng.random() < 0.5 else (x, y)
                cd[q, g, v] = w
    return pack(sz, rf, cd, rch)
def setup_inputs_corners(rng):
    sz, rf, rch = parts(rng); k = kinds(rng, 0.24, 0.06, 0.1, 0.04); other = half(); k[other] = RO + 4
    rf, cd = weave(rng, rf, k); n = np.arange(S)
    for q, g in np.argwhere(other).tolist():
        t = (g // 2 + q) % 6; o = q * S; few = np.array([0, W - 1, o, o + S - 1, o + S // 2, (q + 1) % N * S + S - 1])
        if t < 3:
            rf[q, g] = rng.permutation(np.concatenate([few, rng.choice(few, 10)])); cd[q, g] = (np.maximum(n - 1, 0), 0 * n, n)[t]
        elif t == 3:
            rf[q, g] = (o + n)[:, None]; cd[q, g] = np.maximum(n - 1, 0)
        elif t == 4:
            cd[q, g] = np.minimum((rng.random(S) * (n + 1)).astype(np.int64), n); rch[q, g] = FARTHEST; sz[q, g] = 255
        else:
            j = rng.integers(0, 3, (S, 16)); rf[q, g] = np.where(j == 0, 0, np.where(j == 1, W - 1, (o + n)[:, None]))
            cd[q, g] = np.where(n % 2 == 1, 0, n); sz[q, g] = rng.choice(np.array([16, 255]), (16, S))
        if t in (2, 3, 5): rch[q, g] = 0
    return pack(sz, rf, cd, rch)
def setup_inputs_crowd(rng):
    sz, rf, rch = parts(rng); k = kinds(rng, 0.24, 0.06, 0.06, 0.04); other = half(); k[other] = RO + 4
    rf, cd = weave(rng, rf, k); n = np.arange(S)
    for q, g in np.argwhere(other).tolist():
        t = (g // 2 + q) % 4; pool = np.flatnonzero(k[:, g].reshape(-1) == 1 + (g // 2) % (RO - 1))
        rf[q, g] = int(rng.choice(pool)); rch[q, g] = 0; sz[q, g, ::2] = 255; sz[q, g, 1::4] = 16
        if t == 1: rf[q, g, :, int(rng.integers(0, 16))] = q * S + n
        if t == 2: cd[q, g] = np.minimum((rng.random(S) * n).astype(np.int64), np.maximum(n - 1, 0))
        if t == 3:
            rf[q, g] = rng.choice(pool, 4)[rng.integers(0, 4, 16)]; rf[q, g, S - 1, 15] = q * S + S - 1; cd[q, g] = 0
    return pack(sz, rf, cd, rch)
def setup_inputs_calm(rng):
    sz, rf, rch = parts(rng); k = kinds(rng, 0.24, 0.06, 0.06, 0.04); other = half(); k[other] = RO + 4
    rf, cd = weave(rng, rf, k); n = np.arange(S); m = S // 4 - 1
    for q, g in np.argwhere(other).tolist():
        o = q * S; dist = int(rng.integers(370, 401)); i = int(rng.integers(0, 16)); big = rng.random(m) < 0.4
        b = np.where(big, rng.integers(15, 17, m), rng.integers(0, 4, m)); c = np.where(big, rng.integers(15, 17, m), rng.integers(1, 4, m))
        e = (rng.random((3, m)) < np.array([[0.8], [0.75], [0.5]])).astype(np.int64)
        s1 = np.where(big, rng.integers(17, 35, m), rng.integers(150, 181, m))
        s0 = dist - LEN * b + e[0] - s1; s2 = dist - LEN * c + e[1] - s1; s3 = dist - LEN * c + e[2] - s2
        sz[q, g, i, :4 * m] = np.stack([s3, s2, s1, s0], axis=1).reshape(-1)
        rch[q, g] = FARTHEST; rch[q, g, i] = dist
        put = np.argsort(rng.random((m, 4, 16)), axis=-1) < np.stack([c, c, c, b], axis=1)[..., None]
        self_ = np.repeat((o + n)[:, None], 16, axis=1); to = self_[:4 * m].reshape(m, 4, 16) + 2
        to[:, 3] = (q + rng.integers(1, N, (m, 16))) % N * S + rng.integers(0, S, (m, 16))
        self_[:4 * m] = np.where(put, to, to * 0 + self_[:4 * m].reshape(m, 4, 16)).reshape(4 * m, 16)
        rf[q, g] = self_; cd[q, g] = np.minimum((rng.random(S) * (n + 1)).astype(np.int64), n)
    return pack(sz, rf, cd, rch)
def check_inputs(d):
    bad = []
    for k, lo, hi in (("sz", 16, 255), ("rf", 0, W - 1), ("cd", 0, S - 1), ("rch", 0, FARTHEST)):
        if np.min(d[k]) < lo or np.max(d[k]) > hi: bad.append("range of " + k)
    if any(np.any(gentries(a) > np.arange(S)) for a in d["cd"]): bad.append("cd names a later section")
    return bad
def places(z):
    t = np.ascontiguousarray(z.transpose(2, 0, 1, 3)).reshape(16, N * 8 * S)
    return np.ascontiguousarray((np.add.accumulate(t, axis=1) - t).reshape(16, N, 8, S).transpose(1, 2, 0, 3))
def reference(sz, rf, cd, rch):
    z = sz.astype(np.int64).reshape(N, 8, 16, S); lim = rch.astype(np.int64).reshape(N, 8, 16, 16)
    r = np.stack([gentries(a) for a in rf]).astype(np.int64).reshape(N, 8, S, 16); c = np.stack([gentries(a) for a in cd]).astype(np.int64)
    first = S * np.arange(N)[:, None, None]; n = np.arange(S)
    far = np.zeros((N, 8, S, 16), bool); gone = np.zeros((N, 8, S), bool); j = np.zeros((N, 8, S), np.int64) + first + n
    for rnd in range(RO):
        jw = j.transpose(1, 0, 2).reshape(8, W)
        r = jw[np.arange(8)[None, :, None, None], r]
        a = places(z); aw = np.ascontiguousarray(a.transpose(1, 2, 0, 3)).reshape(8, 16, W)
        now = np.zeros((N, 8, S, 16), bool)
        for q in range(N):
            for g in range(8):
                d = np.abs(aw[g][:, r[q, g]] - a[q, g][:, :, None])
                now[q, g] = np.any(d > lim[q, g][:, None, :], axis=0)
        new = now & ~far & ~gone[..., None]; far = far | new
        like = np.all(r == np.take_along_axis(r, c[..., None], 2), axis=-1)
        fold = ~gone & (c != n) & like
        grow = LEN * np.add.reduce(new.astype(np.int64), axis=-1)
        z = np.where(fold[:, :, None, :], 0, z + grow[:, :, None, :])
        gone = gone | fold; j = np.where(gone, first + c, first + n)
    return {"yr": np.ascontiguousarray(r.transpose(0, 1, 3, 2)).reshape(N, 128, S).astype(np.float32), "yj": j.astype(np.float32),
            "yf": np.ascontiguousarray(far.transpose(0, 1, 3, 2)).reshape(N, 128, S).astype(np.float32), "ya": places(z).reshape(N, 128, S).astype(np.float32)}

@@ -1,0 +1,538 @@
+from concourse.bass import DstId, RemoteDMATransfer
+from concourse.mybir import AluOpType, ActivationFunctionType
+
+N, S, RO, GROW = 5, 768, 3, 18
+W = N * S
+CA, CB = 512, 256
+O = 7
+F32, BF, I32, U16 = "float32", "bfloat16", "int32", "uint16"
+
+ABS_ENDS = ((0, 1, 3, 5, 7, 9, 11, 13, 14, 15), (1, 3, 5, 6, 7))
+PU = 512
+PLAN = {"g": 1.56, "cyc": 1.04e-3, "fix": 0.065, "sem": 0.06, "pe": 0.55e-3, "call": 1.0, "cmpv": 22, "cmps": 5, "renv": 80, "rens": 80, "anyv": 100, "anys": -20,
+        "look": 0.25,
+        "load": 3.7, "z0": 8.5, "z": 2.3, "direct": 10.0, "relay": 16.0, "tot": 6.0}
+
+SCRATCH = {
+    "szi": ("sbuf", [128, S], I32), "rfi": ("sbuf", [128, S], I32),
+    "cdi": ("sbuf", [128, 48], I32), "rci": ("sbuf", [128, 16], I32),
+    "szl": ("sbuf", [128, W], BF),
+    "w1": ("sbuf", [128, W + 8], F32), "w2": ("sbuf", [128, W + 8], F32), "w3": ("sbuf", [128, W + 8], F32),
+    "ph2": ("sbuf", [128, W], BF), "ph3": ("sbuf", [128, W], BF),
+    "dd": ("sbuf", [128, 16 * S], F32), "xx": ("sbuf", [128, 16 * S], BF), "gg": ("sbuf", [128, 16 * S], BF),
+    "off": ("sbuf", [128, S], U16), "rr": ("sbuf", [128, S], F32), "tt": ("sbuf", [128, 2 * S], F32),
+    "pp": ("sbuf", [128, S + 16], F32), "szw": ("sbuf", [128, S + 16], BF), "mb": ("sbuf", [128, 2 * CB], F32),
+    "ne": ("sbuf", [128, S], BF), "sza": ("sbuf", [128, S], BF),
+    "al1": ("sbuf", [128, S], BF), "al2": ("sbuf", [128, S], BF), "al3": ("sbuf", [128, S], BF),
+    "fa": ("sbuf", [128, S], BF),
+    "f1": ("sbuf", [128, S], BF), "f2": ("sbuf", [128, S], BF), "f3": ("sbuf", [128, S], BF),
+    "nf": ("sbuf", [128, S], F32), "hp": ("sbuf", [128, S], BF), "yn": ("sbuf", [128, S], BF),
+    "yj3": ("sbuf", [128, S], BF),
+    "pci": ("sbuf", [128, 8], I32), "pcf": ("sbuf", [128, 16], F32),
+    "cc": ("sbuf", [128, 144], F32), "cm": ("sbuf", [128, 128], F32), "cg": ("sbuf", [128, 128], F32),
+    "zb": ("sbuf", [128, 144], BF), "zw": ("sbuf", [128, 144], BF), "b18": ("sbuf", [128, 128], BF),
+    "idn": ("sbuf", [128, 128], BF), "sw": ("sbuf", [128, 128], F32),
+    "ee": ("sbuf", [128, 128], F32), "el": ("sbuf", [128, 128], F32),
+    "l0": ("sbuf", [128, 48], F32), "l0u": ("sbuf", [128, 48], U16), "nl": ("sbuf", [128, 48], F32),
+    "cdu": ("sbuf", [128, 48], U16), "lim": ("sbuf", [128, 96], F32), "lbase": ("sbuf", [128, 96], F32),
+    "lt": ("sbuf", [128, 96], F32), "lu": ("sbuf", [128, 96], F32),
+    "ju1": ("sbuf", [128, 96], U16), "ju2": ("sbuf", [128, 96], U16), "ju3": ("sbuf", [128, 96], U16),
+    "cl2": ("sbuf", [128, 48], U16), "cl3": ("sbuf", [128, 48], U16), "ofa": ("sbuf", [128, S], U16),
+    "rch_f": ("sbuf", [128, 16], F32), "rch_n": ("sbuf", [128, 16], F32),
+    "base": ("sbuf", [128, 8], F32), "tot": ("sbuf", [128, 16], F32),
+    "c0": ("psum", [128, 512], F32), "c1": ("psum", [128, 512], F32),
+    "q0": ("psum", [128, 512], F32), "q1": ("psum", [128, 512], F32),
+    "r0": ("psum", [128, 512], F32), "r1": ("psum", [128, 512], F32),
+    "s0": ("psum", [128, 512], F32), "s1": ("psum", [128, 512], F32),
+}
+NDMA = 11
+SEMAPHORES = (["ev", "es", "et", "eg"] + ["d%d" % i for i in range(NDMA)]
+              + ["z1", "z2", "z3", "z4", "a2", "a3", "p2", "p3", "tt4", "ha2", "ha3", "hp2", "hp3"]
+              + ["lz", "la2", "la3", "lb2", "lb3", "lp2", "lp3", "lt4"])
+PSUM = ("c0", "c1", "q0", "q1", "r0", "r1", "s0", "s1")
+
+
+def bits(engines):
+    m = 0
+    for e in engines:
+        m |= 1 << e
+    return m
+
+
+def share(engines, parts):
+    n = len(engines) // parts
+    p = 1
+    while 2 * p <= n:
+        p *= 2
+    return [bits(engines[i * n:i * n + p]) for i in range(parts)], p
+
+
+def helpers_of(core, topo):
+    return [c for c in topo.cores_of(core) if topo.die(c) != topo.die(core)]
+
+
+def transfer(topo, dst, mask, sem, ap_src, ap_dst):
+    rid, pid, _ = topo.addr(dst)
+    return RemoteDMATransfer(dst_ids=[DstId(rid=rid, pnc=pid)], dma_engine_mask=mask, remote_sem=sem, src=ap_src, dst=ap_dst)
+
+
+def relay_program(g, core, T, topo, r, j, nh):
+    far = [(r + d) % N for d in range(1, N)]
+    cw, pw = CA // nh, S // nh
+    src_core = T.cores[r]
+    off = topo.engines(src_core, T.cores[far[0]])
+    got = share([e for e in topo.engines(src_core, core) if e not in off], nh)[1]
+    masks, ne = share(topo.engines(core, T.cores[far[0]]), len(far))
+    for t in range(2, RO + 1):
+        for ap, kind in ((T["ph%d" % t][:, r * S + j * pw:r * S + (j + 1) * pw], "p"),
+                         (T["w%d" % t][:, r * S + O + 1 + j * cw:r * S + O + 1 + (j + 1) * cw], "a")):
+            g.wait_ge(T.sem["h%s%d" % (kind, t)], got)
+            g.remote_dma_fused([transfer(topo, T.cores[d], masks[i], T.sem["%s%d" % (kind, t)], ap, ap) for i, d in enumerate(far)],
+                               local_sem=T.sem["l%s%d" % (kind, t)])
+    for t in range(2, RO + 1):
+        g.wait_ge(T.sem["lp%d" % t], ne * len(far))
+        g.wait_ge(T.sem["la%d" % t], ne * len(far))
+
+
+def link(ops):
+    last_w, readers, last_g = {}, {}, None
+    for i, o in enumerate(ops):
+        deps = set()
+        wr = list(o["w"]) + [k for k in o["r"] if k in PSUM]
+        for k in list(o["r"]) + wr:
+            if k in last_w:
+                deps.add(last_w[k])
+        for k in wr:
+            deps.update(readers.get(k, []))
+        deps.discard(i)
+        for k in o["r"]:
+            readers.setdefault(k, []).append(i)
+        for k in wr:
+            last_w[k] = i
+            readers[k] = []
+        o["deps"] = deps
+        o["order"] = set(o["after"])
+        if "g" in o["alt"]:
+            if last_g is not None:
+                o["order"].add(last_g)
+            last_g = i
+
+
+def arrange(ops):
+    P = PLAN
+    n = len(ops)
+    left = [len(o["deps"] | o["order"]) for o in ops]
+    users = [[] for _ in ops]
+    for i, o in enumerate(ops):
+        for d in o["deps"] | o["order"]:
+            users[d].append(i)
+    ready = [0.0] * n
+    free = {e: 0.0 for e in "vstgyx"}
+    pool = [i for i in range(n) if left[i] == 0]
+    out = []
+    while pool:
+        t, e = min((max(free[e], ready[i]), e) for i in pool for e in ops[i]["alt"])
+        cand = [i for i in pool if e in ops[i]["alt"] and ready[i] <= t + (P["look"] if e in "vs" else 0)]
+        i = min(cand, key=lambda i: i + (P[ops[i]["kind"] + e] if len(ops[i]["alt"]) > 1 else 0))
+        o = ops[i]
+        start = max(t, ready[i])
+        o["e"] = e
+        o["fn"], cost = o["alt"][e]
+        free[e] = start + cost
+        pool.remove(i)
+        out.append(i)
+        for u in users[i]:
+            done = start + cost + (o["lat"] + P["sem"] if i in ops[u]["deps"] or "x" in ops[u]["alt"] else 0)
+            ready[u] = max(ready[u], done)
+            left[u] -= 1
+            if left[u] == 0:
+                pool.append(u)
+    return out
+
+
+def emit(g, T, ops):
+    queue = {"v": g.vector, "s": g.scalar, "t": g.tensor, "g": g, "y": g.sync}
+    esem = {"v": "ev", "s": "es", "t": "et", "g": "eg"}
+    link(ops)
+    order = arrange(ops)
+    pos = {i: p for p, i in enumerate(order)}
+    seen_p, needed = {}, set()
+    for i in order:
+        o = ops[i]
+        keep, latest = [], {}
+        for d in sorted(o["deps"], key=lambda d: pos[d]):
+            if ops[d]["tok"] is not None:
+                keep.append(d)
+            elif not (o["e"] == "t" and ops[d]["e"] == "t"):
+                latest[ops[d]["e"]] = d
+        for e, d in sorted(latest.items()):
+            if seen_p.get((o["e"], e), -1) < pos[d]:
+                seen_p[(o["e"], e)] = pos[d]
+                needed.add(d)
+                keep.append(d)
+        o["waits"] = keep
+    count = {e: 0 for e in esem}
+    for i in order:
+        o = ops[i]
+        if i in needed:
+            count[o["e"]] += 1
+            o["tok"] = (esem[o["e"]], count[o["e"]])
+            o["inc"] = 1
+    seen, top, last = {}, {}, {}
+    for i in order:
+        o = ops[i]
+        if o["tok"] is not None:
+            last[o["tok"][0]] = max(last.get(o["tok"][0], 0), o["tok"][1])
+        if o["fn"] is None:
+            continue
+        for d in o["waits"]:
+            name, val = ops[d]["tok"]
+            if seen.get((o["e"], name), 0) < val:
+                seen[(o["e"], name)] = val
+                top[name] = max(top.get(name, 0), val)
+                queue[o["e"]].wait_ge(T.sem[name], val)
+        ins = o["fn"]()
+        if o["inc"]:
+            ins.then_inc(T.sem[o["tok"][0]], o["inc"])
+    for name, val in last.items():
+        if top.get(name, 0) < val:
+            g.sync.wait_ge(T.sem[name], val)
+
+
+def rank_program(g, core, T, topo):
+    r = T.rank_of(core)
+    if r is None:
+        for q in range(N):
+            hs = helpers_of(T.cores[q], topo)
+            if core in hs:
+                relay_program(g, core, T, topo, q, hs.index(core), len(hs))
+        return
+    A, Act = AluOpType, ActivationFunctionType
+    v, sc, pe = g.vector, g.scalar, g.tensor
+    P = PLAN
+    G = P["g"]
+    ops = []
+    ndma = [0]
+
+    def op(alt, rd, wr, tok=None, inc=None, lat=0.0, after=()):
+        ops.append({"alt": alt, "r": list(rd), "w": list(wr), "tok": tok, "inc": inc, "lat": lat, "after": list(after),
+                    "kind": {"xx": "cmp", "gg": "ren"}.get((list(wr) + [""])[0][:2], "any")})
+        return len(ops) - 1
+
+    us = lambda c: P["fix"] + max(64, c) * P["cyc"]
+
+    def dma(e, out, in_, rd, wr, lat=3.0):
+        q = {"s": sc, "y": g.sync}[e]
+        op({e: (lambda: q.dma_start(out, in_), 0.1)}, rd, wr, ("d%d" % ndma[0], 16), 16, lat)
+        ndma[0] += 1
+
+    def f_ts(out, in0, s1, op0, s2=None, op1=None):
+        if op1 is None:
+            return lambda: v.tensor_scalar(out, in0, s1, None, op0)
+        return lambda: v.tensor_scalar(out, in0, s1, s2, op0, op1)
+
+    def f_act(out, in_, f, **kw):
+        return lambda: sc.activation(out, in_, f, **kw)
+
+    def ts(out, in0, s1, op0, rd, wr, s2=None, op1=None, c=64):
+        op({"v": (f_ts(out, in0, s1, op0, s2, op1), us(c))}, rd, wr)
+
+    def tt(out, in0, in1, o, rd, wr, c=96):
+        op({"v": (lambda: v.tensor_tensor(out, in0, in1, o), us(c))}, rd, wr)
+
+    def cp(out, in_, rd, wr, c=64, both=False):
+        alt = {"v": (lambda: v.tensor_copy(out, in_), us(c))}
+        if both:
+            alt["s"] = (f_act(out, in_, Act.Copy), us(c))
+        op(alt, rd, wr)
+
+    def act(out, in_, f, rd, wr, c=64, **kw):
+        op({"s": (f_act(out, in_, f, **kw), us(c))}, rd, wr)
+
+    def either(fv, fs, rd, wr, cv, cs):
+        op({"v": (fv, us(cv)), "s": (fs, us(cs))}, rd, wr)
+
+    def mm(out, lhs, rhs, start, stop, rd, wr, c=64):
+        op({"t": (lambda: pe.matmul(out, lhs, rhs, start, stop), c * P["pe"])}, rd, wr)
+
+    def iota(out, pattern, base, cmul, wr, c, flag=True):
+        if flag:
+            fn = lambda: g.iota(out, pattern, base, cmul, allow_small_or_imprecise_dtypes=True)
+        else:
+            fn = lambda: g.iota(out, pattern, base, cmul)
+        op({"g": (fn, 0.16 + 2 * c * P["cyc"])}, [], wr)
+
+    def ms(ap, val, wr):
+        op({"v": (lambda: v.memset(ap, val), us(64))}, [], wr)
+
+    def scan(out, data, floor, init, rd, wr, c):
+        op({"v": (lambda: v.tensor_tensor_scan(out, data, floor, init, A.add, A.max), us(c))}, rd, wr)
+
+    def remote(trs, local, n, rd, lat):
+        return op({"g": (lambda: g.remote_dma_fused(trs, local_sem=T.sem[local]), P["call"])}, rd, [], (local, n), None, lat)
+
+    def arrive(sem, n, wr, after):
+        op({"x": (None, 0.0)}, [], wr, (sem, n), None, 0.0, after)
+
+    others = [(r + d) % N for d in range(1, N)]
+    hs = helpers_of(core, topo)
+    off_e = topo.engines(core, T.cores[others[0]])
+    on_e = [e for e in topo.engines(core, hs[0]) if e not in off_e]
+    own = slice(r * S, (r + 1) * S)
+    part, wid = [slice(0, CA), slice(CA, S)], [CA, CB]
+    cP, qP, rP = [T.c0[:, 0:CA], T.c1[:, 0:CB]], [T.q0[:, 0:CA], T.q1[:, 0:CB]], [T.r0[:, 0:CA], T.r1[:, 0:CB]]
+    cK, qK, rK = ["c0", "c1"], ["q0", "q1"], ["r0", "r1"]
+    col = lambda i: T.pcf[:, i:i + 1]
+    at = lambda h, k: (k * CA if h == 0 else 16 * CA + k * CB)
+    blk = lambda b, h, k, n=1: b[:, at(h, k):at(h, k) + n * wid[h]]
+    offs = lambda a, n, b=T.off: b[:, a // 16:(a + n) // 16]
+    sent = {}
+
+    def to_helpers(w, a, n, sem, local, key):
+        cw = n // len(hs)
+        masks, ne = share(on_e, len(hs))
+        trs = [transfer(topo, c, masks[j], T.sem[sem], w[:, a + j * cw:a + (j + 1) * cw], w[:, a + j * cw:a + (j + 1) * cw])
+               for j, c in enumerate(hs)]
+        return remote(trs, local, ne * len(hs), [key], P["relay"])
+
+    def send_part(t, h):
+        w = T["w%d" % t]
+        key = "w%d.own%d" % (t, h)
+        a = r * S + O + 1 + h * CA
+        if h == 0:
+            sent[t] = to_helpers(w, a, CA, "ha%d" % t, "lb%d" % t, key)
+        else:
+            masks, ne = share(off_e, N - 1)
+            trs = [transfer(topo, T.cores[d], masks[i], T.sem["a%d" % t], w[:, a:a + CB], w[:, a:a + CB]) for i, d in enumerate(others)]
+            i = remote(trs, "la%d" % t, ne * (N - 1), [key], P["direct"])
+            arrive("a%d" % t, ne * (N - 1) * (1 + len(hs)), ["w%d.%d" % (t, q) for q in others], [sent[t], i])
+
+    def send_names(t):
+        w, cl = T["ph%d" % t], T["cl%d" % t]
+        i = to_helpers(w, r * S, S, "hp%d" % t, "lp%d" % t, "ph%d.own" % t)
+        arrive("p%d" % t, share(off_e, N - 1)[1] * (N - 1) * len(hs), ["ph%d.far" % t], [i])
+        for q in range(16):
+            n = 48 if q < 15 else 47
+            mm(T.s0[:, 64:64 + n], T.zw[:, 15 - q:143 - q], w[:, r * S + q + 1:(r + 1) * S:16], q == 0, q == 15,
+               ["zw", "ph%d.own" % t], ["s0"])
+        ts(cl[:, 0:47], T.s0[:, 64:111], float(-r * S), A.add, ["s0"], ["cl%da" % t])
+        ts(cl[:, 47:48], T.s0[:, 111:112], col(14), A.add, ["s0", "pc14"], ["cl%db" % t])
+
+    def wkeys(t):
+        return ["w%d.%d" % (t, q) for q in others] + ["w%d.own0" % t, "w%d.own1" % t]
+
+    def bases(t):
+        w = T["w%d" % t]
+        mm(T.s1[:, 0:N], T.el[:], w[:, S + O:W + O + 1:S], True, False, wkeys(t) + ["el"], ["s1"], 256)
+        for s in range(1, N):
+            mm(T.s1[:, s:N], T.ee[:], w[:, S + O:(N - s) * S + O + 1:S], False, s == N - 1, wkeys(t) + ["ee"], ["s1"], 256)
+        ts(T.base[:, 0:N], T.s1[:, 0:N], T.s1[:, r:r + 1], A.subtract, ["s1"], ["base"])
+        for q in others:
+            ap, k, b = w[:, q * S + O + 1:(q + 1) * S + O], "w%d.%d" % (t, q), T.base[:, q:q + 1]
+            either(f_ts(ap, ap, b, A.add), f_act(ap, ap, Act.Identity, bias=b), [k, "base"], [k], S, S)
+        cp(w[:, O:W:S], T.base[:, 0:N], ["base"], ["w%d.col0" % t, "w%d.own1" % t, "w%d.z" % t])
+
+    def fold(t):
+        ju, k, al = T["ju%d" % t], "ju%d" % t, T["al%d" % t]
+        win, wk = (T.rfi[:], ["rfi"]) if t == 1 else (T.tt[:, S:2 * S], ["tt.b0", "tt.b1"])
+        tt(T.ne[:], win.indirect(T.cdu[:]), T.rr[:], A.not_equal, ["rr0", "rr1", "cdu"] + wk, ["ne"], S * G)
+        for q in range(16):
+            mm(T.s0[:, 0:48], T.zb[:, 15 - q:143 - q], T.ne[:, q:S:16], q == 0, q == 15, ["zb", "ne"], ["s0"])
+        tt(T.lt[:, 0:48], T.s0[:, 0:48], T.lim[:, 0:48], A.min, ["s0", "lim"], ["lt.a"], 64)
+        tt(T.lt[:, 48:96], T.s0[:, 0:48], T.lim[:, 48:96], A.min, ["s0", "lim"], ["lt.b"], 64)
+        tt(T.lu[:], T.lt[:], T.lbase[:], A.add, ["lt.a", "lt.b", "lbase"], ["lu"], 192)
+        cp(ju[:], T.lu[:], ["lu"], [k], 96)
+        if t == 1:
+            cp(T.ph2[:, own], T.yn[:].indirect(ju[:, 0:48]), ["yn", k], ["ph2.own"], S * G, True)
+            send_names(2)
+        if t == 2:
+            cp(T.yj3[:], T.yn[:].indirect(ju[:, 0:48]), ["yn", k], ["yj3"], S * G, True)
+            cp(T.ph3[:, own], T.yj3[:].indirect(T.ju1[:, 0:48]), ["yj3", "ju1"], ["ph3.own"], S * G, True)
+            send_names(3)
+        cp(T.sza[:], T.szw[:].indirect(ju[:, 48:96]), ["szw", "szw.z", k], ["sza"], S * G, True)
+        either(f_ts(al[:], T.sza[:], 1.0, A.min), f_act(al[:], T.sza[:], Act.Sign), ["sza"], ["al%d" % t], S // 2, S)
+        for h in range(2):
+            mm(qP[h], T.idn[:], T.sza[:, part[h]], True, False, ["idn", "sza"], [qK[h]], wid[h])
+        if t == 3:
+            cp(T.tt[:, 0:S], T.nf[:].indirect(ju[:, 0:48]), ["nf", k], ["tt.a"], S * G, True)
+            dma("y", T.yj[:], T.tt[0:128:16, 0:S], ["tt.a"], [])
+
+    def rename(t):
+        for u in range(16 * S // PU):
+            cp(T.gg[:, u * PU:(u + 1) * PU], T["ph%d" % t][:].indirect(offs(u * PU, PU)),
+               ["ph%d.own" % t, "ph%d.far" % t, "off"], ["gg%d" % u], PU * G, True)
+        for h in range(2):
+            for k in range(16):
+                mm(rP[h], T.zw[:, 15 - k:143 - k], blk(T.gg, h, k), k == 0, k == 15, ["zw", "gg%d" % (at(h, k) // PU)], [rK[h]], wid[h])
+            cp(T.rr[:, part[h]], rP[h], [rK[h]], ["rr%d" % h], wid[h], True)
+            cp(T.tt[:, S + h * CA:S + h * CA + wid[h]], rP[h], [rK[h]], ["tt.b%d" % h], wid[h], True)
+        if t == RO:
+            dma("y", T.yr[:], T.rr[:], ["rr0", "rr1"], [])
+
+    def far(t, h, extra):
+        w = T["w%d" % t]
+        wk = wkeys(t) + ["w%d.col0" % t, "w%d.z" % t, "ofa"]
+        kk = 1 + h
+        mine, mk = (T.pp[:, 0:CA], ["pp0", "pp.z"]) if h == 0 else (T.mb[:], ["mb0", "mb1"])
+        if t > 1:
+            mm(cP[h], T.idn[:], T.fa[:, part[h]], True, False, ["idn", "fa%d" % h], [cK[h]], wid[h])
+        i0 = 0
+        for i in range(16 // kk):
+            tt(blk(T.dd, h, i * kk, kk), w[:].indirect(offs(at(h, i * kk), kk * wid[h], T.ofa)), mine, A.subtract,
+               wk + mk, ["dd%d.%d" % (h, i)], kk * wid[h] * G)
+            if i in ABS_ENDS[h]:
+                d = blk(T.dd, h, i0 * kk, (i + 1 - i0) * kk)
+                dk = ["dd%d.%d" % (h, j) for j in range(i0, i + 1)]
+                act(d, d, Act.Abs, dk, dk, (i + 1 - i0) * kk * wid[h])
+                for k in range(i0 * kk, (i + 1) * kk):
+                    x, d, xk = blk(T.xx, h, k), blk(T.dd, h, k), "xx%d.%d" % (h, k)
+                    either(f_ts(x, d, T.rch_f[:, k:k + 1], A.is_gt), f_act(x, d, Act.Relu, bias=T.rch_n[:, k:k + 1]),
+                           ["dd%d.%d" % (h, k // kk), "rch", "rchn"], [xk], wid[h], wid[h])
+                    mm(cP[h], T.zb[:, 15 - k:143 - k], x, t == 1 and k == 0, k == 15, ["zb", xk], [cK[h]], wid[h])
+                i0 = i + 1
+            for f in extra.get(i, []):
+                f()
+
+    def lengths(t, h):
+        tt(T.fa[:, part[h]], cP[h], T["al%d" % t][:, part[h]], A.min, [cK[h], "al%d" % t], ["fa%d" % h], wid[h])
+        mm(qP[h], T.b18[:], T.fa[:, part[h]], False, True, ["b18", "fa%d" % h], [qK[h]], wid[h])
+        if h == 0:
+            scan(T.pp[:, 1:CA + 1], qP[0], T.sza[:, part[0]], 0.0, ["q0", "sza"], ["pp0"], CA)
+        else:
+            scan(T.pp[:, CA + 1:S + 1], qP[1], T.sza[:, part[1]], T.pp[:, CA:CA + 1], ["q1", "sza", "pp0"], ["pp1"], CB)
+        if t < RO:
+            w, lst, a = T["w%d" % (t + 1)], T["cl%d" % (t + 1)], r * S + O + 1
+            la, lb = "cl%da" % (t + 1), "cl%db" % (t + 1)
+            if h == 0:
+                cp(w[:, a:a + CA], T.pp[:, 0:CA + 1].indirect(lst[:, 0:CA // 16]), ["pp0", "pp.z", la], ["w%d.own0" % (t + 1)], CA * G, True)
+            else:
+                cp(w[:, a + CA:a + S], T.pp[:, 0:S + 1].indirect(lst[:, CA // 16:48]), ["pp0", "pp1", "pp.z", la, lb],
+                   ["w%d.own1" % (t + 1)], CB * G, True)
+            send_part(t + 1, h)
+
+    def twin(src, keys):
+        cp(T.mb[:, 0:CB], src, keys, ["mb0"], CB, True)
+        cp(T.mb[:, CB:2 * CB], src, keys, ["mb1"], CB, True)
+
+    def marks(t, h):
+        f = T["f%d" % t][:, part[h]]
+        if t == 1:
+            either(f_ts(f, cP[h], 1.0, A.min), f_act(f, cP[h], Act.Sign), [cK[h]], ["f1%d" % h], wid[h], wid[h])
+        else:
+            tt(f, cP[h], T["al%d" % (t - 1)][:, part[h]], A.min, [cK[h], "al%d" % (t - 1)], ["f%d%d" % (t, h)], wid[h])
+        if t == RO:
+            for u in range(1, RO + 1):
+                mm(rP[h], T.idn[:], T["f%d" % u][:, part[h]], u == 1, u == RO, ["idn", "f%d%d" % (u, h)], [rK[h]], wid[h])
+            o = T.tt[:, S + h * CA:S + h * CA + wid[h]]
+            either(f_ts(o, rP[h], 1.0, A.min), f_act(o, rP[h], Act.Sign), [rK[h]], ["tt.b%d" % h], wid[h], wid[h])
+            dma("y", T.yf[:, part[h]], o, ["tt.b%d" % h], [])
+
+    dma("y", T.szi[:], T.sz[:], [], ["szi"], P["load"])
+    dma("y", T.rfi[:], T.rf[:], [], ["rfi"], P["load"] + 1.8)
+    dma("s", T.cdi[:], T.cd[:], [], ["cdi"], P["load"])
+    dma("s", T.rci[:], T.rch[:], [], ["rci"], P["load"])
+    iota(T.pci[:, 0:1], [[0, 1]], 0, 1, ["pci0"], 1, False)
+    iota(T.cc[:], [[1, 144]], 0, 0, ["cc"], 144)
+    iota(T.l0[:, 0:32], [[1, 16], [256, 2]], 0, 0, ["l0a"], 32)
+    iota(T.l0[:, 32:48], [[1, 16]], CA, 0, ["l0b"], 16)
+    iota(T.nl[:], [[16, 48]], 0, 0, ["nl"], 48)
+    iota(T.cg[:], [[16, 8], [0, 16]], 0, 0, ["cg"], 128)
+    iota(T.cm[:], [[0, 8], [1, 16]], 0, 0, ["cm"], 128)
+    iota(T.hp[:], [[0, S // 64], [1, 64]], 0, 0, ["hp"], S)
+    cp(T.szw[:, 16:S + 16], T.szi[:], ["szi"], ["szw"], S)
+    for d, q in enumerate(others):
+        trz = [transfer(topo, T.cores[q], bits(off_e), T.sem["z%d" % (d + 1)], T.szw[:, 16:S + 16], T.szl[:, own])]
+        i = remote(trz, "lz", len(off_e) * (N - 1), ["szw"], P["z0"] + d * (P["z"] - P["call"]))
+        arrive("z%d" % (d + 1), len(off_e), ["szl%d" % ((r - d - 1) % N)], [i])
+    iota(T.yj3[:], [[1, S // 64], [0, 64]], r * S // 64, 0, ["yj3"], S)
+    for i, m in enumerate((15, 112, 16, 14, 1, 8, 7)):
+        ts(T.pci[:, i + 1:i + 2], T.pci[:, 0:1], m, A.bitwise_and, ["pci0"], ["pci%d" % (i + 1)])
+    cp(T.pcf[:, 0:8], T.pci[:], ["pci%d" % i for i in range(8)], ["pcf"])
+    ts(col(8), col(5), 16.0, A.mult, ["pcf"], ["pc8"], col(3), A.not_equal)
+    ts(col(9), col(4), 16.0, A.mult, ["pcf"], ["pc9"], col(3), A.add)
+    ts(col(10), col(3), -2.0, A.mult, ["pcf"], ["pc10"], col(0), A.add)
+    ts(col(11), col(6), -7.875, A.mult, ["pcf"], ["pc11"], 64.0, A.add)
+    ts(col(12), col(7), 0.0, A.is_equal, ["pcf", "pc11"], ["pc12"], col(11), A.mult)
+    ts(T.zb[:], T.cc[:], -15.0, A.add, ["cc", "pcf"], ["zb"], col(2), A.is_equal, 144)
+    ts(T.sw[:], T.cc[:, 0:128], -16.0, A.add, ["cc", "pc10"], ["sw"], col(10), A.is_equal, 128)
+    ts(col(13), col(8), float(S), A.mult, ["pc8", "pc9"], ["pc13"], col(9), A.add)
+    ts(T.zw[:], T.zb[:], col(12), A.mult, ["zb", "pc12"], ["zw"])
+    ts(T.zb[:], T.zb[:], 1024.0, A.mult, ["zb"], ["zb"])
+    cp(T.cdu[:], T.cdi[:], ["cdi"], ["cdu"])
+    cp(T.rr[:], T.rfi[:], ["rfi"], ["rr0", "rr1"], S)
+    op({"v": (lambda: v.transpose(T.tt[:, 0:S], T.rr[:]), us(S))}, ["rr0", "rr1"], ["tt.a"])
+    for h in range(2):
+        mm(rP[h], T.sw[:], T.tt[:, part[h]], True, True, ["sw", "tt.a"], [rK[h]], 4 * wid[h])
+        act(T.tt[:, S + h * CA:S + h * CA + wid[h]], rP[h], Act.Copy, [rK[h]], ["tt.b%d" % h], wid[h])
+    ts(T.nl[:], T.nl[:], col(1), A.add, ["nl", "pcf"], ["nl"])
+    tt(T.lim[:, 0:48], T.nl[:], T.cdi[:], A.subtract, ["nl", "cdi"], ["lim.a"])
+    cp(T.lbase[:, 0:48], T.cdi[:], ["cdi"], ["lb.a"])
+    ts(T.nl[:], T.nl[:], 16.0, A.add, ["nl"], ["nl"])
+    ts(T.lbase[:, 48:96], T.lim[:, 0:48], 0.0, A.is_equal, ["lim.a"], ["lb.b"])
+    tt(T.lbase[:, 48:96], T.lbase[:, 48:96], T.nl[:], A.mult, ["lb.b", "nl", "lb.a"], ["lb.b", "lbase"])
+    tt(T.lim[:, 48:96], T.nl[:], T.lbase[:, 48:96], A.subtract, ["nl", "lbase", "lim.a"], ["lim"])
+    ms(T.szw[:, 0:16], 0.0, ["szw.z"])
+    ts(T.idn[:], T.cc[:, 0:128], col(0), A.is_equal, ["cc", "pcf"], ["idn"], c=128)
+    ts(col(15), col(6), 0.125, A.mult, ["pcf"], ["pc15"])
+    ts(col(0), col(6), -0.125, A.mult, ["pcf", "pc10", "idn"], ["pc0"], 1.0, A.add)
+    act(T.ne[:, 0:128], T.idn[:], Act.Copy, ["idn", "pc15"], ["ne", "ne.a"], 128, scale=col(15))
+    act(T.ne[:, 128:256], T.idn[:], Act.Copy, ["idn", "pc0"], ["ne", "ne.b"], 128, scale=col(0))
+    for h in range(2):
+        mm(cP[h], T.ne[:, 0:128], T.hp[:, part[h]], True, False, ["ne", "hp"], [cK[h]], wid[h])
+        mm(cP[h], T.ne[:, 128:256], T.yj3[:, part[h]], False, True, ["ne", "yj3"], [cK[h]], wid[h])
+        act(T.yn[:, part[h]], cP[h], Act.Copy, [cK[h]], ["yn"], wid[h])
+    ts(col(14), col(1), 15.0, A.is_equal, ["pcf"], ["pc14"], float(S + r * S), A.mult)
+    ts(col(14), col(14), float(-r * S), A.add, ["pc14"], ["pc14"])
+    ts(T.l0u[:], T.l0[:], col(13), A.add, ["l0a", "l0b", "pc13"], ["l0u"])
+    cp(T.off[:], T.tt[:].indirect(T.l0u[:]), ["tt.a", "tt.b0", "tt.b1", "l0u"], ["off"], S * G)
+    ts(T.ofa[:], T.off[:], float(O), A.add, ["off"], ["ofa"], c=S // 2)
+    scan(T.w1[:, r * S + O + 1:(r + 1) * S + O + 1], T.szw[:, 16:S + 16], T.szw[:, 16:S + 16], 0.0, ["szw"], ["w1.own0", "w1.own1"], S)
+    for d in range(1, N):
+        q = (r - d) % N
+        scan(T.w1[:, q * S + O + 1:(q + 1) * S + O + 1], T.szl[:, q * S:(q + 1) * S], T.szl[:, q * S:(q + 1) * S], 0.0,
+             ["szl%d" % q], ["w1.%d" % q], S)
+    ts(T.ee[:], T.cm[:], col(1), A.is_equal, ["cm", "pcf"], ["ee"], c=128)
+    ts(T.el[:], T.cg[:], col(2), A.is_gt, ["cg", "pcf"], ["el"], c=128)
+    tt(T.el[:], T.el[:], T.ee[:], A.mult, ["el", "ee"], ["el"], 256)
+    cp(T.rch_f[:], T.rci[:], ["rci"], ["rch"])
+    act(T.rch_n[:], T.rch_f[:], Act.Copy, ["rch"], ["rchn"], scale=-1.0)
+    for t in range(1, RO + 1):
+        ms(T["w%d" % t][:, 0:O + 1], 0.0, ["w%d.z" % t])
+    bases(1)
+    fold(1)
+    iota(T.nf[:], [[1, S]], r * S, 0, ["nf"], S)
+    ms(T.pp[:, 0:1], 0.0, ["pp.z"])
+    ts(T.b18[:], T.cg[:], col(2), A.is_equal, ["cg", "pcf"], ["b18"], float(GROW), A.mult, 128)
+    act(T.pp[:, 1:CA + 1], T.w1[:, r * S + O + 1:r * S + O + CA + 1], Act.Copy, ["w1.own0"], ["pp0"], CA)
+    twin(T.w1[:, r * S + O + CA:(r + 1) * S + O], ["w1.own0"])
+
+    for t in range(1, RO + 1):
+        far(t, 0, {})
+        lengths(t, 0)
+        far(t, 1, {3: [lambda: marks(t, 0)]})
+        lengths(t, 1)
+        if t < RO:
+            bases(t + 1)
+            marks(t, 1)
+            twin(T.pp[:, CA:S], ["pp0", "pp1"])
+            rename(t + 1)
+            fold(t + 1)
+
+    later = [q for q in range(N) if q > r]
+    if later:
+        masks, ne = share(off_e, len(later))
+        trs = [transfer(topo, T.cores[d], masks[i], T.sem.tt4, T.pp[:, S:S + 1], T.tot[:, 4 * r:4 * r + 1]) for i, d in enumerate(later)]
+        remote(trs, "lt4", ne * len(later), ["pp1"], P["tot"])
+    mm(T.s1[:, 0:1], T.el[:], T.pp[:, S:S + 1], True, r == 0, ["el", "pp1"], ["s1"], 256)
+    ops[-1]["lat"] = P["tot"] if r > 0 else 0.0
+    if r > 0:
+        arrive("tt4", sum(share(off_e, N - 1 - q)[1] for q in range(r)), ["tot"], [len(ops) - 1])
+    marks(RO, 1)
+    for q in range(r):
+        mm(T.s1[:, 0:1], T.ee[:], T.tot[:, 4 * q:4 * q + 1], False, q == r - 1, ["ee", "tot"], ["s1"], 256)
+    for h in range(2):
+        hf = slice(h * S // 2, (h + 1) * S // 2)
+        ts(T.w1[:, hf], T.pp[:, hf], T.s1[:, 0:1], A.add, ["pp0", "pp1", "pp.z", "s1"],
+           ["ya%d" % h, "w1.col0", "w1.z"] + wkeys(1), c=S // 2)
+        dma("y" if h == 0 else "s", T.ya[:, hf], T.w1[:, hf], ["ya%d" % h], [])
+    emit(g, T, ops)

@@ -4,14 +4,22 @@ from concourse.mybir import AluOpType, ActivationFunctionType
 N, S, RO, GROW = 5, 768, 3, 18
 W = N * S
 CA, CB = 512, 256
+CR = 384
 O = 7
 F32, BF, I32, U16 = "float32", "bfloat16", "int32", "uint16"
 
-ABS_ENDS = ((0, 1, 3, 5, 7, 9, 11, 13, 14, 15), (1, 3, 5, 6, 7))
+STEPS = ((1, 1, 2, 2, 2, 2, 2, 2, 2), (4, 4, 2, 2, 2, 2))
 PU = 512
-PLAN = {"g": 1.56, "cyc": 1.04e-3, "fix": 0.065, "sem": 0.06, "pe": 0.55e-3, "call": 1.0, "cmpv": 22, "cmps": 5, "renv": 80, "rens": 80, "anyv": 100, "anys": -20,
-        "look": 0.25,
-        "load": 3.7, "z0": 8.5, "z": 2.3, "direct": 10.0, "relay": 16.0, "tot": 6.0}
+PLAN = {"g": 1.5, "cyc": 0.87e-3, "fix": 0.055, "sem": 0.06, "pe": 0.44e-3, "call": 0.7,
+        "cmpv": 25, "cmps": 5, "renv": 72, "rens": 80, "anyv": 100, "anys": -20, "look": 0.25, "early": 1.5, "fold": 2, "ahead": 24,
+        "load": 3.0, "z0": 5.5, "z": 1.4, "direct": 6.5, "hop": 3.5, "relay": 11.0, "tot": 4.5}
+SHIFT = {697: -25, 137: 150, 348: -10, 296: -60, 579: -10, 476: 10, 653: 60, 515: -10, 54: -150, 68: -10, 341: -60, 293: -60,
+         71: 10, 222: -10, 26: 60, 231: -10, 217: -150, 62: 60, 614: 60, 39: 25, 689: -60, 345: 10, 645: 25, 278: -60,
+         165: 150, 204: -60, 577: -25, 136: 10, 533: -25, 41: 60, 81: -150, 346: -60, 627: 25, 76: -10, 80: 60, 658: -10,
+         420: 10, 158: 60, 171: 10, 372: -10, 102: 60, 52: 10, 302: 25, 276: -60, 669: 10, 701: -60, 37: 10, 174: -10,
+         609: -60, 493: 10, 450: -25, 397: 150, 75: -60, 47: -150, 57: -150, 104: 25, 159: 150, 375: -150, 254: -25,
+         188: -10, 259: -60, 350: 150, 69: -10, 42: 150, 38: 10, 243: 150, 258: -10, 291: -25, 727: -25, 24: 150, 3: 60,
+         70: 150, 51: 150, 50: -10, 35: 10, 485: -25, 582: -25, 33: -150, 108: 60, 95: -60, 520: -10, 522: -25, 36: 150}
 
 SCRATCH = {
     "szi": ("sbuf", [128, S], I32), "rfi": ("sbuf", [128, S], I32),
@@ -21,7 +29,8 @@ SCRATCH = {
     "ph2": ("sbuf", [128, W], BF), "ph3": ("sbuf", [128, W], BF),
     "dd": ("sbuf", [128, 16 * S], F32), "xx": ("sbuf", [128, 16 * S], BF), "gg": ("sbuf", [128, 16 * S], BF),
     "off": ("sbuf", [128, S], U16), "rr": ("sbuf", [128, S], F32), "tt": ("sbuf", [128, 2 * S], F32),
-    "pp": ("sbuf", [128, S + 16], F32), "szw": ("sbuf", [128, S + 16], BF), "mb": ("sbuf", [128, 2 * CB], F32),
+    "pp": ("sbuf", [128, S + 16], F32), "szw": ("sbuf", [128, S + 16], BF), "mb": ("sbuf", [128, 4 * CB], F32),
+    "ma": ("sbuf", [128, 2 * CA], F32),
     "ne": ("sbuf", [128, S], BF), "sza": ("sbuf", [128, S], BF),
     "al1": ("sbuf", [128, S], BF), "al2": ("sbuf", [128, S], BF), "al3": ("sbuf", [128, S], BF),
     "fa": ("sbuf", [128, S], BF),
@@ -45,10 +54,10 @@ SCRATCH = {
     "r0": ("psum", [128, 512], F32), "r1": ("psum", [128, 512], F32),
     "s0": ("psum", [128, 512], F32), "s1": ("psum", [128, 512], F32),
 }
-NDMA = 11
+NDMA = 10
 SEMAPHORES = (["ev", "es", "et", "eg"] + ["d%d" % i for i in range(NDMA)]
               + ["z1", "z2", "z3", "z4", "a2", "a3", "p2", "p3", "tt4", "ha2", "ha3", "hp2", "hp3"]
-              + ["lz", "la2", "la3", "lb2", "lb3", "lp2", "lp3", "lt4"])
+              + ["lz", "la2", "la3", "lb2", "lb3", "lc2", "lc3", "lp2", "lp3", "lt4"])
 PSUM = ("c0", "c1", "q0", "q1", "r0", "r1", "s0", "s1")
 
 
@@ -78,15 +87,14 @@ def transfer(topo, dst, mask, sem, ap_src, ap_dst):
 
 def relay_program(g, core, T, topo, r, j, nh):
     far = [(r + d) % N for d in range(1, N)]
-    cw, pw = CA // nh, S // nh
-    src_core = T.cores[r]
-    off = topo.engines(src_core, T.cores[far[0]])
-    got = share([e for e in topo.engines(src_core, core) if e not in off], nh)[1]
+    cw, pw = CR // nh, S // nh
+    on, off = topo.engines(T.cores[r], core), topo.engines(T.cores[r], T.cores[far[0]])
+    got = {"p": share(on, nh)[1], "a": share([e for e in on if e not in off], nh)[1]}
     masks, ne = share(topo.engines(core, T.cores[far[0]]), len(far))
     for t in range(2, RO + 1):
         for ap, kind in ((T["ph%d" % t][:, r * S + j * pw:r * S + (j + 1) * pw], "p"),
                          (T["w%d" % t][:, r * S + O + 1 + j * cw:r * S + O + 1 + (j + 1) * cw], "a")):
-            g.wait_ge(T.sem["h%s%d" % (kind, t)], got)
+            g.wait_ge(T.sem["h%s%d" % (kind, t)], got[kind])
             g.remote_dma_fused([transfer(topo, T.cores[d], masks[i], T.sem["%s%d" % (kind, t)], ap, ap) for i, d in enumerate(far)],
                                local_sem=T.sem["l%s%d" % (kind, t)])
     for t in range(2, RO + 1):
@@ -131,9 +139,9 @@ def arrange(ops):
     pool = [i for i in range(n) if left[i] == 0]
     out = []
     while pool:
-        t, e = min((max(free[e], ready[i]), e) for i in pool for e in ops[i]["alt"])
-        cand = [i for i in pool if e in ops[i]["alt"] and ready[i] <= t + (P["look"] if e in "vs" else 0)]
-        i = min(cand, key=lambda i: i + (P[ops[i]["kind"] + e] if len(ops[i]["alt"]) > 1 else 0))
+        t, e = min((max(free[e], ready[i] - ops[i]["early"]), e) for i in pool for e in ops[i]["alt"])
+        cand = [i for i in pool if e in ops[i]["alt"] and ready[i] - ops[i]["early"] <= t + (P["look"] if e in "vs" else 0)]
+        i = min(cand, key=lambda i: i + SHIFT.get(i, 0) + (P[ops[i]["kind"] + e] if len(ops[i]["alt"]) > 1 else 0))
         o = ops[i]
         start = max(t, ready[i])
         o["e"] = e
@@ -215,7 +223,7 @@ def rank_program(g, core, T, topo):
     ndma = [0]
 
     def op(alt, rd, wr, tok=None, inc=None, lat=0.0, after=()):
-        ops.append({"alt": alt, "r": list(rd), "w": list(wr), "tok": tok, "inc": inc, "lat": lat, "after": list(after),
+        ops.append({"alt": alt, "r": list(rd), "w": list(wr), "tok": tok, "inc": inc, "lat": lat, "after": list(after), "early": 0.0,
                     "kind": {"xx": "cmp", "gg": "ren"}.get((list(wr) + [""])[0][:2], "any")})
         return len(ops) - 1
 
@@ -262,6 +270,9 @@ def rank_program(g, core, T, topo):
             fn = lambda: g.iota(out, pattern, base, cmul)
         op({"g": (fn, 0.16 + 2 * c * P["cyc"])}, [], wr)
 
+    def gcopy(out, in_, rd, wr, c):
+        op({"g": (lambda: g.affine_select(out, in_, [[0, c]], A.is_gt, 0.0, 1, 0), 0.2 + 2 * c * P["cyc"])}, rd, wr)
+
     def ms(ap, val, wr):
         op({"v": (lambda: v.memset(ap, val), us(64))}, [], wr)
 
@@ -277,7 +288,7 @@ def rank_program(g, core, T, topo):
     others = [(r + d) % N for d in range(1, N)]
     hs = helpers_of(core, topo)
     off_e = topo.engines(core, T.cores[others[0]])
-    on_e = [e for e in topo.engines(core, hs[0]) if e not in off_e]
+    on_e = topo.engines(core, hs[0])
     own = slice(r * S, (r + 1) * S)
     part, wid = [slice(0, CA), slice(CA, S)], [CA, CB]
     cP, qP, rP = [T.c0[:, 0:CA], T.c1[:, 0:CB]], [T.q0[:, 0:CA], T.q1[:, 0:CB]], [T.r0[:, 0:CA], T.r1[:, 0:CB]]
@@ -290,26 +301,33 @@ def rank_program(g, core, T, topo):
 
     def to_helpers(w, a, n, sem, local, key):
         cw = n // len(hs)
-        masks, ne = share(on_e, len(hs))
+        masks, ne = share(on_e if n == S else [e for e in on_e if e not in off_e], len(hs))
         trs = [transfer(topo, c, masks[j], T.sem[sem], w[:, a + j * cw:a + (j + 1) * cw], w[:, a + j * cw:a + (j + 1) * cw])
                for j, c in enumerate(hs)]
-        return remote(trs, local, ne * len(hs), [key], P["relay"])
+        i = remote(trs, local, ne * len(hs), key, P["hop"])
+        return op({"x": (None, 0.0)}, [], [], None, None, P["relay"] - P["hop"], [i])
 
     def send_part(t, h):
         w = T["w%d" % t]
         key = "w%d.own%d" % (t, h)
         a = r * S + O + 1 + h * CA
         if h == 0:
-            sent[t] = to_helpers(w, a, CA, "ha%d" % t, "lb%d" % t, key)
+            sent[t] = to_helpers(w, a, CR, "ha%d" % t, "lb%d" % t, [key])
+            if CR < CA:
+                masks, ne = share(off_e, N - 1)
+                ap = w[:, a + CR:a + CA]
+                remote([transfer(topo, T.cores[d], masks[i], T.sem["a%d" % t], ap, ap) for i, d in enumerate(others)],
+                       "lc%d" % t, ne * (N - 1), [key], P["direct"])
         else:
             masks, ne = share(off_e, N - 1)
             trs = [transfer(topo, T.cores[d], masks[i], T.sem["a%d" % t], w[:, a:a + CB], w[:, a:a + CB]) for i, d in enumerate(others)]
-            i = remote(trs, "la%d" % t, ne * (N - 1), [key], P["direct"])
-            arrive("a%d" % t, ne * (N - 1) * (1 + len(hs)), ["w%d.%d" % (t, q) for q in others], [sent[t], i])
+            i = remote(trs, "la%d" % t, ne * (N - 1), [key], P["direct"] - 2.0)
+            i = op({"x": (None, 0.0)}, [], [], None, None, 2.0, [i])
+            arrive("a%d" % t, ne * (N - 1) * (1 + (CR < CA) + len(hs)), ["w%d.%d" % (t, q) for q in others], [sent[t], i])
 
     def send_names(t):
         w, cl = T["ph%d" % t], T["cl%d" % t]
-        i = to_helpers(w, r * S, S, "hp%d" % t, "lp%d" % t, "ph%d.own" % t)
+        i = to_helpers(w, r * S, S, "hp%d" % t, "lp%d" % t, ["ph%d.own" % t])
         arrive("p%d" % t, share(off_e, N - 1)[1] * (N - 1) * len(hs), ["ph%d.far" % t], [i])
         for q in range(16):
             n = 48 if q < 15 else 47
@@ -324,6 +342,7 @@ def rank_program(g, core, T, topo):
     def bases(t):
         w = T["w%d" % t]
         mm(T.s1[:, 0:N], T.el[:], w[:, S + O:W + O + 1:S], True, False, wkeys(t) + ["el"], ["s1"], 256)
+        ops[-1]["early"] = P["early"]
         for s in range(1, N):
             mm(T.s1[:, s:N], T.ee[:], w[:, S + O:(N - s) * S + O + 1:S], False, s == N - 1, wkeys(t) + ["ee"], ["s1"], 256)
         ts(T.base[:, 0:N], T.s1[:, 0:N], T.s1[:, r:r + 1], A.subtract, ["s1"], ["base"])
@@ -353,43 +372,42 @@ def rank_program(g, core, T, topo):
         either(f_ts(al[:], T.sza[:], 1.0, A.min), f_act(al[:], T.sza[:], Act.Sign), ["sza"], ["al%d" % t], S // 2, S)
         for h in range(2):
             mm(qP[h], T.idn[:], T.sza[:, part[h]], True, False, ["idn", "sza"], [qK[h]], wid[h])
-        if t == 3:
-            cp(T.tt[:, 0:S], T.nf[:].indirect(ju[:, 0:48]), ["nf", k], ["tt.a"], S * G, True)
-            dma("y", T.yj[:], T.tt[0:128:16, 0:S], ["tt.a"], [])
 
     def rename(t):
         for u in range(16 * S // PU):
             cp(T.gg[:, u * PU:(u + 1) * PU], T["ph%d" % t][:].indirect(offs(u * PU, PU)),
                ["ph%d.own" % t, "ph%d.far" % t, "off"], ["gg%d" % u], PU * G, True)
+            if u >= P["ahead"]:
+                ops[-1]["after"].append(sent["last"])
         for h in range(2):
             for k in range(16):
                 mm(rP[h], T.zw[:, 15 - k:143 - k], blk(T.gg, h, k), k == 0, k == 15, ["zw", "gg%d" % (at(h, k) // PU)], [rK[h]], wid[h])
+
+    def renamed(t):
+        for h in range(2):
             cp(T.rr[:, part[h]], rP[h], [rK[h]], ["rr%d" % h], wid[h], True)
-            cp(T.tt[:, S + h * CA:S + h * CA + wid[h]], rP[h], [rK[h]], ["tt.b%d" % h], wid[h], True)
+            gcopy(T.tt[:, S + h * CA:S + h * CA + wid[h]], T.rr[:, part[h]], ["rr%d" % h], ["tt.b%d" % h], wid[h])
         if t == RO:
             dma("y", T.yr[:], T.rr[:], ["rr0", "rr1"], [])
 
     def far(t, h, extra):
         w = T["w%d" % t]
         wk = wkeys(t) + ["w%d.col0" % t, "w%d.z" % t, "ofa"]
-        kk = 1 + h
-        mine, mk = (T.pp[:, 0:CA], ["pp0", "pp.z"]) if h == 0 else (T.mb[:], ["mb0", "mb1"])
+        mine, mk = (T.ma, "ma") if h == 0 else (T.mb, "mb")
         if t > 1:
             mm(cP[h], T.idn[:], T.fa[:, part[h]], True, False, ["idn", "fa%d" % h], [cK[h]], wid[h])
-        i0 = 0
-        for i in range(16 // kk):
-            tt(blk(T.dd, h, i * kk, kk), w[:].indirect(offs(at(h, i * kk), kk * wid[h], T.ofa)), mine, A.subtract,
-               wk + mk, ["dd%d.%d" % (h, i)], kk * wid[h] * G)
-            if i in ABS_ENDS[h]:
-                d = blk(T.dd, h, i0 * kk, (i + 1 - i0) * kk)
-                dk = ["dd%d.%d" % (h, j) for j in range(i0, i + 1)]
-                act(d, d, Act.Abs, dk, dk, (i + 1 - i0) * kk * wid[h])
-                for k in range(i0 * kk, (i + 1) * kk):
-                    x, d, xk = blk(T.xx, h, k), blk(T.dd, h, k), "xx%d.%d" % (h, k)
-                    either(f_ts(x, d, T.rch_f[:, k:k + 1], A.is_gt), f_act(x, d, Act.Relu, bias=T.rch_n[:, k:k + 1]),
-                           ["dd%d.%d" % (h, k // kk), "rch", "rchn"], [xk], wid[h], wid[h])
-                    mm(cP[h], T.zb[:, 15 - k:143 - k], x, t == 1 and k == 0, k == 15, ["zb", xk], [cK[h]], wid[h])
-                i0 = i + 1
+        k0 = 0
+        for i, kk in enumerate(STEPS[h]):
+            d, dk = blk(T.dd, h, k0, kk), ["dd%d.%d" % (h, i)]
+            tt(d, w[:].indirect(offs(at(h, k0), kk * wid[h], T.ofa)), mine[:, 0:kk * wid[h]], A.subtract,
+               wk + ["%s%d" % (mk, j) for j in range(kk)], dk, kk * wid[h] * G)
+            act(d, d, Act.Abs, dk, dk, kk * wid[h])
+            for k in range(k0, k0 + kk):
+                x, d, xk = blk(T.xx, h, k), blk(T.dd, h, k), "xx%d.%d" % (h, k)
+                either(f_ts(x, d, T.rch_f[:, k:k + 1], A.is_gt), f_act(x, d, Act.Relu, bias=T.rch_n[:, k:k + 1]),
+                       dk + ["rch", "rchn"], [xk], wid[h], wid[h])
+                mm(cP[h], T.zb[:, 15 - k:143 - k], x, t == 1 and k == 0, k == 15, ["zb", xk], [cK[h]], wid[h])
+            k0 += kk
             for f in extra.get(i, []):
                 f()
 
@@ -408,18 +426,19 @@ def rank_program(g, core, T, topo):
             else:
                 cp(w[:, a + CA:a + S], T.pp[:, 0:S + 1].indirect(lst[:, CA // 16:48]), ["pp0", "pp1", "pp.z", la, lb],
                    ["w%d.own1" % (t + 1)], CB * G, True)
+                sent["last"] = len(ops) - 2
             send_part(t + 1, h)
-
-    def twin(src, keys):
-        cp(T.mb[:, 0:CB], src, keys, ["mb0"], CB, True)
-        cp(T.mb[:, CB:2 * CB], src, keys, ["mb1"], CB, True)
+            m, mk = (T.ma, "ma") if h == 0 else (T.mb, "mb")
+            for j in range(max(STEPS[h])):
+                gcopy(m[:, j * wid[h]:(j + 1) * wid[h]], T.pp[:, part[h]], ["pp0", "pp.z"] + ["pp1"] * h, ["%s%d" % (mk, j)], wid[h])
 
     def marks(t, h):
         f = T["f%d" % t][:, part[h]]
         if t == 1:
             either(f_ts(f, cP[h], 1.0, A.min), f_act(f, cP[h], Act.Sign), [cK[h]], ["f1%d" % h], wid[h], wid[h])
         else:
-            tt(f, cP[h], T["al%d" % (t - 1)][:, part[h]], A.min, [cK[h], "al%d" % (t - 1)], ["f%d%d" % (t, h)], wid[h])
+            tt(f, cP[h], T["al%d" % (t - 1)][:, part[h]], A.min, [cK[h], "al%d" % (t - 1)] + (["pp1"] if t == RO else []),
+               ["f%d%d" % (t, h)], wid[h])
         if t == RO:
             for u in range(1, RO + 1):
                 mm(rP[h], T.idn[:], T["f%d" % u][:, part[h]], u == 1, u == RO, ["idn", "f%d%d" % (u, h)], [rK[h]], wid[h])
@@ -428,8 +447,8 @@ def rank_program(g, core, T, topo):
             dma("y", T.yf[:, part[h]], o, ["tt.b%d" % h], [])
 
     dma("y", T.szi[:], T.sz[:], [], ["szi"], P["load"])
-    dma("y", T.rfi[:], T.rf[:], [], ["rfi"], P["load"] + 1.8)
-    dma("s", T.cdi[:], T.cd[:], [], ["cdi"], P["load"])
+    dma("y", T.rfi[:], T.rf[:], [], ["rfi"], P["load"] + 1.1)
+    dma("s", T.cdi[:], T.cd[:], [], ["cdi"], P["load"] - 0.7)
     dma("s", T.rci[:], T.rch[:], [], ["rci"], P["load"])
     iota(T.pci[:, 0:1], [[0, 1]], 0, 1, ["pci0"], 1, False)
     iota(T.cc[:], [[1, 144]], 0, 0, ["cc"], 144)
@@ -475,17 +494,16 @@ def rank_program(g, core, T, topo):
     ts(T.idn[:], T.cc[:, 0:128], col(0), A.is_equal, ["cc", "pcf"], ["idn"], c=128)
     ts(col(15), col(6), 0.125, A.mult, ["pcf"], ["pc15"])
     ts(col(0), col(6), -0.125, A.mult, ["pcf", "pc10", "idn"], ["pc0"], 1.0, A.add)
-    act(T.ne[:, 0:128], T.idn[:], Act.Copy, ["idn", "pc15"], ["ne", "ne.a"], 128, scale=col(15))
-    act(T.ne[:, 128:256], T.idn[:], Act.Copy, ["idn", "pc0"], ["ne", "ne.b"], 128, scale=col(0))
+    act(T.fa[:, 0:128], T.idn[:], Act.Copy, ["idn", "pc15"], ["fa0"], 128, scale=col(15))
+    act(T.fa[:, 128:256], T.idn[:], Act.Copy, ["idn", "pc0"], ["fa0"], 128, scale=col(0))
     for h in range(2):
-        mm(cP[h], T.ne[:, 0:128], T.hp[:, part[h]], True, False, ["ne", "hp"], [cK[h]], wid[h])
-        mm(cP[h], T.ne[:, 128:256], T.yj3[:, part[h]], False, True, ["ne", "yj3"], [cK[h]], wid[h])
+        mm(cP[h], T.fa[:, 0:128], T.hp[:, part[h]], True, False, ["fa0", "hp"], [cK[h]], wid[h])
+        mm(cP[h], T.fa[:, 128:256], T.yj3[:, part[h]], False, True, ["fa0", "yj3"], [cK[h]], wid[h])
         act(T.yn[:, part[h]], cP[h], Act.Copy, [cK[h]], ["yn"], wid[h])
     ts(col(14), col(1), 15.0, A.is_equal, ["pcf"], ["pc14"], float(S + r * S), A.mult)
     ts(col(14), col(14), float(-r * S), A.add, ["pc14"], ["pc14"])
     ts(T.l0u[:], T.l0[:], col(13), A.add, ["l0a", "l0b", "pc13"], ["l0u"])
-    cp(T.off[:], T.tt[:].indirect(T.l0u[:]), ["tt.a", "tt.b0", "tt.b1", "l0u"], ["off"], S * G)
-    ts(T.ofa[:], T.off[:], float(O), A.add, ["off"], ["ofa"], c=S // 2)
+    ts(T.ofa[:], T.tt[:].indirect(T.l0u[:]), float(O), A.add, ["tt.a", "tt.b0", "tt.b1", "l0u"], ["ofa"], c=S * G)
     scan(T.w1[:, r * S + O + 1:(r + 1) * S + O + 1], T.szw[:, 16:S + 16], T.szw[:, 16:S + 16], 0.0, ["szw"], ["w1.own0", "w1.own1"], S)
     for d in range(1, N):
         q = (r - d) % N
@@ -499,24 +517,25 @@ def rank_program(g, core, T, topo):
     for t in range(1, RO + 1):
         ms(T["w%d" % t][:, 0:O + 1], 0.0, ["w%d.z" % t])
     bases(1)
-    fold(1)
-    iota(T.nf[:], [[1, S]], r * S, 0, ["nf"], S)
     ms(T.pp[:, 0:1], 0.0, ["pp.z"])
     ts(T.b18[:], T.cg[:], col(2), A.is_equal, ["cg", "pcf"], ["b18"], float(GROW), A.mult, 128)
-    act(T.pp[:, 1:CA + 1], T.w1[:, r * S + O + 1:r * S + O + CA + 1], Act.Copy, ["w1.own0"], ["pp0"], CA)
-    twin(T.w1[:, r * S + O + CA:(r + 1) * S + O], ["w1.own0"])
+    act(T.pp[:, 1:S + 1], T.w1[:, r * S + O + 1:(r + 1) * S + O + 1], Act.Copy, ["w1.own0"], ["pp0", "pp1"], S)
+    for h, (m, mk) in enumerate(((T.ma, "ma"), (T.mb, "mb"))):
+        for j in range(max(STEPS[h])):
+            act(m[:, j * wid[h]:(j + 1) * wid[h]], T.pp[:, part[h]], Act.Copy, ["pp0", "pp1", "pp.z"], ["%s%d" % (mk, j)], wid[h])
 
     for t in range(1, RO + 1):
-        far(t, 0, {})
+        far(t, 0, {P["fold"]: ([lambda: renamed(t)] if t > 1 else []) + [lambda: fold(t)]})
+        if t == 1:
+            ts(T.off[:], T.ofa[:], float(-O), A.add, ["ofa"], ["off"], c=S // 2)
+            iota(T.nf[:], [[1, S]], r * S, 0, ["nf"], S)
         lengths(t, 0)
-        far(t, 1, {3: [lambda: marks(t, 0)]})
+        far(t, 1, {3: [lambda: marks(t, 0)]} if t < RO else {})
         lengths(t, 1)
         if t < RO:
             bases(t + 1)
             marks(t, 1)
-            twin(T.pp[:, CA:S], ["pp0", "pp1"])
             rename(t + 1)
-            fold(t + 1)
 
     later = [q for q in range(N) if q > r]
     if later:
@@ -527,12 +546,20 @@ def rank_program(g, core, T, topo):
     ops[-1]["lat"] = P["tot"] if r > 0 else 0.0
     if r > 0:
         arrive("tt4", sum(share(off_e, N - 1 - q)[1] for q in range(r)), ["tot"], [len(ops) - 1])
+    marks(RO, 0)
     marks(RO, 1)
+    cp(T.tt[:, 0:S], T.nf[:].indirect(T.ju3[:, 0:48]), ["nf", "ju3", "pp1"], ["tt.a"], S * G, True)
+    dma("y", T.yj[:], T.tt[0:128:16, 0:S], ["tt.a"], [])
     for q in range(r):
         mm(T.s1[:, 0:1], T.ee[:], T.tot[:, 4 * q:4 * q + 1], False, q == r - 1, ["ee", "tot"], ["s1"], 256)
+    cp(T.base[:, 0:1], T.s1[:, 0:1], ["s1"], ["base"])
     for h in range(2):
         hf = slice(h * S // 2, (h + 1) * S // 2)
-        ts(T.w1[:, hf], T.pp[:, hf], T.s1[:, 0:1], A.add, ["pp0", "pp1", "pp.z", "s1"],
-           ["ya%d" % h, "w1.col0", "w1.z"] + wkeys(1), c=S // 2)
-        dma("y" if h == 0 else "s", T.ya[:, hf], T.w1[:, hf], ["ya%d" % h], [])
+        rd, wr = ["pp0", "pp1", "pp.z", "base"], ["dd0.%d" % h]
+        out = T.dd[:, h * CA:h * CA + S // 2]
+        if h == 0:
+            ts(out, T.pp[:, hf], T.base[:, 0:1], A.add, rd, wr, c=S // 2)
+        else:
+            act(out, T.pp[:, hf], Act.Identity, rd, wr, S // 2, bias=T.base[:, 0:1])
+        dma("y" if h == 0 else "s", T.ya[:, hf], out, wr, [])
     emit(g, T, ops)

@@ -3,62 +3,61 @@ from concourse.mybir import AluOpType, ActivationFunctionType
 
 N, S, RO, GROW = 5, 768, 3, 18
 W = N * S
+SPAN = S * (255 + 16 * GROW)
 CA, CB = 512, 256
 CR = 384
 O = 7
-F32, BF, I32, U16 = "float32", "bfloat16", "int32", "uint16"
+UNIT = 1024
+GONE = 4096.0
+F32, BF, I32, U16, F16 = "float32", "bfloat16", "int32", "uint16", "float16"
 
-STEPS = ((1, 1, 2, 2, 2, 2, 2, 2, 2), (4, 4, 2, 2, 2, 2))
-PU = 512
-PLAN = {"g": 1.5, "cyc": 0.87e-3, "fix": 0.055, "sem": 0.06, "pe": 0.44e-3, "call": 0.7,
-        "cmpv": 25, "cmps": 5, "renv": 72, "rens": 80, "anyv": 100, "anys": -20, "look": 0.25, "early": 1.5, "fold": 2, "ahead": 24,
-        "load": 3.0, "z0": 5.5, "z": 1.4, "direct": 6.5, "hop": 3.5, "relay": 11.0, "tot": 4.5}
-SHIFT = {697: -25, 137: 150, 348: -10, 296: -60, 579: -10, 476: 10, 653: 60, 515: -10, 54: -150, 68: -10, 341: -60, 293: -60,
-         71: 10, 222: -10, 26: 60, 231: -10, 217: -150, 62: 60, 614: 60, 39: 25, 689: -60, 345: 10, 645: 25, 278: -60,
-         165: 150, 204: -60, 577: -25, 136: 10, 533: -25, 41: 60, 81: -150, 346: -60, 627: 25, 76: -10, 80: 60, 658: -10,
-         420: 10, 158: 60, 171: 10, 372: -10, 102: 60, 52: 10, 302: 25, 276: -60, 669: 10, 701: -60, 37: 10, 174: -10,
-         609: -60, 493: 10, 450: -25, 397: 150, 75: -60, 47: -150, 57: -150, 104: 25, 159: 150, 375: -150, 254: -25,
-         188: -10, 259: -60, 350: 150, 69: -10, 42: 150, 38: 10, 243: 150, 258: -10, 291: -25, 727: -25, 24: 150, 3: 60,
-         70: 150, 51: 150, 50: -10, 35: 10, 485: -25, 582: -25, 33: -150, 108: 60, 95: -60, 520: -10, 522: -25, 36: 150}
+MODES = (("gaccgcga", "cgag"), ("caccgcag", "ggac"), ("gcaccgcc", "cagc"))
+PU = 768
+PLAN = {"g": 1.5, "cyc": 0.87e-3, "fix": 0.055, "sem": 0.06, "pe": 0.5e-3, "call": 0.7,
+        "pelat": 0.1, "spare": 1.0, "lov": 1, "totat": 0, "passes": 3, "shake": 2.0, "early": 1.5, "ahead": 99, "marks": 12, "after": -150,
+        "load": 3.0, "z0": 5.5, "z": 1.4, "direct": 6.5, "hop": 3.5, "relay": 11.0, "tot": 4.5, "tile": 4.5}
 
 SCRATCH = {
-    "szi": ("sbuf", [128, S], I32), "rfi": ("sbuf", [128, S], I32),
+    "szi": ("sbuf", [128, S], I32), "rfi": ("sbuf", [128, S + 16], I32),
     "cdi": ("sbuf", [128, 48], I32), "rci": ("sbuf", [128, 16], I32),
-    "szl": ("sbuf", [128, W], BF),
+    "szb": ("sbuf", [128, S], BF), "szl": ("sbuf", [128, W], BF),
     "w1": ("sbuf", [128, W + 8], F32), "w2": ("sbuf", [128, W + 8], F32), "w3": ("sbuf", [128, W + 8], F32),
-    "ph2": ("sbuf", [128, W], BF), "ph3": ("sbuf", [128, W], BF),
-    "dd": ("sbuf", [128, 16 * S], F32), "xx": ("sbuf", [128, 16 * S], BF), "gg": ("sbuf", [128, 16 * S], BF),
-    "off": ("sbuf", [128, S], U16), "rr": ("sbuf", [128, S], F32), "tt": ("sbuf", [128, 2 * S], F32),
-    "pp": ("sbuf", [128, S + 16], F32), "szw": ("sbuf", [128, S + 16], BF), "mb": ("sbuf", [128, 4 * CB], F32),
-    "ma": ("sbuf", [128, 2 * CA], F32),
-    "ne": ("sbuf", [128, S], BF), "sza": ("sbuf", [128, S], BF),
-    "al1": ("sbuf", [128, S], BF), "al2": ("sbuf", [128, S], BF), "al3": ("sbuf", [128, S], BF),
-    "fa": ("sbuf", [128, S], BF),
+    "nm2": ("dram", [4 * N, 128, S // 32], BF), "nm3": ("dram", [N, 128, S // 8], BF),
+    "dd": ("sbuf", [128, 16 * S], F32), "xx": ("sbuf", [128, 4 * UNIT], BF), "gg": ("sbuf", [128, 16 * S], BF),
+    "off": ("sbuf", [128, S], U16), "ofa": ("sbuf", [128, S], U16),
+    "rr": ("sbuf", [128, S], F32), "rw": ("sbuf", [128, S + 16], F32), "tt": ("sbuf", [128, 2 * S], F32),
+    "pp": ("sbuf", [128, S + 16], F32), "ln": ("sbuf", [128, S], F32),
+    "ma": ("sbuf", [128, UNIT], F32), "mb": ("sbuf", [128, UNIT], F32),
+    "hi": ("sbuf", [128, S], BF), "lo": ("sbuf", [128, S], F16),
+    "ne": ("sbuf", [128, S], BF), "up": ("sbuf", [128, S], BF),
     "f1": ("sbuf", [128, S], BF), "f2": ("sbuf", [128, S], BF), "f3": ("sbuf", [128, S], BF),
+    "idc": ("sbuf", [128, 512], BF), "rcn": ("sbuf", [128, 16], F32),
+    "dv1": ("sbuf", [128, S], BF), "dv2": ("sbuf", [128, S], BF), "dv3": ("sbuf", [128, S], BF),
+    "tl0": ("sbuf", [128, 4 * CA], BF), "tl1": ("sbuf", [128, 4 * CB], BF), "neg": ("sbuf", [128, CA], BF),
+    "src": ("sbuf", [128, 2048], BF), "wk": ("sbuf", [128, 2048], BF),
+    "ud": ("sbuf", [128, 32], F32), "wd": ("sbuf", [128, 32], I32), "dg": ("sbuf", [128, 96], I32), "sl": ("sbuf", [128, 8], U16),
     "nf": ("sbuf", [128, S], F32), "hp": ("sbuf", [128, S], BF), "yn": ("sbuf", [128, S], BF),
-    "yj3": ("sbuf", [128, S], BF),
-    "pci": ("sbuf", [128, 8], I32), "pcf": ("sbuf", [128, 16], F32),
+    "yj3": ("sbuf", [128, S], BF), "dg2": ("sbuf", [128, 256], BF),
+    "pci": ("sbuf", [128, 16], I32), "pcf": ("sbuf", [128, 32], F32),
     "cc": ("sbuf", [128, 144], F32), "cm": ("sbuf", [128, 128], F32), "cg": ("sbuf", [128, 128], F32),
-    "zb": ("sbuf", [128, 144], BF), "zw": ("sbuf", [128, 144], BF), "b18": ("sbuf", [128, 128], BF),
-    "idn": ("sbuf", [128, 128], BF), "sw": ("sbuf", [128, 128], F32),
+    "zb": ("sbuf", [128, 144], BF), "zf": ("sbuf", [128, 144], BF), "zw": ("sbuf", [128, 144], BF), "b18": ("sbuf", [128, 128], BF),
+    "idn": ("sbuf", [128, 128], BF), "id2": ("sbuf", [128, 128], BF), "idm": ("sbuf", [128, 128], BF),
+    "idh": ("sbuf", [128, 128], F16), "idf": ("sbuf", [128, 128], F32), "sw": ("sbuf", [128, 128], F32),
     "ee": ("sbuf", [128, 128], F32), "el": ("sbuf", [128, 128], F32),
     "l0": ("sbuf", [128, 48], F32), "l0u": ("sbuf", [128, 48], U16), "nl": ("sbuf", [128, 48], F32),
-    "cdu": ("sbuf", [128, 48], U16), "lim": ("sbuf", [128, 96], F32), "lbase": ("sbuf", [128, 96], F32),
-    "lt": ("sbuf", [128, 96], F32), "lu": ("sbuf", [128, 96], F32),
-    "ju1": ("sbuf", [128, 96], U16), "ju2": ("sbuf", [128, 96], U16), "ju3": ("sbuf", [128, 96], U16),
-    "cl2": ("sbuf", [128, 48], U16), "cl3": ("sbuf", [128, 48], U16), "ofa": ("sbuf", [128, S], U16),
-    "rch_f": ("sbuf", [128, 16], F32), "rch_n": ("sbuf", [128, 16], F32),
-    "base": ("sbuf", [128, 8], F32), "tot": ("sbuf", [128, 16], F32),
+    "cdu": ("sbuf", [128, 48], U16), "cdf": ("sbuf", [128, 48], F32), "lt": ("sbuf", [128, 48], F32),
+    "ju1": ("sbuf", [128, 48], U16), "ju2": ("sbuf", [128, 48], U16), "ju3": ("sbuf", [128, 48], U16),
+    "cl2": ("sbuf", [128, 48], U16), "cl3": ("sbuf", [128, 48], U16),
+    "base": ("sbuf", [128, 8], F32), "tot1": ("sbuf", [128, 32], F32), "tot4": ("sbuf", [128, 16], F32),
+    "tp": ("psum", [128, 2048], F32),
     "c0": ("psum", [128, 512], F32), "c1": ("psum", [128, 512], F32),
-    "q0": ("psum", [128, 512], F32), "q1": ("psum", [128, 512], F32),
     "r0": ("psum", [128, 512], F32), "r1": ("psum", [128, 512], F32),
-    "s0": ("psum", [128, 512], F32), "s1": ("psum", [128, 512], F32),
 }
-NDMA = 10
+NDMA = 48
 SEMAPHORES = (["ev", "es", "et", "eg"] + ["d%d" % i for i in range(NDMA)]
-              + ["z1", "z2", "z3", "z4", "a2", "a3", "p2", "p3", "tt4", "ha2", "ha3", "hp2", "hp3"]
-              + ["lz", "la2", "la3", "lb2", "lb3", "lc2", "lc3", "lp2", "lp3", "lt4"])
-PSUM = ("c0", "c1", "q0", "q1", "r0", "r1", "s0", "s1")
+              + ["z1", "z2", "z3", "z4", "tt1", "a2", "a3", "p2", "p3", "tt4", "ha2", "ha3", "hp2", "hp3"]
+              + ["lz", "lt1", "la2", "la3", "lb2", "lb3", "lc2", "lc3", "lp2", "lp3", "lt4"])
+PSUM = ("c0", "c1", "r0", "r1", "t0", "t1")
 
 
 def bits(engines):
@@ -87,19 +86,18 @@ def transfer(topo, dst, mask, sem, ap_src, ap_dst):
 
 def relay_program(g, core, T, topo, r, j, nh):
     far = [(r + d) % N for d in range(1, N)]
-    cw, pw = CR // nh, S // nh
+    cw = CR // nh
     on, off = topo.engines(T.cores[r], core), topo.engines(T.cores[r], T.cores[far[0]])
-    got = {"p": share(on, nh)[1], "a": share([e for e in on if e not in off], nh)[1]}
+    got = share([e for e in on if e not in off], nh)[1]
     masks, ne = share(topo.engines(core, T.cores[far[0]]), len(far))
-    for t in range(2, RO + 1):
-        for ap, kind in ((T["ph%d" % t][:, r * S + j * pw:r * S + (j + 1) * pw], "p"),
-                         (T["w%d" % t][:, r * S + O + 1 + j * cw:r * S + O + 1 + (j + 1) * cw], "a")):
-            g.wait_ge(T.sem["h%s%d" % (kind, t)], got[kind])
-            g.remote_dma_fused([transfer(topo, T.cores[d], masks[i], T.sem["%s%d" % (kind, t)], ap, ap) for i, d in enumerate(far)],
-                               local_sem=T.sem["l%s%d" % (kind, t)])
-    for t in range(2, RO + 1):
-        g.wait_ge(T.sem["lp%d" % t], ne * len(far))
-        g.wait_ge(T.sem["la%d" % t], ne * len(far))
+    piece = lambda t: T["w%d" % t][:, r * S + O + 1 + j * cw:r * S + O + 1 + (j + 1) * cw]
+    jobs = [("p2", T.nm2[nh * r + j])] + [("a%d" % t, piece(t)) for t in range(2, RO + 1)]
+    for name, ap in jobs:
+        g.wait_ge(T.sem["h" + name], got)
+        g.remote_dma_fused([transfer(topo, T.cores[d], masks[i], T.sem[name], ap, ap) for i, d in enumerate(far)],
+                           local_sem=T.sem["l" + name])
+    for name, _ in jobs:
+        g.wait_ge(T.sem["l" + name], ne * len(far))
 
 
 def link(ops):
@@ -120,42 +118,80 @@ def link(ops):
             readers[k] = []
         o["deps"] = deps
         o["order"] = set(o["after"])
-        if "g" in o["alt"]:
-            if last_g is not None:
-                o["order"].add(last_g)
-            last_g = i
+    last_g = None
+    for i in (i for i, o in enumerate(ops) if "g" in o["alt"]):
+        if last_g is not None:
+            ops[i]["order"].add(last_g)
+        last_g = i
 
 
 def arrange(ops):
     P = PLAN
     n = len(ops)
-    left = [len(o["deps"] | o["order"]) for o in ops]
-    users = [[] for _ in ops]
+    before, after = [[] for _ in ops], [[] for _ in ops]
     for i, o in enumerate(ops):
         for d in o["deps"] | o["order"]:
-            users[d].append(i)
-    ready = [0.0] * n
-    free = {e: 0.0 for e in "vstgyx"}
-    pool = [i for i in range(n) if left[i] == 0]
-    out = []
-    while pool:
-        t, e = min((max(free[e], ready[i] - ops[i]["early"]), e) for i in pool for e in ops[i]["alt"])
-        cand = [i for i in pool if e in ops[i]["alt"] and ready[i] - ops[i]["early"] <= t + (P["look"] if e in "vs" else 0)]
-        i = min(cand, key=lambda i: i + SHIFT.get(i, 0) + (P[ops[i]["kind"] + e] if len(ops[i]["alt"]) > 1 else 0))
-        o = ops[i]
-        start = max(t, ready[i])
-        o["e"] = e
-        o["fn"], cost = o["alt"][e]
-        free[e] = start + cost
-        pool.remove(i)
-        out.append(i)
-        for u in users[i]:
-            done = start + cost + (o["lat"] + P["sem"] if i in ops[u]["deps"] or "x" in ops[u]["alt"] else 0)
-            ready[u] = max(ready[u], done)
-            left[u] -= 1
-            if left[u] == 0:
-                pool.append(u)
-    return out
+            lag = 0.0
+            if "x" in o["alt"] or (d in o["deps"] and not ("t" in o["alt"] and "t" in ops[d]["alt"])):
+                lag = ops[d]["lat"] + P["sem"] + (P["pelat"] if "t" in ops[d]["alt"] else 0.0)
+            before[i].append((d, lag))
+            after[d].append((i, lag))
+
+    def place(prev, nxt, key, head):
+        left = [len(x) for x in prev]
+        pool = [i for i in range(n) if left[i] == 0]
+        busy = {e: [] for e in "vstgy"}
+        start, end, eng, seq = [0.0] * n, [0.0] * n, [None] * n, []
+        while pool:
+            i = min(pool, key=lambda i: key[i])
+            pool.remove(i)
+            ready = max([end[d] + lag for d, lag in prev[i]] + [head[i]])
+            best = None
+            for e, (_, cost) in ops[i]["alt"].items():
+                t, p = ready, 0
+                if e != "x":
+                    row = busy[e]
+                    p = len(row)
+                    while p > 0 and row[p - 1][1] > ready:
+                        p -= 1
+                    while p < len(row) and row[p][0] < t + cost:
+                        t = max(t, row[p][1])
+                        p += 1
+                bias = P["spare"] if e == "v" else 0.0
+                if best is None or t + cost + bias < best[0]:
+                    best = (t + cost + bias, t, cost, e, p)
+            _, start[i], cost, eng[i], p = best
+            end[i] = start[i] + cost
+            if eng[i] != "x":
+                busy[eng[i]].insert(p, (start[i], end[i]))
+            seq.append(i)
+            for u, _ in nxt[i]:
+                left[u] -= 1
+                if left[u] == 0:
+                    pool.append(u)
+        return start, end, eng, seq
+
+    tail, best = [o["lat"] for o in ops], None
+    key = [float(o["rank"]) for o in ops]
+    seed = 1
+    for turn in range(P["passes"]):
+        start, end, eng, seq = place(before, after, key, [0.0] * n)
+        span = max(end[i] + tail[i] for i in range(n))
+        if best is None or span < best[0]:
+            best = (span, start, eng, seq, end)
+        late = [-(end[i] + tail[i]) for i in range(n)]
+        if turn % 3 == 2:
+            for i in range(n):
+                seed = (seed * 1103515245 + 12345) % 2 ** 31
+                late[i] = -(best[4][i] + tail[i]) + P["shake"] * seed / 2 ** 31
+        back = place(after, before, late, tail)
+        key = [-back[1][i] for i in range(n)]
+    _, start, eng, seq, _ = best
+    for i, o in enumerate(ops):
+        o["e"] = eng[i]
+        o["fn"] = o["alt"][eng[i]][0]
+    pos = {i: p for p, i in enumerate(seq)}
+    return sorted(range(n), key=lambda i: (start[i], pos[i]))
 
 
 def emit(g, T, ops):
@@ -220,11 +256,12 @@ def rank_program(g, core, T, topo):
     P = PLAN
     G = P["g"]
     ops = []
-    ndma = [0]
+    ndma, shift, units = [0], [0], [0, 0]
+    plain = sorted({m[h].count("c") * UNIT // (CA, CB)[h] for m in MODES for h in range(2)} - {0})
 
     def op(alt, rd, wr, tok=None, inc=None, lat=0.0, after=()):
         ops.append({"alt": alt, "r": list(rd), "w": list(wr), "tok": tok, "inc": inc, "lat": lat, "after": list(after), "early": 0.0,
-                    "kind": {"xx": "cmp", "gg": "ren"}.get((list(wr) + [""])[0][:2], "any")})
+                    "rank": len(ops) + shift[0], "kind": "ren" if (list(wr) + [""])[0][:2] == "gg" else "any"})
         return len(ops) - 1
 
     us = lambda c: P["fix"] + max(64, c) * P["cyc"]
@@ -260,6 +297,12 @@ def rank_program(g, core, T, topo):
     def either(fv, fs, rd, wr, cv, cs):
         op({"v": (fv, us(cv)), "s": (fs, us(cs))}, rd, wr)
 
+    def scaled(out, in_, s, rd, wr, c=128):
+        either(f_ts(out, in_, s, A.mult), f_act(out, in_, Act.Copy, scale=s), rd, wr, c, c)
+
+    def lin(out, in_, a, b, rd, wr):
+        either(f_ts(out, in_, a, A.mult, b, A.add), f_act(out, in_, Act.Identity, scale=a, bias=b), rd, wr, 64, 64)
+
     def mm(out, lhs, rhs, start, stop, rd, wr, c=64):
         op({"t": (lambda: pe.matmul(out, lhs, rhs, start, stop), c * P["pe"])}, rd, wr)
 
@@ -273,11 +316,14 @@ def rank_program(g, core, T, topo):
     def gcopy(out, in_, rd, wr, c):
         op({"g": (lambda: g.affine_select(out, in_, [[0, c]], A.is_gt, 0.0, 1, 0), 0.2 + 2 * c * P["cyc"])}, rd, wr)
 
-    def ms(ap, val, wr):
-        op({"v": (lambda: v.memset(ap, val), us(64))}, [], wr)
+    def ms(ap, val, wr, c=64):
+        op({"v": (lambda: v.memset(ap, val), us(c))}, [], wr)
 
-    def scan(out, data, floor, init, rd, wr, c):
-        op({"v": (lambda: v.tensor_tensor_scan(out, data, floor, init, A.add, A.max), us(c))}, rd, wr)
+    def fill(ap, val, wr, c):
+        either(lambda: v.memset(ap, val), f_act(ap, T.hp[:, 0:c], Act.Identity, scale=0.0, bias=val), ["hp"], wr, c // 2, c)
+
+    def scan(out, data, init, rd, wr, c):
+        op({"v": (lambda: v.tensor_tensor_scan(out, data, data, init, A.add, A.max), us(c))}, rd, wr)
 
     def remote(trs, local, n, rd, lat):
         return op({"g": (lambda: g.remote_dma_fused(trs, local_sem=T.sem[local]), P["call"])}, rd, [], (local, n), None, lat)
@@ -291,8 +337,9 @@ def rank_program(g, core, T, topo):
     on_e = topo.engines(core, hs[0])
     own = slice(r * S, (r + 1) * S)
     part, wid = [slice(0, CA), slice(CA, S)], [CA, CB]
-    cP, qP, rP = [T.c0[:, 0:CA], T.c1[:, 0:CB]], [T.q0[:, 0:CA], T.q1[:, 0:CB]], [T.r0[:, 0:CA], T.r1[:, 0:CB]]
-    cK, qK, rK = ["c0", "c1"], ["q0", "q1"], ["r0", "r1"]
+    cP, rP = [T.c0[:, 0:CA], T.c1[:, 0:CB]], [T.r0[:, 0:CA], T.r1[:, 0:CB]]
+    cK, rK = ["c0", "c1"], ["r0", "r1"]
+    tl = [T.tl0, T.tl1]
     col = lambda i: T.pcf[:, i:i + 1]
     at = lambda h, k: (k * CA if h == 0 else 16 * CA + k * CB)
     blk = lambda b, h, k, n=1: b[:, at(h, k):at(h, k) + n * wid[h]]
@@ -311,113 +358,191 @@ def rank_program(g, core, T, topo):
         w = T["w%d" % t]
         key = "w%d.own%d" % (t, h)
         a = r * S + O + 1 + h * CA
+        masks, ne = share(off_e, N - 1)
         if h == 0:
             sent[t] = to_helpers(w, a, CR, "ha%d" % t, "lb%d" % t, [key])
-            if CR < CA:
-                masks, ne = share(off_e, N - 1)
-                ap = w[:, a + CR:a + CA]
-                remote([transfer(topo, T.cores[d], masks[i], T.sem["a%d" % t], ap, ap) for i, d in enumerate(others)],
-                       "lc%d" % t, ne * (N - 1), [key], P["direct"])
+            ap = w[:, a + CR:a + CA]
+            remote([transfer(topo, T.cores[d], masks[i], T.sem["a%d" % t], ap, ap) for i, d in enumerate(others)],
+                   "lc%d" % t, ne * (N - 1), [key], P["direct"])
         else:
-            masks, ne = share(off_e, N - 1)
             trs = [transfer(topo, T.cores[d], masks[i], T.sem["a%d" % t], w[:, a:a + CB], w[:, a:a + CB]) for i, d in enumerate(others)]
             i = remote(trs, "la%d" % t, ne * (N - 1), [key], P["direct"] - 2.0)
             i = op({"x": (None, 0.0)}, [], [], None, None, 2.0, [i])
-            arrive("a%d" % t, ne * (N - 1) * (1 + (CR < CA) + len(hs)), ["w%d.%d" % (t, q) for q in others], [sent[t], i])
+            arrive("a%d" % t, ne * (N - 1) * (2 + len(hs)), ["w%d.%d" % (t, q) for q in others], [sent[t], i])
 
     def send_names(t):
-        w, cl = T["ph%d" % t], T["cl%d" % t]
-        i = to_helpers(w, r * S, S, "hp%d" % t, "lp%d" % t, ["ph%d.own" % t])
-        arrive("p%d" % t, share(off_e, N - 1)[1] * (N - 1) * len(hs), ["ph%d.far" % t], [i])
+        w, cl, nm = T.szl, T["cl%d" % t], T["nm%d" % t]
+        masks, ne = share(off_e, N - 1)
+        if t == 2:
+            nh = len(hs)
+            dma("y", nm[nh * r:nh * r + nh], w[0:128:8, own], ["szl%d" % r], ["nm2.own"], P["tile"])
+            inner, ni = share([e for e in on_e if e not in off_e], nh)
+            i = remote([transfer(topo, c, inner[j], T.sem.hp2, nm[nh * r + j], nm[nh * r + j]) for j, c in enumerate(hs)],
+                       "lp2", ni * nh, ["nm2.own"], P["hop"])
+            i = op({"x": (None, 0.0)}, [], [], None, None, P["relay"] - P["hop"] - 1.0, [i])
+            arrive("p2", ne * (N - 1) * nh, ["nm2.far"], [i])
+        else:
+            dma("y", nm[r], w[0:128:8, own], ["szl%d" % r], ["nm%d.own" % t], P["tile"])
+            i = remote([transfer(topo, T.cores[d], masks[j], T.sem["p%d" % t], nm[r], nm[r]) for j, d in enumerate(others)],
+                       "lp%d" % t, ne * (N - 1), ["nm%d.own" % t], P["tot"])
+            arrive("p%d" % t, ne * (N - 1), ["nm%d.far" % t], [i])
         for q in range(16):
             n = 48 if q < 15 else 47
-            mm(T.s0[:, 64:64 + n], T.zw[:, 15 - q:143 - q], w[:, r * S + q + 1:(r + 1) * S:16], q == 0, q == 15,
-               ["zw", "ph%d.own" % t], ["s0"])
-        ts(cl[:, 0:47], T.s0[:, 64:111], float(-r * S), A.add, ["s0"], ["cl%da" % t])
-        ts(cl[:, 47:48], T.s0[:, 111:112], col(14), A.add, ["s0", "pc14"], ["cl%db" % t])
+            mm(T.r1[:, 320:320 + n], T.zw[:, 15 - q:143 - q], w[:, r * S + q + 1:(r + 1) * S:16], q == 0, q == 15,
+               ["zw", "szl%d" % r], ["r1"])
+        ts(cl[:, 0:47], T.r1[:, 320:367], float(-r * S), A.add, ["r1"], ["cl%da" % t])
+        ts(cl[:, 47:48], T.r1[:, 367:368], col(14), A.add, ["r1", "pc14"], ["cl%db" % t])
 
     def wkeys(t):
         return ["w%d.%d" % (t, q) for q in others] + ["w%d.own0" % t, "w%d.own1" % t]
 
-    def bases(t):
-        w = T["w%d" % t]
-        mm(T.s1[:, 0:N], T.el[:], w[:, S + O:W + O + 1:S], True, False, wkeys(t) + ["el"], ["s1"], 256)
+    def starts(tot, rd):
+        mm(T.c1[:, CB:CB + N], T.el[:], tot(0, N), True, False, rd + ["el"], ["c1"], 256)
         ops[-1]["early"] = P["early"]
         for s in range(1, N):
-            mm(T.s1[:, s:N], T.ee[:], w[:, S + O:(N - s) * S + O + 1:S], False, s == N - 1, wkeys(t) + ["ee"], ["s1"], 256)
-        ts(T.base[:, 0:N], T.s1[:, 0:N], T.s1[:, r:r + 1], A.subtract, ["s1"], ["base"])
+            mm(T.c1[:, CB + s:CB + N], T.ee[:], tot(0, N - s), False, s == N - 1, rd + ["ee"], ["c1"], 256)
+        ts(T.base[:, 0:N], T.c1[:, CB:CB + N], T.c1[:, CB + r:CB + r + 1], A.subtract, ["c1"], ["base"])
+
+    def bases(t):
+        w = T["w%d" % t]
+        starts(lambda a, b: w[:, (a + 1) * S + O:b * S + O + 1:S], wkeys(t))
         for q in others:
             ap, k, b = w[:, q * S + O + 1:(q + 1) * S + O], "w%d.%d" % (t, q), T.base[:, q:q + 1]
             either(f_ts(ap, ap, b, A.add), f_act(ap, ap, Act.Identity, bias=b), [k, "base"], [k], S, S)
         cp(w[:, O:W:S], T.base[:, 0:N], ["base"], ["w%d.col0" % t, "w%d.own1" % t, "w%d.z" % t])
 
     def fold(t):
-        ju, k, al = T["ju%d" % t], "ju%d" % t, T["al%d" % t]
-        win, wk = (T.rfi[:], ["rfi"]) if t == 1 else (T.tt[:, S:2 * S], ["tt.b0", "tt.b1"])
+        ju, k, dv = T["ju%d" % t], "ju%d" % t, T["dv%d" % t]
+        win, wk = (T.rfi[:], ["rfi", "rfi.z"]) if t == 1 else (T.rw[:], ["rw0", "rw1", "rw.z"])
         tt(T.ne[:], win.indirect(T.cdu[:]), T.rr[:], A.not_equal, ["rr0", "rr1", "cdu"] + wk, ["ne"], S * G)
+        mm(T.r1[:, CB:CB + 48], T.idf[:], T.cdf[:], True, False, ["idf", "cdf"], ["r1"], 256)
         for q in range(16):
-            mm(T.s0[:, 0:48], T.zb[:, 15 - q:143 - q], T.ne[:, q:S:16], q == 0, q == 15, ["zb", "ne"], ["s0"])
-        tt(T.lt[:, 0:48], T.s0[:, 0:48], T.lim[:, 0:48], A.min, ["s0", "lim"], ["lt.a"], 64)
-        tt(T.lt[:, 48:96], T.s0[:, 0:48], T.lim[:, 48:96], A.min, ["s0", "lim"], ["lt.b"], 64)
-        tt(T.lu[:], T.lt[:], T.lbase[:], A.add, ["lt.a", "lt.b", "lbase"], ["lu"], 192)
-        cp(ju[:], T.lu[:], ["lu"], [k], 96)
+            mm(T.r1[:, CB:CB + 48], T.zf[:, 15 - q:143 - q], T.ne[:, q:S:16], False, q == 15, ["zf", "ne"], ["r1"])
+        tt(T.lt[:], T.r1[:, CB:CB + 48], T.nl[:], A.min, ["r1", "nl"], ["lt"], 64)
+        cp(ju[:], T.lt[:], ["lt"], [k])
         if t == 1:
-            cp(T.ph2[:, own], T.yn[:].indirect(ju[:, 0:48]), ["yn", k], ["ph2.own"], S * G, True)
+            cp(T.szl[:, own], T.yn[:].indirect(ju[:]), ["yn", k], ["szl%d" % r], S * G, True)
             send_names(2)
         if t == 2:
-            cp(T.yj3[:], T.yn[:].indirect(ju[:, 0:48]), ["yn", k], ["yj3"], S * G, True)
-            cp(T.ph3[:, own], T.yj3[:].indirect(T.ju1[:, 0:48]), ["yj3", "ju1"], ["ph3.own"], S * G, True)
+            cp(T.yj3[:], T.yn[:].indirect(ju[:]), ["yn", k], ["yj3"], S * G, True)
+            cp(T.szl[:, own], T.yj3[:].indirect(T.ju1[:]), ["yj3", "ju1"], ["szl%d" % r], S * G, True)
             send_names(3)
-        cp(T.sza[:], T.szw[:].indirect(ju[:, 48:96]), ["szw", "szw.z", k], ["sza"], S * G, True)
-        either(f_ts(al[:], T.sza[:], 1.0, A.min), f_act(al[:], T.sza[:], Act.Sign), ["sza"], ["al%d" % t], S // 2, S)
         for h in range(2):
-            mm(qP[h], T.idn[:], T.sza[:, part[h]], True, False, ["idn", "sza"], [qK[h]], wid[h])
+            mm(rP[h], T.b18[:], T.ne[:, part[h]], True, True, ["b18", "ne"], [rK[h]], wid[h])
+            o = dv[:, part[h]]
+            either(f_ts(o, rP[h], 0.0, A.is_equal, GONE, A.mult), f_act(o, rP[h], Act.Relu, bias=GONE, scale=-GONE),
+                   [rK[h]], ["dv%d%d" % (t, h)], wid[h], wid[h])
+
+    def sides(t, h):
+        if t == 1:
+            mm(rP[h], T.idf[:], T.rr[:, part[h]], True, True, ["idf", "rr%d" % h], [rK[h]], 4 * wid[h])
+        tt(T.up[:, part[h]], rP[h], T.nf[:, part[h]], A.is_ge, [rK[h], "nf"], ["up%d" % h], wid[h])
+        for d in range(3):
+            dma("y", tl[h][32 * d:32 * d + 32, :], T.up[:, part[h]], ["up%d" % h], ["tl%d.%d" % (h, d)], P["tile"])
 
     def rename(t):
-        for u in range(16 * S // PU):
-            cp(T.gg[:, u * PU:(u + 1) * PU], T["ph%d" % t][:].indirect(offs(u * PU, PU)),
-               ["ph%d.own" % t, "ph%d.far" % t, "off"], ["gg%d" % u], PU * G, True)
-            if u >= P["ahead"]:
-                ops[-1]["after"].append(sent["last"])
+        for q in others:
+            nm = T.nm2[len(hs) * q:len(hs) * (q + 1)] if t == 2 else T.nm3[q]
+            dma("y", T.szl[0:128:8, q * S:(q + 1) * S], nm, ["nm%d.far" % t], ["szl%d" % q], P["tile"])
         for h in range(2):
+            pu = PU * 4 // 3 if h == 0 else PU * 2 // 3
+            for a in range(at(h, 0), at(h, 16), pu):
+                cp(T.gg[:, a:a + pu], T.szl[:].indirect(offs(a, pu)),
+                   ["szl%d" % q for q in range(N)] + ["off"], ["gg%d" % a], pu * G, True)
+                if a >= P["ahead"] * PU:
+                    ops[-1]["after"].append(sent["last"])
+            shift[0] = P["after"]
             for k in range(16):
-                mm(rP[h], T.zw[:, 15 - k:143 - k], blk(T.gg, h, k), k == 0, k == 15, ["zw", "gg%d" % (at(h, k) // PU)], [rK[h]], wid[h])
-
-    def renamed(t):
-        for h in range(2):
+                mm(rP[h], T.zw[:, 15 - k:143 - k], blk(T.gg, h, k), k == 0, k == 15,
+                   ["zw", "gg%d" % (at(h, 0) + k * wid[h] // pu * pu)], [rK[h]], wid[h])
+            sides(t, h)
             cp(T.rr[:, part[h]], rP[h], [rK[h]], ["rr%d" % h], wid[h], True)
-            gcopy(T.tt[:, S + h * CA:S + h * CA + wid[h]], T.rr[:, part[h]], ["rr%d" % h], ["tt.b%d" % h], wid[h])
+            gcopy(T.rw[:, part[h]], T.rr[:, part[h]], ["rr%d" % h], ["rw%d" % h], wid[h])
+            shift[0] = 0
         if t == RO:
             dma("y", T.yr[:], T.rr[:], ["rr0", "rr1"], [])
 
-    def far(t, h, extra):
+    def far(t, h):
         w = T["w%d" % t]
         wk = wkeys(t) + ["w%d.col0" % t, "w%d.z" % t, "ofa"]
         mine, mk = (T.ma, "ma") if h == 0 else (T.mb, "mb")
+        nk, modes, first = UNIT // wid[h], MODES[t - 1][h], [True]
+
+        def count(lhs, rhs, rd, last=False):
+            mm(cP[h], lhs, rhs, first[0], last, rd, [cK[h]], wid[h])
+            first[0] = False
+
         if t > 1:
-            mm(cP[h], T.idn[:], T.fa[:, part[h]], True, False, ["idn", "fa%d" % h], [cK[h]], wid[h])
-        k0 = 0
-        for i, kk in enumerate(STEPS[h]):
-            d, dk = blk(T.dd, h, k0, kk), ["dd%d.%d" % (h, i)]
-            tt(d, w[:].indirect(offs(at(h, k0), kk * wid[h], T.ofa)), mine[:, 0:kk * wid[h]], A.subtract,
-               wk + ["%s%d" % (mk, j) for j in range(kk)], dk, kk * wid[h] * G)
-            act(d, d, Act.Abs, dk, dk, kk * wid[h])
-            for k in range(k0, k0 + kk):
-                x, d, xk = blk(T.xx, h, k), blk(T.dd, h, k), "xx%d.%d" % (h, k)
-                either(f_ts(x, d, T.rch_f[:, k:k + 1], A.is_gt), f_act(x, d, Act.Relu, bias=T.rch_n[:, k:k + 1]),
-                       dk + ["rch", "rchn"], [xk], wid[h], wid[h])
-                mm(cP[h], T.zb[:, 15 - k:143 - k], x, t == 1 and k == 0, k == 15, ["zb", xk], [cK[h]], wid[h])
-            k0 += kk
-            for f in extra.get(i, []):
-                f()
+            count(T.id2[:], T["f%d" % (t - 1)][:, part[h]], ["id2", "f%d%d" % (t - 1, h)])
+        nc = modes.count("c")
+        if nc:
+            j = plain.index(nc * nk)
+            count(T.idc[:, 128 * j:128 * j + 128], T.up[:, part[h]], ["idc%d" % j, "up%d" % h])
+        todo = {False: list(range(len(modes) - nc)), True: list(range(len(modes) - nc, len(modes)))}
+        for n, mode in enumerate(modes):
+            u = todo[mode == "c"].pop(0)
+            xa, k0 = units[1] % 4 * UNIT, u * nk
+            units[1] += 1
+            d, x, dk = blk(T.dd, h, k0, nk), T.xx[:, xa:xa + UNIT], "dd%d.%d" % (h, u)
+            xk = ["xx%d" % (xa + j * UNIT // 4) for j in range(4)]
+            piece = lambda ap, a, j: ap[:, a + j * wid[h]:a + (j + 1) * wid[h]]
+            if mode != "c":
+                b = units[0] % 2
+                units[0] += 1
+                for j in range(nk):
+                    k, o, tk = k0 + j, piece(T.tp, b * UNIT, j), "t%d" % b
+                    if mode == "g":
+                        mm(o, T.idn[:], T.hi[:, part[h]], True, False, ["idn", "hi%d" % h], [tk], wid[h])
+                        mm(o, T.idh[:], T.lo[:, part[h]], False, False, ["idh", "lo%d" % h], [tk], wid[h])
+                    mm(o, T.wk[0:120, 128 * k:128 * k + 128], tl[h][0:120, k % 4 * wid[h]:(k % 4 + 1) * wid[h]], mode == "a", True,
+                       ["wk%d" % (k // 8), "tl%d.n" % h] + ["tl%d.%d" % (h, d) for d in range(3)], [tk], wid[h])
+            win = w[:, 0:W + O].indirect(offs(at(h, k0), UNIT, T.ofa))
+            if mode == "g":
+                act(d, win, Act.Copy, wk, [dk], UNIT * G)
+            else:
+                tt(d, win, mine[:], A.subtract, wk + ["%s%d" % (mk, j) for j in range(nk)], [dk], UNIT * G)
+            if mode == "c":
+                act(d, d, Act.Abs, [dk], [dk], UNIT)
+            else:
+                tt(x, d, T.tp[:, b * UNIT:(b + 1) * UNIT], A.is_le, [dk, tk], xk, UNIT)
+            for j in range(nk):
+                k, xj = k0 + j, xk[j * 4 // nk:(j + 1) * 4 // nk]
+                if mode == "c":
+                    o, a = piece(T.xx, xa, j), blk(T.dd, h, k)
+                    either(f_ts(o, a, T.rcn[:, k:k + 1], A.add, 0.0, A.max), f_act(o, a, Act.Relu, bias=T.rcn[:, k:k + 1]),
+                           [dk, "rcn"], xj, wid[h], wid[h])
+                count(T.zb[:, 15 - k:143 - k], piece(T.xx, xa, j), ["zb"] + xj, n == len(modes) - 1 and j == nk - 1)
+
+    def own_forms(t, h, copy):
+        m, mk = (T.ma, "ma") if h == 0 else (T.mb, "mb")
+        rd = ["pp0", "pp.z"] + ["pp1"] * h
+        for j in range(UNIT // wid[h]):
+            copy(m[:, j * wid[h]:(j + 1) * wid[h]], T.pp[:, part[h]], rd, ["%s%d" % (mk, j)], wid[h])
+        if "g" not in MODES[t - 1][h]:
+            return
+        copy(T.hi[:, part[h]], T.pp[:, part[h]], rd, ["hi%d" % h], wid[h])
+        if t > 1:
+            tt(T.lo[:, part[h]], T.pp[:, part[h]], T.hi[:, part[h]], A.subtract, rd + ["hi%d" % h], ["lo%d" % h], 2 * wid[h])
+            return
+        mm(T.c0[:, 0:wid[h]], T.idf[:], T.pp[:, part[h]], True, False, rd + ["idf"], ["c0"], 4 * wid[h])
+        mm(T.c0[:, 0:wid[h]], T.idm[:], T.hi[:, part[h]], False, True, ["idm", "hi%d" % h], ["c0"], wid[h])
+        cp(T.lo[:, part[h]], T.c0[:, 0:wid[h]], ["c0"], ["lo%d" % h], wid[h])
 
     def lengths(t, h):
-        tt(T.fa[:, part[h]], cP[h], T["al%d" % t][:, part[h]], A.min, [cK[h], "al%d" % t], ["fa%d" % h], wid[h])
-        mm(qP[h], T.b18[:], T.fa[:, part[h]], False, True, ["b18", "fa%d" % h], [qK[h]], wid[h])
+        f, fk = T["f%d" % t][:, part[h]], "f%d%d" % (t, h)
+        tt(f, cP[h], T.up[:, part[h]], A.not_equal, [cK[h], "up%d" % h], [fk], wid[h])
+        b = units[0] % 2
+        q, qk = (cP[0], "c0") if h == 0 else (T.tp[:, b * UNIT:b * UNIT + CB], "t%d" % b)
+        mm(q, T.idn[:], T.szb[:, part[h]], True, False, ["idn", "szb"], [qk], wid[h])
+        mm(q, T.idm[:], T["dv%d" % t][:, part[h]], False, False, ["idm", "dv%d%d" % (t, h)], [qk], wid[h])
+        mm(q, T.b18[:], f, False, True, ["b18", fk], [qk], wid[h])
+        o = T.ln[:, part[h]]
         if h == 0:
-            scan(T.pp[:, 1:CA + 1], qP[0], T.sza[:, part[0]], 0.0, ["q0", "sza"], ["pp0"], CA)
+            either(f_ts(o, q, 0.0, A.max), f_act(o, q, Act.Relu), [qk], ["ln0"], CA, CA)
+            scan(T.pp[:, 1:CA + 1], o, 0.0, ["ln0"], ["pp0"], CA)
         else:
-            scan(T.pp[:, CA + 1:S + 1], qP[1], T.sza[:, part[1]], T.pp[:, CA:CA + 1], ["q1", "sza", "pp0"], ["pp1"], CB)
+            ts(o, q, 0.0, A.max, [qk], ["ln1"], c=CB)
+            scan(T.pp[:, CA + 1:S + 1], o, T.pp[:, CA:CA + 1], ["ln1", "pp0"], ["pp1"], CB)
         if t < RO:
             w, lst, a = T["w%d" % (t + 1)], T["cl%d" % (t + 1)], r * S + O + 1
             la, lb = "cl%da" % (t + 1), "cl%db" % (t + 1)
@@ -425,138 +550,172 @@ def rank_program(g, core, T, topo):
                 cp(w[:, a:a + CA], T.pp[:, 0:CA + 1].indirect(lst[:, 0:CA // 16]), ["pp0", "pp.z", la], ["w%d.own0" % (t + 1)], CA * G, True)
             else:
                 cp(w[:, a + CA:a + S], T.pp[:, 0:S + 1].indirect(lst[:, CA // 16:48]), ["pp0", "pp1", "pp.z", la, lb],
-                   ["w%d.own1" % (t + 1)], CB * G, True)
+                   ["w%d.own1" % (t + 1)], CB * G)
                 sent["last"] = len(ops) - 2
             send_part(t + 1, h)
-            m, mk = (T.ma, "ma") if h == 0 else (T.mb, "mb")
-            for j in range(max(STEPS[h])):
-                gcopy(m[:, j * wid[h]:(j + 1) * wid[h]], T.pp[:, part[h]], ["pp0", "pp.z"] + ["pp1"] * h, ["%s%d" % (mk, j)], wid[h])
+            own_forms(t + 1, h, gcopy)
 
-    def marks(t, h):
-        f = T["f%d" % t][:, part[h]]
-        if t == 1:
-            either(f_ts(f, cP[h], 1.0, A.min), f_act(f, cP[h], Act.Sign), [cK[h]], ["f1%d" % h], wid[h], wid[h])
-        else:
-            tt(f, cP[h], T["al%d" % (t - 1)][:, part[h]], A.min, [cK[h], "al%d" % (t - 1)] + (["pp1"] if t == RO else []),
-               ["f%d%d" % (t, h)], wid[h])
-        if t == RO:
-            for u in range(1, RO + 1):
-                mm(rP[h], T.idn[:], T["f%d" % u][:, part[h]], u == 1, u == RO, ["idn", "f%d%d" % (u, h)], [rK[h]], wid[h])
-            o = T.tt[:, S + h * CA:S + h * CA + wid[h]]
-            either(f_ts(o, rP[h], 1.0, A.min), f_act(o, rP[h], Act.Sign), [rK[h]], ["tt.b%d" % h], wid[h], wid[h])
-            dma("y", T.yf[:, part[h]], o, ["tt.b%d" % h], [])
+    def marks(h, rd):
+        for u in range(1, RO + 1):
+            mm(rP[h], T.id2[:], T["f%d" % u][:, part[h]], u == 1, False, ["id2", "f%d%d" % (u, h)] + rd, [rK[h]], wid[h])
+        for u in range(1, RO):
+            mm(rP[h], T.idm[:], T["dv%d" % u][:, part[h]], False, u == RO - 1, ["idm", "dv%d%d" % (u, h)], [rK[h]], wid[h])
+        o = T.tt[:, S + h * CA:S + h * CA + wid[h]]
+        ts(o, rP[h], GONE, A.is_ge, [rK[h]], ["tt.b%d" % h], c=wid[h])
+        dma("y", T.yf[:, part[h]], o, ["tt.b%d" % h], [])
 
     dma("y", T.szi[:], T.sz[:], [], ["szi"], P["load"])
-    dma("y", T.rfi[:], T.rf[:], [], ["rfi"], P["load"] + 1.1)
+    dma("y", T.rfi[:, 0:S], T.rf[:], [], ["rfi"], P["load"] + 1.1)
     dma("s", T.cdi[:], T.cd[:], [], ["cdi"], P["load"] - 0.7)
     dma("s", T.rci[:], T.rch[:], [], ["rci"], P["load"])
     iota(T.pci[:, 0:1], [[0, 1]], 0, 1, ["pci0"], 1, False)
     iota(T.cc[:], [[1, 144]], 0, 0, ["cc"], 144)
+    iota(T.nl[:], [[16, 48]], 0, 0, ["nl"], 48)
     iota(T.l0[:, 0:32], [[1, 16], [256, 2]], 0, 0, ["l0a"], 32)
     iota(T.l0[:, 32:48], [[1, 16]], CA, 0, ["l0b"], 16)
-    iota(T.nl[:], [[16, 48]], 0, 0, ["nl"], 48)
     iota(T.cg[:], [[16, 8], [0, 16]], 0, 0, ["cg"], 128)
     iota(T.cm[:], [[0, 8], [1, 16]], 0, 0, ["cm"], 128)
+    iota(T.rfi[:, S:S + 16], [[0, 16]], -1, 0, ["rfi.z"], 16, False)
+    iota(T.pp[:, 0:1], [[0, 1]], 0, 0, ["pp.z"], 1)
     iota(T.hp[:], [[0, S // 64], [1, 64]], 0, 0, ["hp"], S)
-    cp(T.szw[:, 16:S + 16], T.szi[:], ["szi"], ["szw"], S)
+    cp(T.szb[:], T.szi[:], ["szi"], ["szb"], S)
+    scan(T.pp[:, 1:S + 1], T.szb[:], 0.0, ["szb"], ["pp0", "pp1"], S)
     for d, q in enumerate(others):
-        trz = [transfer(topo, T.cores[q], bits(off_e), T.sem["z%d" % (d + 1)], T.szw[:, 16:S + 16], T.szl[:, own])]
-        i = remote(trz, "lz", len(off_e) * (N - 1), ["szw"], P["z0"] + d * (P["z"] - P["call"]))
+        trz = [transfer(topo, T.cores[q], bits(off_e), T.sem["z%d" % (d + 1)], T.szb[:], T.szl[:, own])]
+        i = remote(trz, "lz", len(off_e) * (N - 1), ["szb"], P["z0"] + d * (P["z"] - P["call"]))
         arrive("z%d" % (d + 1), len(off_e), ["szl%d" % ((r - d - 1) % N)], [i])
+        if d == P["totat"]:
+            masks, ne = share(off_e, N - 1)
+            trs = [transfer(topo, T.cores[e], masks[j], T.sem.tt1, T.pp[:, S:S + 1], T.tot1[:, 4 * r:4 * r + 1]) for j, e in enumerate(others)]
+            i = remote(trs, "lt1", ne * (N - 1), ["pp1"], P["z0"] + d * (P["z"] - P["call"]))
+            arrive("tt1", ne * (N - 1), ["tot1"], [i])
     iota(T.yj3[:], [[1, S // 64], [0, 64]], r * S // 64, 0, ["yj3"], S)
-    for i, m in enumerate((15, 112, 16, 14, 1, 8, 7)):
+    iota(T.nf[:], [[1, S]], r * S, 0, ["nf"], S)
+    iota(T.rw[:, S:S + 16], [[0, 16]], -1, 0, ["rw.z"], 16)
+    for t in range(1, RO + 1):
+        iota(T["w%d" % t][:, 0:O + 1], [[0, O + 1]], 0, 0, ["w%d.z" % t], 8)
+    for i, m in enumerate((15, 112, 16, 14, 1, 8, 7, 124)):
         ts(T.pci[:, i + 1:i + 2], T.pci[:, 0:1], m, A.bitwise_and, ["pci0"], ["pci%d" % (i + 1)])
-    cp(T.pcf[:, 0:8], T.pci[:], ["pci%d" % i for i in range(8)], ["pcf"])
-    ts(col(8), col(5), 16.0, A.mult, ["pcf"], ["pc8"], col(3), A.not_equal)
-    ts(col(9), col(4), 16.0, A.mult, ["pcf"], ["pc9"], col(3), A.add)
-    ts(col(10), col(3), -2.0, A.mult, ["pcf"], ["pc10"], col(0), A.add)
-    ts(col(11), col(6), -7.875, A.mult, ["pcf"], ["pc11"], 64.0, A.add)
-    ts(col(12), col(7), 0.0, A.is_equal, ["pcf", "pc11"], ["pc12"], col(11), A.mult)
+    cp(T.pcf[:, 0:9], T.pci[:, 0:9], ["pci%d" % i for i in range(9)], ["pcf"])
+    fill(T.neg[:], -1.0, ["neg"], CA)
+    for j in range(4):
+        fill(T.src[:, j * CA:(j + 1) * CA], 0.0, ["src"], CA)
+    fill(T.f3[:], 1.0, ["f30", "f31"], S)
+    for h in range(2):
+        dma("y", tl[h][96:120, :], T.neg[0:96, 0:wid[h]], ["neg"], ["tl%d.n" % h], P["tile"])
+    ts(col(9), col(5), 16.0, A.mult, ["pcf"], ["pc9"], col(3), A.not_equal)
+    lin(col(10), col(4), 16.0, col(3), ["pcf"], ["pc10"])
+    lin(col(11), col(3), -2.0, col(0), ["pcf"], ["pc11"])
+    ts(col(12), col(7), 0.0, A.is_equal, ["pcf"], ["pc12"])
     ts(T.zb[:], T.cc[:], -15.0, A.add, ["cc", "pcf"], ["zb"], col(2), A.is_equal, 144)
-    ts(T.sw[:], T.cc[:, 0:128], -16.0, A.add, ["cc", "pc10"], ["sw"], col(10), A.is_equal, 128)
-    ts(col(13), col(8), float(S), A.mult, ["pc8", "pc9"], ["pc13"], col(9), A.add)
-    ts(T.zw[:], T.zb[:], col(12), A.mult, ["zb", "pc12"], ["zw"])
-    ts(T.zb[:], T.zb[:], 1024.0, A.mult, ["zb"], ["zb"])
-    cp(T.cdu[:], T.cdi[:], ["cdi"], ["cdu"])
-    cp(T.rr[:], T.rfi[:], ["rfi"], ["rr0", "rr1"], S)
+    ts(T.sw[:], T.cc[:, 0:128], -16.0, A.add, ["cc", "pc11"], ["sw"], col(11), A.is_equal, 128)
+    ts(T.idf[:], T.cc[:, 0:128], col(0), A.is_equal, ["cc", "pcf"], ["idf"], c=128)
+    lin(col(13), col(9), float(S), col(10), ["pc9", "pc10"], ["pc13"])
+    scaled(T.zw[:], T.zb[:], col(12), ["zb", "pc12"], ["zw"], 144)
+    scaled(T.zf[:], T.zb[:], 1024.0, ["zb"], ["zf"], 144)
+    scaled(T.zb[:], T.zb[:], 1 / 16, ["zb"], ["zb"], 144)
+    scaled(T.idn[:], T.idf[:], 1.0, ["idf"], ["idn"])
+    lin(T.nl[:], T.nl[:], 1.0, col(1), ["nl", "pcf"], ["nl"])
+    cp(T.cdf[:], T.cdi[:], ["cdi"], ["cdf"])
+    tt(T.lt[:], T.nl[:], T.cdi[:], A.is_equal, ["nl", "cdi"], ["lt"])
+    lin(T.lt[:], T.lt[:], 1024.0, 0.0, ["lt"], ["lt"])
+    tt(T.lt[:], T.lt[:], T.cdf[:], A.add, ["lt", "cdf"], ["lt"])
+    ts(T.cdu[:], T.lt[:], float(S), A.min, ["lt"], ["cdu"])
+    cp(T.rr[:], T.rfi[:, 0:S], ["rfi"], ["rr0", "rr1"], S)
+    lin(col(15), col(6), 0.125, 0.0, ["pcf"], ["pc15"])
+    lin(col(17), col(6), -8.0, 64.0, ["pcf"], ["pc17"])
+    scaled(T.dg2[:, 0:128], T.idf[:], col(15), ["idf", "pc15"], ["dg2a"])
+    scaled(T.dg2[:, 128:256], T.idf[:], col(17), ["idf", "pc17"], ["dg2b"])
+    for h in range(2):
+        mm(cP[h], T.dg2[:, 0:128], T.hp[:, part[h]], True, False, ["dg2a", "hp"], [cK[h]], wid[h])
+        mm(cP[h], T.dg2[:, 128:256], T.yj3[:, part[h]], False, True, ["dg2b", "yj3"], [cK[h]], wid[h])
+        cp(T.yn[:, part[h]], cP[h], [cK[h]], ["yn"], wid[h], True)
+    ts(col(14), col(1), 15.0, A.is_equal, ["pcf"], ["pc14"], float(S + r * S), A.mult)
+    lin(col(14), col(14), 1.0, float(-r * S), ["pc14"], ["pc14"])
+    ts(T.b18[:], T.cg[:], col(2), A.is_equal, ["cg", "pcf"], ["b18"], float(GROW), A.mult, 128)
     op({"v": (lambda: v.transpose(T.tt[:, 0:S], T.rr[:]), us(S))}, ["rr0", "rr1"], ["tt.a"])
     for h in range(2):
         mm(rP[h], T.sw[:], T.tt[:, part[h]], True, True, ["sw", "tt.a"], [rK[h]], 4 * wid[h])
-        act(T.tt[:, S + h * CA:S + h * CA + wid[h]], rP[h], Act.Copy, [rK[h]], ["tt.b%d" % h], wid[h])
-    ts(T.nl[:], T.nl[:], col(1), A.add, ["nl", "pcf"], ["nl"])
-    tt(T.lim[:, 0:48], T.nl[:], T.cdi[:], A.subtract, ["nl", "cdi"], ["lim.a"])
-    cp(T.lbase[:, 0:48], T.cdi[:], ["cdi"], ["lb.a"])
-    ts(T.nl[:], T.nl[:], 16.0, A.add, ["nl"], ["nl"])
-    ts(T.lbase[:, 48:96], T.lim[:, 0:48], 0.0, A.is_equal, ["lim.a"], ["lb.b"])
-    tt(T.lbase[:, 48:96], T.lbase[:, 48:96], T.nl[:], A.mult, ["lb.b", "nl", "lb.a"], ["lb.b", "lbase"])
-    tt(T.lim[:, 48:96], T.nl[:], T.lbase[:, 48:96], A.subtract, ["nl", "lbase", "lim.a"], ["lim"])
-    ms(T.szw[:, 0:16], 0.0, ["szw.z"])
-    ts(T.idn[:], T.cc[:, 0:128], col(0), A.is_equal, ["cc", "pcf"], ["idn"], c=128)
-    ts(col(15), col(6), 0.125, A.mult, ["pcf"], ["pc15"])
-    ts(col(0), col(6), -0.125, A.mult, ["pcf", "pc10", "idn"], ["pc0"], 1.0, A.add)
-    act(T.fa[:, 0:128], T.idn[:], Act.Copy, ["idn", "pc15"], ["fa0"], 128, scale=col(15))
-    act(T.fa[:, 128:256], T.idn[:], Act.Copy, ["idn", "pc0"], ["fa0"], 128, scale=col(0))
-    for h in range(2):
-        mm(cP[h], T.fa[:, 0:128], T.hp[:, part[h]], True, False, ["fa0", "hp"], [cK[h]], wid[h])
-        mm(cP[h], T.fa[:, 128:256], T.yj3[:, part[h]], False, True, ["fa0", "yj3"], [cK[h]], wid[h])
-        act(T.yn[:, part[h]], cP[h], Act.Copy, [cK[h]], ["yn"], wid[h])
-    ts(col(14), col(1), 15.0, A.is_equal, ["pcf"], ["pc14"], float(S + r * S), A.mult)
-    ts(col(14), col(14), float(-r * S), A.add, ["pc14"], ["pc14"])
+        cp(T.tt[:, S + h * CA:S + h * CA + wid[h]], rP[h], [rK[h]], ["tt.b%d" % h], wid[h], True)
+    scaled(T.idm[:], T.idf[:], -1.0, ["idf"], ["idm"])
+    gcopy(T.w1[:, r * S + O + 1:(r + 1) * S + O], T.pp[:, 1:S], ["pp0", "pp1"], ["w1.own0", "w1.own1"], S - 1)
+    own_forms(1, 0, gcopy)
+    fold(1)
     ts(T.l0u[:], T.l0[:], col(13), A.add, ["l0a", "l0b", "pc13"], ["l0u"])
     ts(T.ofa[:], T.tt[:].indirect(T.l0u[:]), float(O), A.add, ["tt.a", "tt.b0", "tt.b1", "l0u"], ["ofa"], c=S * G)
-    scan(T.w1[:, r * S + O + 1:(r + 1) * S + O + 1], T.szw[:, 16:S + 16], T.szw[:, 16:S + 16], 0.0, ["szw"], ["w1.own0", "w1.own1"], S)
-    for d in range(1, N):
-        q = (r - d) % N
-        scan(T.w1[:, q * S + O + 1:(q + 1) * S + O + 1], T.szl[:, q * S:(q + 1) * S], T.szl[:, q * S:(q + 1) * S], 0.0,
-             ["szl%d" % q], ["w1.%d" % q], S)
+    lin(col(18), col(2), -SPAN / 16, float((8 * N - 8 * r) * SPAN), ["pcf"], ["pc18"])
+    lin(col(19), col(2), SPAN / 16, float((8 * r + 1) * SPAN + 1), ["pcf"], ["pc19"])
+    ts(T.ud[:, 0:16], T.rci[:], col(18), A.min, ["rci", "pc18"], ["ud0"])
+    ts(T.ud[:, 16:32], T.rci[:], 1.0, A.add, ["rci", "pc19"], ["ud1"], col(19), A.min)
+    tt(T.wd[:, 0:16], T.ud[:, 0:16], T.ud[:, 16:32], A.add, ["ud0", "ud1"], ["wd0"])
+    cp(T.wd[:, 16:32], T.ud[:, 16:32], ["ud1"], ["wd1"])
+    for d in range(3):
+        ts(T.dg[:, 32 * d:32 * d + 32], T.wd[:], 255 << (8 * d), A.bitwise_and, ["wd0", "wd1"], ["dg%d" % d])
+    lin(col(20), col(1), 128.0, 0.0, ["pcf"], ["pc20"])
+    lin(col(21), col(8), 0.25, col(20), ["pcf", "pc20"], ["pc21"])
+    lin(col(22), col(2), 1 / 16, col(20), ["pcf", "pc20"], ["pc22"])
+    ts(T.sl[:, 0:6:2], T.cc[:, 0:96:32], col(21), A.add, ["cc", "pc21"], ["sl0"])
+    ts(T.sl[:, 1:7:2], T.cc[:, 96:120:8], col(22), A.add, ["cc", "pc22"], ["sl1"])
+    cp(T.src[:].indirect(T.sl[:, 0:6]), T.dg[:], ["sl0", "sl1", "dg0", "dg1", "dg2"], ["src"], 96 * 4)
+    for b in range(2):
+        for k in range(8 * b, 8 * b + 8):
+            mm(T.tp[:, 128 * k:128 * k + 128], T.src[:, 128 * k:128 * k + 128], T.idn[:], True, True, ["src", "idn"], ["t%d" % b], 128)
+        cp(T.wk[:, b * UNIT:(b + 1) * UNIT], T.tp[:, b * UNIT:(b + 1) * UNIT], ["t%d" % b], ["wk%d" % b], UNIT, True)
+    for h in range(2):
+        sides(1, h)
     ts(T.ee[:], T.cm[:], col(1), A.is_equal, ["cm", "pcf"], ["ee"], c=128)
     ts(T.el[:], T.cg[:], col(2), A.is_gt, ["cg", "pcf"], ["el"], c=128)
     tt(T.el[:], T.el[:], T.ee[:], A.mult, ["el", "ee"], ["el"], 256)
-    cp(T.rch_f[:], T.rci[:], ["rci"], ["rch"])
-    act(T.rch_n[:], T.rch_f[:], Act.Copy, ["rch"], ["rchn"], scale=-1.0)
-    for t in range(1, RO + 1):
-        ms(T["w%d" % t][:, 0:O + 1], 0.0, ["w%d.z" % t])
-    bases(1)
-    ms(T.pp[:, 0:1], 0.0, ["pp.z"])
-    ts(T.b18[:], T.cg[:], col(2), A.is_equal, ["cg", "pcf"], ["b18"], float(GROW), A.mult, 128)
-    act(T.pp[:, 1:S + 1], T.w1[:, r * S + O + 1:(r + 1) * S + O + 1], Act.Copy, ["w1.own0"], ["pp0", "pp1"], S)
-    for h, (m, mk) in enumerate(((T.ma, "ma"), (T.mb, "mb"))):
-        for j in range(max(STEPS[h])):
-            act(m[:, j * wid[h]:(j + 1) * wid[h]], T.pp[:, part[h]], Act.Copy, ["pp0", "pp1", "pp.z"], ["%s%d" % (mk, j)], wid[h])
+    scaled(T.id2[:], T.idf[:], GONE, ["idf"], ["id2"])
+    cp(T.idh[:], T.idf[:], ["idf"], ["idh"], 128)
+    for j, n in enumerate(plain):
+        ts(col(23 + j), col(1), float(16 - n), A.is_ge, ["pcf"], ["pc%d" % (23 + j)])
+        scaled(T.idc[:, 128 * j:128 * j + 128], T.idf[:], col(23 + j), ["idf", "pc%d" % (23 + j)], ["idc%d" % j])
+    if plain:
+        ts(T.rcn[:], T.rci[:], -1.0, A.mult, ["rci"], ["rcn"])
+    cp(T.tot1[:, 4 * r:4 * r + 1], T.pp[:, S:S + 1], ["pp1"], ["tot1.own"], 64, True)
+    starts(lambda a, b: T.tot1[:, 4 * a:4 * b:4], ["tot1", "tot1.own"])
+    for d in range(1, N):
+        q = (r - d) % N
+        op({"v": (lambda q=q: v.tensor_tensor_scan(T.w1[:, q * S + O + 1:(q + 1) * S + O], T.szl[:, q * S:(q + 1) * S - 1], T.f3[:, 0:S - 1],
+                                                   T.base[:, q:q + 1], A.add, A.mult), us(S))},
+           ["szl%d" % q, "base", "f30", "f31"], ["w1.%d" % q])
+    cp(T.w1[:, O:W:S], T.base[:, 0:N], ["base"], ["w1.col0", "w1.z"])
+    own_forms(1, 1, gcopy)
+    ts(T.off[:], T.ofa[:], float(-O), A.add, ["ofa"], ["off"], c=S // 2)
 
     for t in range(1, RO + 1):
-        far(t, 0, {P["fold"]: ([lambda: renamed(t)] if t > 1 else []) + [lambda: fold(t)]})
-        if t == 1:
-            ts(T.off[:], T.ofa[:], float(-O), A.add, ["ofa"], ["off"], c=S // 2)
-            iota(T.nf[:], [[1, S]], r * S, 0, ["nf"], S)
+        far(t, 0)
         lengths(t, 0)
-        far(t, 1, {3: [lambda: marks(t, 0)]} if t < RO else {})
+        far(t, 1)
         lengths(t, 1)
         if t < RO:
             bases(t + 1)
-            marks(t, 1)
             rename(t + 1)
+            shift[0] = P["after"]
+            fold(t + 1)
+            shift[0] = 0
 
     later = [q for q in range(N) if q > r]
     if later:
         masks, ne = share(off_e, len(later))
-        trs = [transfer(topo, T.cores[d], masks[i], T.sem.tt4, T.pp[:, S:S + 1], T.tot[:, 4 * r:4 * r + 1]) for i, d in enumerate(later)]
+        trs = [transfer(topo, T.cores[d], masks[i], T.sem.tt4, T.pp[:, S:S + 1], T.tot4[:, 4 * r:4 * r + 1]) for i, d in enumerate(later)]
         remote(trs, "lt4", ne * len(later), ["pp1"], P["tot"])
-    mm(T.s1[:, 0:1], T.el[:], T.pp[:, S:S + 1], True, r == 0, ["el", "pp1"], ["s1"], 256)
+    mm(T.c1[:, 0:1], T.el[:], T.pp[:, S:S + 1], True, r == 0, ["el", "pp1"], ["c1"], 256)
     ops[-1]["lat"] = P["tot"] if r > 0 else 0.0
     if r > 0:
-        arrive("tt4", sum(share(off_e, N - 1 - q)[1] for q in range(r)), ["tot"], [len(ops) - 1])
-    marks(RO, 0)
-    marks(RO, 1)
-    cp(T.tt[:, 0:S], T.nf[:].indirect(T.ju3[:, 0:48]), ["nf", "ju3", "pp1"], ["tt.a"], S * G, True)
+        arrive("tt4", sum(share(off_e, N - 1 - q)[1] for q in range(r)), ["tot4"], [len(ops) - 1])
+    for h in range(2):
+        marks(h, ["ln1"])
+    cp(T.tt[:, 0:S], T.nf[:].indirect(T.ju3[:]), ["nf", "ju3"], ["tt.a"], S * G, True)
     dma("y", T.yj[:], T.tt[0:128:16, 0:S], ["tt.a"], [])
     for q in range(r):
-        mm(T.s1[:, 0:1], T.ee[:], T.tot[:, 4 * q:4 * q + 1], False, q == r - 1, ["ee", "tot"], ["s1"], 256)
-    cp(T.base[:, 0:1], T.s1[:, 0:1], ["s1"], ["base"])
+        mm(T.c1[:, 0:1], T.ee[:], T.tot4[:, 4 * q:4 * q + 1], False, q == r - 1, ["ee", "tot4"], ["c1"], 256)
+    cp(T.base[:, 0:1], T.c1[:, 0:1], ["c1"], ["base"])
     for h in range(2):
         hf = slice(h * S // 2, (h + 1) * S // 2)
         rd, wr = ["pp0", "pp1", "pp.z", "base"], ["dd0.%d" % h]
-        out = T.dd[:, h * CA:h * CA + S // 2]
+        out = T.dd[:, h * UNIT:h * UNIT + S // 2]
         if h == 0:
             ts(out, T.pp[:, hf], T.base[:, 0:1], A.add, rd, wr, c=S // 2)
         else:

@@ -1,5 +1,5 @@
 from concourse.bass import DstId, RemoteDMATransfer
-from concourse.mybir import AluOpType, ActivationFunctionType
+from concourse.mybir import AluOpType, ActivationFunctionType, AxisListType
 
 N, S, RO, GROW = 5, 768, 3, 18
 W = N * S
@@ -11,11 +11,12 @@ UNIT = 1024
 GONE = 4096.0
 F32, BF, I32, U16, F16 = "float32", "bfloat16", "int32", "uint16", "float16"
 
-MODES = (("gaccgcga", "cgag"), ("caccgcag", "ggac"), ("gcaccgcc", "cagc"))
-PU = 768
-PLAN = {"g": 1.5, "cyc": 0.87e-3, "fix": 0.055, "sem": 0.06, "pe": 0.5e-3, "call": 0.7,
-        "pelat": 0.1, "spare": 1.0, "lov": 1, "totat": 0, "passes": 3, "shake": 2.0, "early": 1.5, "ahead": 99, "marks": 12, "after": -150,
-        "load": 3.0, "z0": 5.5, "z": 1.4, "direct": 6.5, "hop": 3.5, "relay": 11.0, "tot": 4.5, "tile": 4.5}
+MODES = (("aggcdadg", "gcda"), ("agaadgcd", "dcad"), ("gdagcdcd", "dcca"))
+PU = (1024, 512)
+PLAN = {"g": 1.5, "cyc": 0.87e-3, "fix": 0.055, "sem": 0.06, "pe": 0.5e-3, "pelat": 0.1, "call": 0.7, "gdma": 1.0,
+        "load": 3.0, "z0": 5.5, "z": 1.4, "direct": 6.5, "hop": 3.5, "relay": 11.0, "tot": 4.5, "tile": 3.5,
+        "nm": 4.5, "nrel": 6.0, "add": 3.5, "dq": 1.2, "spares": (0.7, 1.0, 1.4), "passes": 4, "tries": 1200, "after": -150}
+CASES = ((1.0, 1.0, 0.9, 1.0, 1.0), (1.3, 1.6, 1.0, 1.0, 1.4), (1.15, 0.9, 1.0, 1.2, 1.1), (1.1, 1.15, 1.7, 1.0, 1.3))
 
 SCRATCH = {
     "szi": ("sbuf", [128, S], I32), "rfi": ("sbuf", [128, S + 16], I32),
@@ -36,7 +37,7 @@ SCRATCH = {
     "tl0": ("sbuf", [128, 4 * CA], BF), "tl1": ("sbuf", [128, 4 * CB], BF), "neg": ("sbuf", [128, CA], BF),
     "src": ("sbuf", [128, 2048], BF), "wk": ("sbuf", [128, 2048], BF),
     "ud": ("sbuf", [128, 32], F32), "wd": ("sbuf", [128, 32], I32), "dg": ("sbuf", [128, 96], I32), "sl": ("sbuf", [128, 8], U16),
-    "nf": ("sbuf", [128, S], F32), "hp": ("sbuf", [128, S], BF), "yn": ("sbuf", [128, S], BF),
+    "nf": ("sbuf", [128, S], F32), "hp": ("sbuf", [128, 128], BF), "yn": ("sbuf", [128, S], BF),
     "yj3": ("sbuf", [128, S], BF), "dg2": ("sbuf", [128, 256], BF),
     "pci": ("sbuf", [128, 16], I32), "pcf": ("sbuf", [128, 32], F32),
     "cc": ("sbuf", [128, 144], F32), "cm": ("sbuf", [128, 128], F32), "cg": ("sbuf", [128, 128], F32),
@@ -54,8 +55,8 @@ SCRATCH = {
     "r0": ("psum", [128, 512], F32), "r1": ("psum", [128, 512], F32),
 }
 NDMA = 48
-SEMAPHORES = (["ev", "es", "et", "eg"] + ["d%d" % i for i in range(NDMA)]
-              + ["z1", "z2", "z3", "z4", "tt1", "a2", "a3", "p2", "p3", "tt4", "ha2", "ha3", "hp2", "hp3"]
+SEMAPHORES = (["ev", "es", "et", "eg"] + ["d%d" % i for i in range(NDMA)] + ["e%d" % i for i in range(36)]
+              + ["z1", "z2", "z3", "z4", "tt1", "a2", "a3", "p2", "p3", "tt4", "ha2", "ha3", "hp2"]
               + ["lz", "lt1", "la2", "la3", "lb2", "lb3", "lc2", "lc3", "lp2", "lp3", "lt4"])
 PSUM = ("c0", "c1", "r0", "r1", "t0", "t1")
 
@@ -88,12 +89,12 @@ def relay_program(g, core, T, topo, r, j, nh):
     far = [(r + d) % N for d in range(1, N)]
     cw = CR // nh
     on, off = topo.engines(T.cores[r], core), topo.engines(T.cores[r], T.cores[far[0]])
-    got = share([e for e in on if e not in off], nh)[1]
+    got = {"p": share([e for e in on if e not in off], nh)[1], "a": share(on, nh)[1]}
     masks, ne = share(topo.engines(core, T.cores[far[0]]), len(far))
     piece = lambda t: T["w%d" % t][:, r * S + O + 1 + j * cw:r * S + O + 1 + (j + 1) * cw]
     jobs = [("p2", T.nm2[nh * r + j])] + [("a%d" % t, piece(t)) for t in range(2, RO + 1)]
     for name, ap in jobs:
-        g.wait_ge(T.sem["h" + name], got)
+        g.wait_ge(T.sem["h" + name], got[name[0]])
         g.remote_dma_fused([transfer(topo, T.cores[d], masks[i], T.sem[name], ap, ap) for i, d in enumerate(far)],
                            local_sem=T.sem["l" + name])
     for name, _ in jobs:
@@ -119,16 +120,19 @@ def link(ops):
         o["deps"] = deps
         o["order"] = set(o["after"])
     last_g = None
-    for i in (i for i, o in enumerate(ops) if "g" in o["alt"]):
+    for i in (i for i, o in enumerate(ops) if "g" in o["alt"] and (not o["w"] or not o["r"])):
         if last_g is not None:
             ops[i]["order"].add(last_g)
         last_g = i
 
 
+KEPT = {}
+
+
 def arrange(ops):
     P = PLAN
     n = len(ops)
-    before, after = [[] for _ in ops], [[] for _ in ops]
+    before, after, lean = [[] for _ in ops], [[] for _ in ops], [0.0] * n
     for i, o in enumerate(ops):
         for d in o["deps"] | o["order"]:
             lag = 0.0
@@ -140,7 +144,7 @@ def arrange(ops):
     def place(prev, nxt, key, head):
         left = [len(x) for x in prev]
         pool = [i for i in range(n) if left[i] == 0]
-        busy = {e: [] for e in "vstgy"}
+        busy = {e: [] for e in "vstgyq"}
         start, end, eng, seq = [0.0] * n, [0.0] * n, [None] * n, []
         while pool:
             i = min(pool, key=lambda i: key[i])
@@ -157,7 +161,7 @@ def arrange(ops):
                     while p < len(row) and row[p][0] < t + cost:
                         t = max(t, row[p][1])
                         p += 1
-                bias = P["spare"] if e == "v" else 0.0
+                bias = lean[i] if e == "v" else 0.0
                 if best is None or t + cost + bias < best[0]:
                     best = (t + cost + bias, t, cost, e, p)
             _, start[i], cost, eng[i], p = best
@@ -171,22 +175,72 @@ def arrange(ops):
                     pool.append(u)
         return start, end, eng, seq
 
-    tail, best = [o["lat"] for o in ops], None
-    key = [float(o["rank"]) for o in ops]
-    seed = 1
-    for turn in range(P["passes"]):
-        start, end, eng, seq = place(before, after, key, [0.0] * n)
-        span = max(end[i] + tail[i] for i in range(n))
-        if best is None or span < best[0]:
-            best = (span, start, eng, seq, end)
-        late = [-(end[i] + tail[i]) for i in range(n)]
-        if turn % 3 == 2:
+    tail = [o["lat"] for o in ops]
+
+    def worth(start, eng, seq):
+        pos = {i: p for p, i in enumerate(seq)}
+        order = sorted(range(n), key=lambda i: (start[i], pos[i]))
+        total = 0.0
+        for calc, pick, tens, wait, scale in CASES:
+            end, free = [0.0] * n, {}
+            for i in order:
+                e, t = eng[i], 0.0
+                for d, lag in before[i]:
+                    if end[d] + lag * wait > t:
+                        t = end[d] + lag * wait
+                if e != "x":
+                    t = max(t, free.get(e, 0.0)) + ops[i]["alt"][e][1] * (tens if e == "t" else wait if e == "q" else pick if ops[i]["pick"] else calc)
+                    free[e] = t
+                end[i] = t
+            total += max(end[i] + tail[i] * wait for i in range(n)) / scale
+        return total
+
+    names, seen = [], {}
+    for o in ops:
+        k = ("".join(o["alt"]), len(o["r"]), len(o["w"]), o["line"])
+        seen[k] = seen.get(k, 0) + 1
+        names.append(k + (seen[k],))
+    if KEPT:
+        key = [KEPT[k][0] if k in KEPT else 1e6 + i for i, k in enumerate(names)]
+        for i, k in enumerate(names):
+            lean[i] = KEPT[k][1] if k in KEPT else 0.0
+        start, _, eng, seq = place(before, after, key, [0.0] * n)
+    else:
+        best = None
+        for spare in P["spares"]:
+            lean[:] = [spare] * n
+            key = [float(o["rank"]) for o in ops]
+            for _ in range(P["passes"]):
+                start, end, eng, seq = place(before, after, key, [0.0] * n)
+                got = worth(start, eng, seq)
+                if best is None or got < best[0]:
+                    best = (got, start, eng, seq)
+                back = place(after, before, [-(end[i] + tail[i]) for i in range(n)], tail)
+                key = [-back[1][i] for i in range(n)]
+        now, start, eng, seq = best
+        lean[:] = [-50.0 if e == "v" else 50.0 for e in eng]
+        state, span = [7], max(start)
+
+        def draw():
+            state[0] = (state[0] * 1103515245 + 12345) % 2 ** 31
+            return state[0] / 2 ** 31
+
+        for _ in range(P["tries"]):
+            c, w, a = draw() * span, 1.0 + 5.0 * draw(), 0.5 + 3.0 * draw()
+            key, old = list(start), list(lean)
             for i in range(n):
-                seed = (seed * 1103515245 + 12345) % 2 ** 31
-                late[i] = -(best[4][i] + tail[i]) + P["shake"] * seed / 2 ** 31
-        back = place(after, before, late, tail)
-        key = [-back[1][i] for i in range(n)]
-    _, start, eng, seq, _ = best
+                if c <= start[i] < c + w:
+                    key[i] += a * (draw() - 0.5)
+                    if len(ops[i]["alt"]) > 1 and draw() < 0.15:
+                        lean[i] = -lean[i]
+            other = place(before, after, key, [0.0] * n)
+            got = worth(other[0], other[2], other[3])
+            if got <= now:
+                now, start, eng, seq = got, other[0], other[2], other[3]
+            else:
+                lean[:] = old
+        for i, k in enumerate(names):
+            KEPT[k] = (start[i], -50.0 if eng[i] == "v" else 50.0)
     for i, o in enumerate(ops):
         o["e"] = eng[i]
         o["fn"] = o["alt"][eng[i]][0]
@@ -256,15 +310,18 @@ def rank_program(g, core, T, topo):
     P = PLAN
     G = P["g"]
     ops = []
-    ndma, shift, units = [0], [0], [0, 0]
+    ndma, nadd, shift, units, picked, stage = [0], [0], [0], [0, 0], [False], [0]
     plain = sorted({m[h].count("c") * UNIT // (CA, CB)[h] for m in MODES for h in range(2)} - {0})
 
     def op(alt, rd, wr, tok=None, inc=None, lat=0.0, after=()):
-        ops.append({"alt": alt, "r": list(rd), "w": list(wr), "tok": tok, "inc": inc, "lat": lat, "after": list(after), "early": 0.0,
-                    "rank": len(ops) + shift[0], "kind": "ren" if (list(wr) + [""])[0][:2] == "gg" else "any"})
+        ops.append({"alt": alt, "r": list(rd), "w": list(wr), "tok": tok, "inc": inc, "lat": lat, "after": list(after),
+                    "rank": len(ops) + shift[0], "pick": picked[0], "line": stage[0]})
+        picked[0] = False
         return len(ops) - 1
 
-    us = lambda c: P["fix"] + max(64, c) * P["cyc"]
+    def us(c):
+        picked[0] = isinstance(c, float)
+        return P["fix"] + max(64, c) * P["cyc"]
 
     def dma(e, out, in_, rd, wr, lat=3.0):
         q = {"s": sc, "y": g.sync}[e]
@@ -316,14 +373,17 @@ def rank_program(g, core, T, topo):
     def gcopy(out, in_, rd, wr, c):
         op({"g": (lambda: g.affine_select(out, in_, [[0, c]], A.is_gt, 0.0, 1, 0), 0.2 + 2 * c * P["cyc"])}, rd, wr)
 
+    def keep(out, in_, pattern, base, cmul, rd, wr):
+        op({"g": (lambda: g.affine_select(out, in_, pattern, A.is_gt, 0.0, base, cmul), 0.2 + 256 * P["cyc"])}, rd, wr)
+
     def ms(ap, val, wr, c=64):
         op({"v": (lambda: v.memset(ap, val), us(c))}, [], wr)
 
     def fill(ap, val, wr, c):
-        either(lambda: v.memset(ap, val), f_act(ap, T.hp[:, 0:c], Act.Identity, scale=0.0, bias=val), ["hp"], wr, c // 2, c)
+        either(lambda: v.memset(ap, val), f_act(ap, T.yj3[:, 0:c], Act.Identity, scale=0.0, bias=val), ["yj3"], wr, c // 2, c)
 
     def scan(out, data, init, rd, wr, c):
-        op({"v": (lambda: v.tensor_tensor_scan(out, data, data, init, A.add, A.max), us(c))}, rd, wr)
+        op({"v": (lambda: v.tensor_tensor_scan(out, data, data, init, A.min, A.subtract), us(c))}, rd, wr)
 
     def remote(trs, local, n, rd, lat):
         return op({"g": (lambda: g.remote_dma_fused(trs, local_sem=T.sem[local]), P["call"])}, rd, [], (local, n), None, lat)
@@ -346,13 +406,13 @@ def rank_program(g, core, T, topo):
     offs = lambda a, n, b=T.off: b[:, a // 16:(a + n) // 16]
     sent = {}
 
-    def to_helpers(w, a, n, sem, local, key):
+    def to_helpers(w, a, n, sem, local, key, rest):
         cw = n // len(hs)
-        masks, ne = share(on_e if n == S else [e for e in on_e if e not in off_e], len(hs))
+        masks, ne = share(on_e, len(hs))
         trs = [transfer(topo, c, masks[j], T.sem[sem], w[:, a + j * cw:a + (j + 1) * cw], w[:, a + j * cw:a + (j + 1) * cw])
                for j, c in enumerate(hs)]
         i = remote(trs, local, ne * len(hs), key, P["hop"])
-        return op({"x": (None, 0.0)}, [], [], None, None, P["relay"] - P["hop"], [i])
+        return op({"q": (None, 2.0)}, [], [], None, None, rest + P["hop"] - 2.0, [i])
 
     def send_part(t, h):
         w = T["w%d" % t]
@@ -360,29 +420,30 @@ def rank_program(g, core, T, topo):
         a = r * S + O + 1 + h * CA
         masks, ne = share(off_e, N - 1)
         if h == 0:
-            sent[t] = to_helpers(w, a, CR, "ha%d" % t, "lb%d" % t, [key])
-            ap = w[:, a + CR:a + CA]
-            remote([transfer(topo, T.cores[d], masks[i], T.sem["a%d" % t], ap, ap) for i, d in enumerate(others)],
-                   "lc%d" % t, ne * (N - 1), [key], P["direct"])
+            sent[t] = to_helpers(w, a, CR, "ha%d" % t, "lb%d" % t, [key], P["relay"] - P["hop"])
+            if CR < CA:
+                ap = w[:, a + CR:a + CA]
+                remote([transfer(topo, T.cores[d], masks[i], T.sem["a%d" % t], ap, ap) for i, d in enumerate(others)],
+                       "lc%d" % t, ne * (N - 1), [key], P["direct"])
         else:
             trs = [transfer(topo, T.cores[d], masks[i], T.sem["a%d" % t], w[:, a:a + CB], w[:, a:a + CB]) for i, d in enumerate(others)]
             i = remote(trs, "la%d" % t, ne * (N - 1), [key], P["direct"] - 2.0)
-            i = op({"x": (None, 0.0)}, [], [], None, None, 2.0, [i])
-            arrive("a%d" % t, ne * (N - 1) * (2 + len(hs)), ["w%d.%d" % (t, q) for q in others], [sent[t], i])
+            i = op({"q": (None, 3.0)}, [], [], None, None, P["direct"] - 3.0, [i])
+            arrive("a%d" % t, ne * (N - 1) * (1 + (CR < CA) + len(hs)), ["w%d.%d" % (t, q) for q in others], [sent[t], i])
 
     def send_names(t):
         w, cl, nm = T.szl, T["cl%d" % t], T["nm%d" % t]
         masks, ne = share(off_e, N - 1)
         if t == 2:
             nh = len(hs)
-            dma("y", nm[nh * r:nh * r + nh], w[0:128:8, own], ["szl%d" % r], ["nm2.own"], P["tile"])
+            dma("y", nm[nh * r:nh * r + nh], w[0:128:8, own], ["szl%d" % r], ["nm2.own"], P["nm"])
             inner, ni = share([e for e in on_e if e not in off_e], nh)
             i = remote([transfer(topo, c, inner[j], T.sem.hp2, nm[nh * r + j], nm[nh * r + j]) for j, c in enumerate(hs)],
                        "lp2", ni * nh, ["nm2.own"], P["hop"])
-            i = op({"x": (None, 0.0)}, [], [], None, None, P["relay"] - P["hop"] - 1.0, [i])
+            i = op({"x": (None, 0.0)}, [], [], None, None, P["nrel"], [i])
             arrive("p2", ne * (N - 1) * nh, ["nm2.far"], [i])
         else:
-            dma("y", nm[r], w[0:128:8, own], ["szl%d" % r], ["nm%d.own" % t], P["tile"])
+            dma("y", nm[r], w[0:128:8, own], ["szl%d" % r], ["nm%d.own" % t], P["nm"])
             i = remote([transfer(topo, T.cores[d], masks[j], T.sem["p%d" % t], nm[r], nm[r]) for j, d in enumerate(others)],
                        "lp%d" % t, ne * (N - 1), ["nm%d.own" % t], P["tot"])
             arrive("p%d" % t, ne * (N - 1), ["nm%d.far" % t], [i])
@@ -396,12 +457,11 @@ def rank_program(g, core, T, topo):
     def wkeys(t):
         return ["w%d.%d" % (t, q) for q in others] + ["w%d.own0" % t, "w%d.own1" % t]
 
-    def starts(tot, rd):
+    def starts(tot, rd, sign=1.0):
         mm(T.c1[:, CB:CB + N], T.el[:], tot(0, N), True, False, rd + ["el"], ["c1"], 256)
-        ops[-1]["early"] = P["early"]
         for s in range(1, N):
             mm(T.c1[:, CB + s:CB + N], T.ee[:], tot(0, N - s), False, s == N - 1, rd + ["ee"], ["c1"], 256)
-        ts(T.base[:, 0:N], T.c1[:, CB:CB + N], T.c1[:, CB + r:CB + r + 1], A.subtract, ["c1"], ["base"])
+        ts(T.base[:, 0:N], T.c1[:, CB:CB + N], T.c1[:, CB + r:CB + r + 1], A.subtract, ["c1"], ["base"], sign, A.mult)
 
     def bases(t):
         w = T["w%d" % t]
@@ -438,19 +498,19 @@ def rank_program(g, core, T, topo):
             mm(rP[h], T.idf[:], T.rr[:, part[h]], True, True, ["idf", "rr%d" % h], [rK[h]], 4 * wid[h])
         tt(T.up[:, part[h]], rP[h], T.nf[:, part[h]], A.is_ge, [rK[h], "nf"], ["up%d" % h], wid[h])
         for d in range(3):
-            dma("y", tl[h][32 * d:32 * d + 32, :], T.up[:, part[h]], ["up%d" % h], ["tl%d.%d" % (h, d)], P["tile"])
+            k = ["tl%d.%d" % (h, d)]
+            dma("y", tl[h][32 * d:32 * d + 32, :], T.up[:, part[h]], ["up%d" % h], k, 0.0)
+            op({"q": (None, 0.4)}, ["up%d" % h], k, ops[-1]["tok"], None, P["tile"] - 0.4)
 
     def rename(t):
         for q in others:
             nm = T.nm2[len(hs) * q:len(hs) * (q + 1)] if t == 2 else T.nm3[q]
-            dma("y", T.szl[0:128:8, q * S:(q + 1) * S], nm, ["nm%d.far" % t], ["szl%d" % q], P["tile"])
+            dma("y", T.szl[0:128:8, q * S:(q + 1) * S], nm, ["nm%d.far" % t], ["szl%d" % q], P["nm"])
+        wk = ["szl%d" % q for q in range(N)]
         for h in range(2):
-            pu = PU * 4 // 3 if h == 0 else PU * 2 // 3
+            pu = PU[h]
             for a in range(at(h, 0), at(h, 16), pu):
-                cp(T.gg[:, a:a + pu], T.szl[:].indirect(offs(a, pu)),
-                   ["szl%d" % q for q in range(N)] + ["off"], ["gg%d" % a], pu * G, True)
-                if a >= P["ahead"] * PU:
-                    ops[-1]["after"].append(sent["last"])
+                cp(T.gg[:, a:a + pu], T.szl[:].indirect(offs(a, pu)), wk + ["off"], ["gg%d" % a], pu * G, True)
             shift[0] = P["after"]
             for k in range(16):
                 mm(rP[h], T.zw[:, 15 - k:143 - k], blk(T.gg, h, k), k == 0, k == 15,
@@ -475,11 +535,11 @@ def rank_program(g, core, T, topo):
         if t > 1:
             count(T.id2[:], T["f%d" % (t - 1)][:, part[h]], ["id2", "f%d%d" % (t - 1, h)])
         nc = modes.count("c")
-        if nc:
-            j = plain.index(nc * nk)
-            count(T.idc[:, 128 * j:128 * j + 128], T.up[:, part[h]], ["idc%d" % j, "up%d" % h])
         todo = {False: list(range(len(modes) - nc)), True: list(range(len(modes) - nc, len(modes)))}
         for n, mode in enumerate(modes):
+            if nc and n == len(modes) - 2:
+                j = plain.index(nc * nk)
+                count(T.idc[:, 128 * j:128 * j + 128], T.up[:, part[h]], ["idc%d" % j, "up%d" % h])
             u = todo[mode == "c"].pop(0)
             xa, k0 = units[1] % 4 * UNIT, u * nk
             units[1] += 1
@@ -492,15 +552,21 @@ def rank_program(g, core, T, topo):
                 for j in range(nk):
                     k, o, tk = k0 + j, piece(T.tp, b * UNIT, j), "t%d" % b
                     if mode == "g":
-                        mm(o, T.idn[:], T.hi[:, part[h]], True, False, ["idn", "hi%d" % h], [tk], wid[h])
+                        mm(o, T.idm[:], T.hi[:, part[h]], True, False, ["idm", "hi%d" % h], [tk], wid[h])
                         mm(o, T.idh[:], T.lo[:, part[h]], False, False, ["idh", "lo%d" % h], [tk], wid[h])
-                    mm(o, T.wk[0:120, 128 * k:128 * k + 128], tl[h][0:120, k % 4 * wid[h]:(k % 4 + 1) * wid[h]], mode == "a", True,
+                    mm(o, T.wk[0:120, 128 * k:128 * k + 128], tl[h][0:120, k % 4 * wid[h]:(k % 4 + 1) * wid[h]], mode != "g", True,
                        ["wk%d" % (k // 8), "tl%d.n" % h] + ["tl%d.%d" % (h, d) for d in range(3)], [tk], wid[h])
             win = w[:, 0:W + O].indirect(offs(at(h, k0), UNIT, T.ofa))
-            if mode == "g":
+            mks = ["%s%d" % (mk, j) for j in range(nk)]
+            if mode in "gd":
                 act(d, win, Act.Copy, wk, [dk], UNIT * G)
             else:
-                tt(d, win, mine[:], A.subtract, wk + ["%s%d" % (mk, j) for j in range(nk)], [dk], UNIT * G)
+                tt(d, win, mine[:], A.add, wk + mks, [dk], UNIT * G)
+            if mode == "d":
+                tok = ("e%d" % nadd[0], 16)
+                op({"g": (lambda d=d: g.dma_start(d, mine[:], accum_op=A.add), P["gdma"])}, [dk] + mks, [dk], tok, 16)
+                op({"q": (None, P["dq"])}, [dk] + mks, [dk], tok, None, P["add"] - P["dq"])
+                nadd[0] += 1
             if mode == "c":
                 act(d, d, Act.Abs, [dk], [dk], UNIT)
             else:
@@ -541,17 +607,20 @@ def rank_program(g, core, T, topo):
             either(f_ts(o, q, 0.0, A.max), f_act(o, q, Act.Relu), [qk], ["ln0"], CA, CA)
             scan(T.pp[:, 1:CA + 1], o, 0.0, ["ln0"], ["pp0"], CA)
         else:
-            ts(o, q, 0.0, A.max, [qk], ["ln1"], c=CB)
+            if t < RO:
+                ts(o, q, 0.0, A.max, [qk], ["ln1"], c=CB)
+            else:
+                scaled(T.base[:, 4:5], T.pp[:, CA:CA + 1], -1.0, ["pp0"], ["sum0", "base"], 64)
+                act(o, q, Act.Relu, [qk], ["ln1", "sum1"], CB, accum_out=T.base[:, 5:6])
             scan(T.pp[:, CA + 1:S + 1], o, T.pp[:, CA:CA + 1], ["ln1", "pp0"], ["pp1"], CB)
         if t < RO:
             w, lst, a = T["w%d" % (t + 1)], T["cl%d" % (t + 1)], r * S + O + 1
             la, lb = "cl%da" % (t + 1), "cl%db" % (t + 1)
             if h == 0:
-                cp(w[:, a:a + CA], T.pp[:, 0:CA + 1].indirect(lst[:, 0:CA // 16]), ["pp0", "pp.z", la], ["w%d.own0" % (t + 1)], CA * G, True)
+                scaled(w[:, a:a + CA], T.pp[:, 0:CA + 1].indirect(lst[:, 0:CA // 16]), -1.0, ["pp0", "pp.z", la], ["w%d.own0" % (t + 1)], CA * G)
             else:
-                cp(w[:, a + CA:a + S], T.pp[:, 0:S + 1].indirect(lst[:, CA // 16:48]), ["pp0", "pp1", "pp.z", la, lb],
-                   ["w%d.own1" % (t + 1)], CB * G)
-                sent["last"] = len(ops) - 2
+                ts(w[:, a + CA:a + S], T.pp[:, 0:S + 1].indirect(lst[:, CA // 16:48]), -1.0, A.mult, ["pp0", "pp1", "pp.z", la, lb],
+                   ["w%d.own1" % (t + 1)], c=CB * G)
             send_part(t + 1, h)
             own_forms(t + 1, h, gcopy)
 
@@ -571,25 +640,25 @@ def rank_program(g, core, T, topo):
     iota(T.pci[:, 0:1], [[0, 1]], 0, 1, ["pci0"], 1, False)
     iota(T.cc[:], [[1, 144]], 0, 0, ["cc"], 144)
     iota(T.nl[:], [[16, 48]], 0, 0, ["nl"], 48)
-    iota(T.l0[:, 0:32], [[1, 16], [256, 2]], 0, 0, ["l0a"], 32)
-    iota(T.l0[:, 32:48], [[1, 16]], CA, 0, ["l0b"], 16)
     iota(T.cg[:], [[16, 8], [0, 16]], 0, 0, ["cg"], 128)
     iota(T.cm[:], [[0, 8], [1, 16]], 0, 0, ["cm"], 128)
     iota(T.rfi[:, S:S + 16], [[0, 16]], -1, 0, ["rfi.z"], 16, False)
-    iota(T.pp[:, 0:1], [[0, 1]], 0, 0, ["pp.z"], 1)
-    iota(T.hp[:], [[0, S // 64], [1, 64]], 0, 0, ["hp"], S)
+    iota(T.yj3[:], [[1, S // 64], [0, 64]], r * S // 64, 0, ["yj3"], S)
     cp(T.szb[:], T.szi[:], ["szi"], ["szb"], S)
     scan(T.pp[:, 1:S + 1], T.szb[:], 0.0, ["szb"], ["pp0", "pp1"], S)
     for d, q in enumerate(others):
         trz = [transfer(topo, T.cores[q], bits(off_e), T.sem["z%d" % (d + 1)], T.szb[:], T.szl[:, own])]
         i = remote(trz, "lz", len(off_e) * (N - 1), ["szb"], P["z0"] + d * (P["z"] - P["call"]))
         arrive("z%d" % (d + 1), len(off_e), ["szl%d" % ((r - d - 1) % N)], [i])
-        if d == P["totat"]:
+        if d == 0:
             masks, ne = share(off_e, N - 1)
             trs = [transfer(topo, T.cores[e], masks[j], T.sem.tt1, T.pp[:, S:S + 1], T.tot1[:, 4 * r:4 * r + 1]) for j, e in enumerate(others)]
-            i = remote(trs, "lt1", ne * (N - 1), ["pp1"], P["z0"] + d * (P["z"] - P["call"]))
+            i = remote(trs, "lt1", ne * (N - 1), ["pp1"], P["z0"])
             arrive("tt1", ne * (N - 1), ["tot1"], [i])
-    iota(T.yj3[:], [[1, S // 64], [0, 64]], r * S // 64, 0, ["yj3"], S)
+    iota(T.pp[:, 0:1], [[0, 1]], 0, 0, ["pp.z"], 1)
+    iota(T.hp[:], [[0, 2], [1, 64]], 0, 0, ["hp"], 128)
+    iota(T.l0[:, 0:32], [[1, 16], [256, 2]], 0, 0, ["l0a"], 32)
+    iota(T.l0[:, 32:48], [[1, 16]], CA, 0, ["l0b"], 16)
     iota(T.nf[:], [[1, S]], r * S, 0, ["nf"], S)
     iota(T.rw[:, S:S + 16], [[0, 16]], -1, 0, ["rw.z"], 16)
     for t in range(1, RO + 1):
@@ -597,12 +666,12 @@ def rank_program(g, core, T, topo):
     for i, m in enumerate((15, 112, 16, 14, 1, 8, 7, 124)):
         ts(T.pci[:, i + 1:i + 2], T.pci[:, 0:1], m, A.bitwise_and, ["pci0"], ["pci%d" % (i + 1)])
     cp(T.pcf[:, 0:9], T.pci[:, 0:9], ["pci%d" % i for i in range(9)], ["pcf"])
-    fill(T.neg[:], -1.0, ["neg"], CA)
+    ms(T.neg[:], -1.0, ["neg"], CA // 2)
     for j in range(4):
         fill(T.src[:, j * CA:(j + 1) * CA], 0.0, ["src"], CA)
     fill(T.f3[:], 1.0, ["f30", "f31"], S)
-    for h in range(2):
-        dma("y", tl[h][96:120, :], T.neg[0:96, 0:wid[h]], ["neg"], ["tl%d.n" % h], P["tile"])
+    dma("y", T.tl0[96:120, :], T.neg[0:96, 0:CA], ["neg"], ["tl0.n"], P["tile"])
+    op({"g": (lambda: g.dma_start(T.tl1[96:120, :], T.neg[0:96, 0:CB]), P["gdma"])}, ["neg", "nf"], ["tl1.n"], ("e35", 16), 16, P["tile"])
     ts(col(9), col(5), 16.0, A.mult, ["pcf"], ["pc9"], col(3), A.not_equal)
     lin(col(10), col(4), 16.0, col(3), ["pcf"], ["pc10"])
     lin(col(11), col(3), -2.0, col(0), ["pcf"], ["pc11"])
@@ -616,8 +685,8 @@ def rank_program(g, core, T, topo):
     scaled(T.zb[:], T.zb[:], 1 / 16, ["zb"], ["zb"], 144)
     scaled(T.idn[:], T.idf[:], 1.0, ["idf"], ["idn"])
     lin(T.nl[:], T.nl[:], 1.0, col(1), ["nl", "pcf"], ["nl"])
-    cp(T.cdf[:], T.cdi[:], ["cdi"], ["cdf"])
-    tt(T.lt[:], T.nl[:], T.cdi[:], A.is_equal, ["nl", "cdi"], ["lt"])
+    cp(T.cdf[:], T.cdi[:], ["cdi", "szb"], ["cdf"])
+    tt(T.lt[:], T.nl[:], T.cdi[:], A.is_equal, ["nl", "cdi", "szb"], ["lt"])
     lin(T.lt[:], T.lt[:], 1024.0, 0.0, ["lt"], ["lt"])
     tt(T.lt[:], T.lt[:], T.cdf[:], A.add, ["lt", "cdf"], ["lt"])
     ts(T.cdu[:], T.lt[:], float(S), A.min, ["lt"], ["cdu"])
@@ -627,8 +696,9 @@ def rank_program(g, core, T, topo):
     scaled(T.dg2[:, 0:128], T.idf[:], col(15), ["idf", "pc15"], ["dg2a"])
     scaled(T.dg2[:, 128:256], T.idf[:], col(17), ["idf", "pc17"], ["dg2b"])
     for h in range(2):
-        mm(cP[h], T.dg2[:, 0:128], T.hp[:, part[h]], True, False, ["dg2a", "hp"], [cK[h]], wid[h])
-        mm(cP[h], T.dg2[:, 128:256], T.yj3[:, part[h]], False, True, ["dg2b", "yj3"], [cK[h]], wid[h])
+        mm(cP[h], T.dg2[:, 128:256], T.yj3[:, part[h]], True, False, ["dg2b", "yj3"], [cK[h]], wid[h])
+        for a in range(0, wid[h], 128):
+            mm((T.c0, T.c1)[h][:, a:a + 128], T.dg2[:, 0:128], T.hp[:], False, a + 128 == wid[h], ["dg2a", "hp"], [cK[h]], 128)
         cp(T.yn[:, part[h]], cP[h], [cK[h]], ["yn"], wid[h], True)
     ts(col(14), col(1), 15.0, A.is_equal, ["pcf"], ["pc14"], float(S + r * S), A.mult)
     lin(col(14), col(14), 1.0, float(-r * S), ["pc14"], ["pc14"])
@@ -638,15 +708,15 @@ def rank_program(g, core, T, topo):
         mm(rP[h], T.sw[:], T.tt[:, part[h]], True, True, ["sw", "tt.a"], [rK[h]], 4 * wid[h])
         cp(T.tt[:, S + h * CA:S + h * CA + wid[h]], rP[h], [rK[h]], ["tt.b%d" % h], wid[h], True)
     scaled(T.idm[:], T.idf[:], -1.0, ["idf"], ["idm"])
-    gcopy(T.w1[:, r * S + O + 1:(r + 1) * S + O], T.pp[:, 1:S], ["pp0", "pp1"], ["w1.own0", "w1.own1"], S - 1)
-    own_forms(1, 0, gcopy)
+    scaled(T.w1[:, r * S + O + 1:(r + 1) * S + O + 1], T.pp[:, 1:S + 1], -1.0, ["pp0", "pp1"], ["w1.own0", "w1.own1", "w1.z"], S)
+    own_forms(1, 0, lambda out, in_, rd, wr, c: cp(out, in_, rd, wr, c, True))
     fold(1)
     ts(T.l0u[:], T.l0[:], col(13), A.add, ["l0a", "l0b", "pc13"], ["l0u"])
     ts(T.ofa[:], T.tt[:].indirect(T.l0u[:]), float(O), A.add, ["tt.a", "tt.b0", "tt.b1", "l0u"], ["ofa"], c=S * G)
     lin(col(18), col(2), -SPAN / 16, float((8 * N - 8 * r) * SPAN), ["pcf"], ["pc18"])
     lin(col(19), col(2), SPAN / 16, float((8 * r + 1) * SPAN + 1), ["pcf"], ["pc19"])
-    ts(T.ud[:, 0:16], T.rci[:], col(18), A.min, ["rci", "pc18"], ["ud0"])
-    ts(T.ud[:, 16:32], T.rci[:], 1.0, A.add, ["rci", "pc19"], ["ud1"], col(19), A.min)
+    ts(T.ud[:, 0:16], T.rci[:], col(18), A.min, ["rci", "pc18", "szb"], ["ud0"])
+    ts(T.ud[:, 16:32], T.rci[:], 1.0, A.add, ["rci", "pc19", "szb"], ["ud1"], col(19), A.min)
     tt(T.wd[:, 0:16], T.ud[:, 0:16], T.ud[:, 16:32], A.add, ["ud0", "ud1"], ["wd0"])
     cp(T.wd[:, 16:32], T.ud[:, 16:32], ["ud1"], ["wd1"])
     for d in range(3):
@@ -664,23 +734,20 @@ def rank_program(g, core, T, topo):
     for h in range(2):
         sides(1, h)
     ts(T.ee[:], T.cm[:], col(1), A.is_equal, ["cm", "pcf"], ["ee"], c=128)
-    ts(T.el[:], T.cg[:], col(2), A.is_gt, ["cg", "pcf"], ["el"], c=128)
-    tt(T.el[:], T.el[:], T.ee[:], A.mult, ["el", "ee"], ["el"], 256)
+    keep(T.el[:], T.ee[:], [[16, 8], [0, 16]], 0, -1, ["ee", "hp"], ["el"])
     scaled(T.id2[:], T.idf[:], GONE, ["idf"], ["id2"])
-    cp(T.idh[:], T.idf[:], ["idf"], ["idh"], 128)
+    ts(T.idh[:], T.idf[:], -1.0, A.mult, ["idf"], ["idh"], c=128)
     for j, n in enumerate(plain):
-        ts(col(23 + j), col(1), float(16 - n), A.is_ge, ["pcf"], ["pc%d" % (23 + j)])
-        scaled(T.idc[:, 128 * j:128 * j + 128], T.idf[:], col(23 + j), ["idf", "pc%d" % (23 + j)], ["idc%d" % j])
-    if plain:
-        ts(T.rcn[:], T.rci[:], -1.0, A.mult, ["rci"], ["rcn"])
+        keep(T.idc[:, 128 * j:128 * j + 128], T.idf[:], [[0, 8], [1, 16]], n - 15, 0, ["idf", "nf"], ["idc%d" % j])
+    ts(T.rcn[:], T.rci[:], -1.0, A.mult, ["rci"], ["rcn"])
     cp(T.tot1[:, 4 * r:4 * r + 1], T.pp[:, S:S + 1], ["pp1"], ["tot1.own"], 64, True)
-    starts(lambda a, b: T.tot1[:, 4 * a:4 * b:4], ["tot1", "tot1.own"])
+    starts(lambda a, b: T.tot1[:, 4 * a:4 * b:4], ["tot1", "tot1.own"], -1.0)
+    cp(T.w1[:, O:W:S], T.base[:, 0:N], ["base"], ["w1.col0", "w1.z"])
     for d in range(1, N):
         q = (r - d) % N
         op({"v": (lambda q=q: v.tensor_tensor_scan(T.w1[:, q * S + O + 1:(q + 1) * S + O], T.szl[:, q * S:(q + 1) * S - 1], T.f3[:, 0:S - 1],
                                                    T.base[:, q:q + 1], A.add, A.mult), us(S))},
            ["szl%d" % q, "base", "f30", "f31"], ["w1.%d" % q])
-    cp(T.w1[:, O:W:S], T.base[:, 0:N], ["base"], ["w1.col0", "w1.z"])
     own_forms(1, 1, gcopy)
     ts(T.off[:], T.ofa[:], float(-O), A.add, ["ofa"], ["off"], c=S // 2)
 
@@ -696,29 +763,30 @@ def rank_program(g, core, T, topo):
             fold(t + 1)
             shift[0] = 0
 
+    stage[0] = 1
     later = [q for q in range(N) if q > r]
     if later:
         masks, ne = share(off_e, len(later))
-        trs = [transfer(topo, T.cores[d], masks[i], T.sem.tt4, T.pp[:, S:S + 1], T.tot4[:, 4 * r:4 * r + 1]) for i, d in enumerate(later)]
-        remote(trs, "lt4", ne * len(later), ["pp1"], P["tot"])
-    mm(T.c1[:, 0:1], T.el[:], T.pp[:, S:S + 1], True, r == 0, ["el", "pp1"], ["c1"], 256)
-    ops[-1]["lat"] = P["tot"] if r > 0 else 0.0
+        trs = [transfer(topo, T.cores[d], masks[i], T.sem.tt4, T.base[:, 4:6], T.tot4[:, 2 * r:2 * r + 2]) for i, d in enumerate(later)]
+        remote(trs, "lt4", ne * len(later), ["sum0", "sum1"], P["tot"])
+    mm(T.c1[:, 0:2], T.el[:], T.base[:, 4:6], True, True, ["el", "sum0", "sum1"], ["c1", "own"], 256)
     if r > 0:
-        arrive("tt4", sum(share(off_e, N - 1 - q)[1] for q in range(r)), ["tot4"], [len(ops) - 1])
+        i = op({"x": (None, 0.0)}, [], [], None, None, P["tot"], [len(ops) - 1])
+        arrive("tt4", sum(share(off_e, N - 1 - q)[1] for q in range(r)), ["tot4"], [i])
     for h in range(2):
-        marks(h, ["ln1"])
+        marks(h, ["own"])
     cp(T.tt[:, 0:S], T.nf[:].indirect(T.ju3[:]), ["nf", "ju3"], ["tt.a"], S * G, True)
     dma("y", T.yj[:], T.tt[0:128:16, 0:S], ["tt.a"], [])
-    for q in range(r):
-        mm(T.c1[:, 0:1], T.ee[:], T.tot4[:, 4 * q:4 * q + 1], False, q == r - 1, ["ee", "tot4"], ["c1"], 256)
-    cp(T.base[:, 0:1], T.c1[:, 0:1], ["c1"], ["base"])
+    if r > 0:
+        mm(T.c1[:, 2:2 * r + 2], T.ee[:], T.tot4[:, 0:2 * r], True, True, ["ee", "tot4"], ["c1"], 256)
+    op({"v": (lambda: v.tensor_reduce(T.base[:, 0:1], T.c1[:, 0:2 * r + 2], AxisListType.X, A.add), us(64))}, ["c1"], ["base"])
     for h in range(2):
         hf = slice(h * S // 2, (h + 1) * S // 2)
         rd, wr = ["pp0", "pp1", "pp.z", "base"], ["dd0.%d" % h]
         out = T.dd[:, h * UNIT:h * UNIT + S // 2]
         if h == 0:
-            ts(out, T.pp[:, hf], T.base[:, 0:1], A.add, rd, wr, c=S // 2)
+            ts(out, T.pp[:, hf], -1.0, A.mult, rd, wr, T.base[:, 0:1], A.add, S // 2)
         else:
-            act(out, T.pp[:, hf], Act.Identity, rd, wr, S // 2, bias=T.base[:, 0:1])
+            act(out, T.pp[:, hf], Act.Identity, rd, wr, S // 2, bias=T.base[:, 0:1], scale=-1.0)
         dma("y" if h == 0 else "s", T.ya[:, hf], out, wr, [])
     emit(g, T, ops)

from concourse.bass import DstId, RemoteDMATransfer
from concourse.mybir import AluOpType, ActivationFunctionType, AxisListType

N, S, RO, GROW = 5, 768, 3, 18
W = N * S
SPAN = S * (255 + 16 * GROW)
CA, CB = 512, 256
CR = 384
O = 7
UNIT = 1024
GONE = 4096.0
F32, BF, I32, U16, F16 = "float32", "bfloat16", "int32", "uint16", "float16"

MODES = (("aggcdadg", "gcda"), ("agaadgcd", "dcad"), ("gdagcdcd", "dcca"))
PU = (1024, 512)
PLAN = {"g": 1.5, "cyc": 0.87e-3, "fix": 0.055, "sem": 0.06, "pe": 0.5e-3, "pelat": 0.1, "call": 0.7, "gdma": 1.0,
        "load": 3.0, "z0": 5.5, "z": 1.4, "direct": 6.5, "hop": 3.5, "relay": 11.0, "tot": 4.5, "tile": 3.5,
        "nm": 4.5, "nrel": 6.0, "add": 3.5, "dq": 1.2, "spares": (0.7, 1.0, 1.4), "passes": 4, "tries": 1200, "after": -150}
CASES = ((1.0, 1.0, 0.9, 1.0, 1.0), (1.3, 1.6, 1.0, 1.0, 1.4), (1.15, 0.9, 1.0, 1.2, 1.1), (1.1, 1.15, 1.7, 1.0, 1.3))

SCRATCH = {
    "szi": ("sbuf", [128, S], I32), "rfi": ("sbuf", [128, S + 16], I32),
    "cdi": ("sbuf", [128, 48], I32), "rci": ("sbuf", [128, 16], I32),
    "szb": ("sbuf", [128, S], BF), "szl": ("sbuf", [128, W], BF),
    "w1": ("sbuf", [128, W + 8], F32), "w2": ("sbuf", [128, W + 8], F32), "w3": ("sbuf", [128, W + 8], F32),
    "nm2": ("dram", [4 * N, 128, S // 32], BF), "nm3": ("dram", [N, 128, S // 8], BF),
    "dd": ("sbuf", [128, 16 * S], F32), "xx": ("sbuf", [128, 4 * UNIT], BF), "gg": ("sbuf", [128, 16 * S], BF),
    "off": ("sbuf", [128, S], U16), "ofa": ("sbuf", [128, S], U16),
    "rr": ("sbuf", [128, S], F32), "rw": ("sbuf", [128, S + 16], F32), "tt": ("sbuf", [128, 2 * S], F32),
    "pp": ("sbuf", [128, S + 16], F32), "ln": ("sbuf", [128, S], F32),
    "ma": ("sbuf", [128, UNIT], F32), "mb": ("sbuf", [128, UNIT], F32),
    "hi": ("sbuf", [128, S], BF), "lo": ("sbuf", [128, S], F16),
    "ne": ("sbuf", [128, S], BF), "up": ("sbuf", [128, S], BF),
    "f1": ("sbuf", [128, S], BF), "f2": ("sbuf", [128, S], BF), "f3": ("sbuf", [128, S], BF),
    "idc": ("sbuf", [128, 512], BF), "rcn": ("sbuf", [128, 16], F32),
    "dv1": ("sbuf", [128, S], BF), "dv2": ("sbuf", [128, S], BF), "dv3": ("sbuf", [128, S], BF),
    "tl0": ("sbuf", [128, 4 * CA], BF), "tl1": ("sbuf", [128, 4 * CB], BF), "neg": ("sbuf", [128, CA], BF),
    "src": ("sbuf", [128, 2048], BF), "wk": ("sbuf", [128, 2048], BF),
    "ud": ("sbuf", [128, 32], F32), "wd": ("sbuf", [128, 32], I32), "dg": ("sbuf", [128, 96], I32), "sl": ("sbuf", [128, 8], U16),
    "nf": ("sbuf", [128, S], F32), "hp": ("sbuf", [128, 128], BF), "yn": ("sbuf", [128, S], BF),
    "yj3": ("sbuf", [128, S], BF), "dg2": ("sbuf", [128, 256], BF),
    "pci": ("sbuf", [128, 16], I32), "pcf": ("sbuf", [128, 32], F32),
    "cc": ("sbuf", [128, 144], F32), "cm": ("sbuf", [128, 128], F32), "cg": ("sbuf", [128, 128], F32),
    "zb": ("sbuf", [128, 144], BF), "zf": ("sbuf", [128, 144], BF), "zw": ("sbuf", [128, 144], BF), "b18": ("sbuf", [128, 128], BF),
    "idn": ("sbuf", [128, 128], BF), "id2": ("sbuf", [128, 128], BF), "idm": ("sbuf", [128, 128], BF),
    "idh": ("sbuf", [128, 128], F16), "idf": ("sbuf", [128, 128], F32), "sw": ("sbuf", [128, 128], F32),
    "ee": ("sbuf", [128, 128], F32), "el": ("sbuf", [128, 128], F32),
    "l0": ("sbuf", [128, 48], F32), "l0u": ("sbuf", [128, 48], U16), "nl": ("sbuf", [128, 48], F32),
    "cdu": ("sbuf", [128, 48], U16), "cdf": ("sbuf", [128, 48], F32), "lt": ("sbuf", [128, 48], F32),
    "ju1": ("sbuf", [128, 48], U16), "ju2": ("sbuf", [128, 48], U16), "ju3": ("sbuf", [128, 48], U16),
    "cl2": ("sbuf", [128, 48], U16), "cl3": ("sbuf", [128, 48], U16),
    "base": ("sbuf", [128, 8], F32), "tot1": ("sbuf", [128, 32], F32), "tot4": ("sbuf", [128, 16], F32),
    "tp": ("psum", [128, 2048], F32),
    "c0": ("psum", [128, 512], F32), "c1": ("psum", [128, 512], F32),
    "r0": ("psum", [128, 512], F32), "r1": ("psum", [128, 512], F32),
}
NDMA = 48
SEMAPHORES = (["ev", "es", "et", "eg"] + ["d%d" % i for i in range(NDMA)] + ["e%d" % i for i in range(36)]
              + ["z1", "z2", "z3", "z4", "tt1", "a2", "a3", "p2", "p3", "tt4", "ha2", "ha3", "hp2"]
              + ["lz", "lt1", "la2", "la3", "lb2", "lb3", "lc2", "lc3", "lp2", "lp3", "lt4"])
PSUM = ("c0", "c1", "r0", "r1", "t0", "t1")


def bits(engines):
    m = 0
    for e in engines:
        m |= 1 << e
    return m


def share(engines, parts):
    n = len(engines) // parts
    p = 1
    while 2 * p <= n:
        p *= 2
    return [bits(engines[i * n:i * n + p]) for i in range(parts)], p


def helpers_of(core, topo):
    return [c for c in topo.cores_of(core) if topo.die(c) != topo.die(core)]


def transfer(topo, dst, mask, sem, ap_src, ap_dst):
    rid, pid, _ = topo.addr(dst)
    return RemoteDMATransfer(dst_ids=[DstId(rid=rid, pnc=pid)], dma_engine_mask=mask, remote_sem=sem, src=ap_src, dst=ap_dst)


def relay_program(g, core, T, topo, r, j, nh):
    far = [(r + d) % N for d in range(1, N)]
    cw = CR // nh
    on, off = topo.engines(T.cores[r], core), topo.engines(T.cores[r], T.cores[far[0]])
    got = {"p": share([e for e in on if e not in off], nh)[1], "a": share(on, nh)[1]}
    masks, ne = share(topo.engines(core, T.cores[far[0]]), len(far))
    piece = lambda t: T["w%d" % t][:, r * S + O + 1 + j * cw:r * S + O + 1 + (j + 1) * cw]
    jobs = [("p2", T.nm2[nh * r + j])] + [("a%d" % t, piece(t)) for t in range(2, RO + 1)]
    for name, ap in jobs:
        g.wait_ge(T.sem["h" + name], got[name[0]])
        g.remote_dma_fused([transfer(topo, T.cores[d], masks[i], T.sem[name], ap, ap) for i, d in enumerate(far)],
                           local_sem=T.sem["l" + name])
    for name, _ in jobs:
        g.wait_ge(T.sem["l" + name], ne * len(far))


def link(ops):
    last_w, readers, last_g = {}, {}, None
    for i, o in enumerate(ops):
        deps = set()
        wr = list(o["w"]) + [k for k in o["r"] if k in PSUM]
        for k in list(o["r"]) + wr:
            if k in last_w:
                deps.add(last_w[k])
        for k in wr:
            deps.update(readers.get(k, []))
        deps.discard(i)
        for k in o["r"]:
            readers.setdefault(k, []).append(i)
        for k in wr:
            last_w[k] = i
            readers[k] = []
        o["deps"] = deps
        o["order"] = set(o["after"])
    last_g = None
    for i in (i for i, o in enumerate(ops) if "g" in o["alt"] and (not o["w"] or not o["r"])):
        if last_g is not None:
            ops[i]["order"].add(last_g)
        last_g = i


KEPT = {}


def arrange(ops):
    P = PLAN
    n = len(ops)
    before, after, lean = [[] for _ in ops], [[] for _ in ops], [0.0] * n
    for i, o in enumerate(ops):
        for d in o["deps"] | o["order"]:
            lag = 0.0
            if "x" in o["alt"] or (d in o["deps"] and not ("t" in o["alt"] and "t" in ops[d]["alt"])):
                lag = ops[d]["lat"] + P["sem"] + (P["pelat"] if "t" in ops[d]["alt"] else 0.0)
            before[i].append((d, lag))
            after[d].append((i, lag))

    def place(prev, nxt, key, head):
        left = [len(x) for x in prev]
        pool = [i for i in range(n) if left[i] == 0]
        busy = {e: [] for e in "vstgyq"}
        start, end, eng, seq = [0.0] * n, [0.0] * n, [None] * n, []
        while pool:
            i = min(pool, key=lambda i: key[i])
            pool.remove(i)
            ready = max([end[d] + lag for d, lag in prev[i]] + [head[i]])
            best = None
            for e, (_, cost) in ops[i]["alt"].items():
                t, p = ready, 0
                if e != "x":
                    row = busy[e]
                    p = len(row)
                    while p > 0 and row[p - 1][1] > ready:
                        p -= 1
                    while p < len(row) and row[p][0] < t + cost:
                        t = max(t, row[p][1])
                        p += 1
                bias = lean[i] if e == "v" else 0.0
                if best is None or t + cost + bias < best[0]:
                    best = (t + cost + bias, t, cost, e, p)
            _, start[i], cost, eng[i], p = best
            end[i] = start[i] + cost
            if eng[i] != "x":
                busy[eng[i]].insert(p, (start[i], end[i]))
            seq.append(i)
            for u, _ in nxt[i]:
                left[u] -= 1
                if left[u] == 0:
                    pool.append(u)
        return start, end, eng, seq

    tail = [o["lat"] for o in ops]

    def worth(start, eng, seq):
        pos = {i: p for p, i in enumerate(seq)}
        order = sorted(range(n), key=lambda i: (start[i], pos[i]))
        total = 0.0
        for calc, pick, tens, wait, scale in CASES:
            end, free = [0.0] * n, {}
            for i in order:
                e, t = eng[i], 0.0
                for d, lag in before[i]:
                    if end[d] + lag * wait > t:
                        t = end[d] + lag * wait
                if e != "x":
                    t = max(t, free.get(e, 0.0)) + ops[i]["alt"][e][1] * (tens if e == "t" else wait if e == "q" else pick if ops[i]["pick"] else calc)
                    free[e] = t
                end[i] = t
            total += max(end[i] + tail[i] * wait for i in range(n)) / scale
        return total

    names, seen = [], {}
    for o in ops:
        k = ("".join(o["alt"]), len(o["r"]), len(o["w"]), o["line"])
        seen[k] = seen.get(k, 0) + 1
        names.append(k + (seen[k],))
    if KEPT:
        key = [KEPT[k][0] if k in KEPT else 1e6 + i for i, k in enumerate(names)]
        for i, k in enumerate(names):
            lean[i] = KEPT[k][1] if k in KEPT else 0.0
        start, _, eng, seq = place(before, after, key, [0.0] * n)
    else:
        best = None
        for spare in P["spares"]:
            lean[:] = [spare] * n
            key = [float(o["rank"]) for o in ops]
            for _ in range(P["passes"]):
                start, end, eng, seq = place(before, after, key, [0.0] * n)
                got = worth(start, eng, seq)
                if best is None or got < best[0]:
                    best = (got, start, eng, seq)
                back = place(after, before, [-(end[i] + tail[i]) for i in range(n)], tail)
                key = [-back[1][i] for i in range(n)]
        now, start, eng, seq = best
        lean[:] = [-50.0 if e == "v" else 50.0 for e in eng]
        state, span = [7], max(start)

        def draw():
            state[0] = (state[0] * 1103515245 + 12345) % 2 ** 31
            return state[0] / 2 ** 31

        for _ in range(P["tries"]):
            c, w, a = draw() * span, 1.0 + 5.0 * draw(), 0.5 + 3.0 * draw()
            key, old = list(start), list(lean)
            for i in range(n):
                if c <= start[i] < c + w:
                    key[i] += a * (draw() - 0.5)
                    if len(ops[i]["alt"]) > 1 and draw() < 0.15:
                        lean[i] = -lean[i]
            other = place(before, after, key, [0.0] * n)
            got = worth(other[0], other[2], other[3])
            if got <= now:
                now, start, eng, seq = got, other[0], other[2], other[3]
            else:
                lean[:] = old
        for i, k in enumerate(names):
            KEPT[k] = (start[i], -50.0 if eng[i] == "v" else 50.0)
    for i, o in enumerate(ops):
        o["e"] = eng[i]
        o["fn"] = o["alt"][eng[i]][0]
    pos = {i: p for p, i in enumerate(seq)}
    return sorted(range(n), key=lambda i: (start[i], pos[i]))


def emit(g, T, ops):
    queue = {"v": g.vector, "s": g.scalar, "t": g.tensor, "g": g, "y": g.sync}
    esem = {"v": "ev", "s": "es", "t": "et", "g": "eg"}
    link(ops)
    order = arrange(ops)
    pos = {i: p for p, i in enumerate(order)}
    seen_p, needed = {}, set()
    for i in order:
        o = ops[i]
        keep, latest = [], {}
        for d in sorted(o["deps"], key=lambda d: pos[d]):
            if ops[d]["tok"] is not None:
                keep.append(d)
            elif not (o["e"] == "t" and ops[d]["e"] == "t"):
                latest[ops[d]["e"]] = d
        for e, d in sorted(latest.items()):
            if seen_p.get((o["e"], e), -1) < pos[d]:
                seen_p[(o["e"], e)] = pos[d]
                needed.add(d)
                keep.append(d)
        o["waits"] = keep
    count = {e: 0 for e in esem}
    for i in order:
        o = ops[i]
        if i in needed:
            count[o["e"]] += 1
            o["tok"] = (esem[o["e"]], count[o["e"]])
            o["inc"] = 1
    seen, top, last = {}, {}, {}
    for i in order:
        o = ops[i]
        if o["tok"] is not None:
            last[o["tok"][0]] = max(last.get(o["tok"][0], 0), o["tok"][1])
        if o["fn"] is None:
            continue
        for d in o["waits"]:
            name, val = ops[d]["tok"]
            if seen.get((o["e"], name), 0) < val:
                seen[(o["e"], name)] = val
                top[name] = max(top.get(name, 0), val)
                queue[o["e"]].wait_ge(T.sem[name], val)
        ins = o["fn"]()
        if o["inc"]:
            ins.then_inc(T.sem[o["tok"][0]], o["inc"])
    for name, val in last.items():
        if top.get(name, 0) < val:
            g.sync.wait_ge(T.sem[name], val)


def rank_program(g, core, T, topo):
    r = T.rank_of(core)
    if r is None:
        for q in range(N):
            hs = helpers_of(T.cores[q], topo)
            if core in hs:
                relay_program(g, core, T, topo, q, hs.index(core), len(hs))
        return
    A, Act = AluOpType, ActivationFunctionType
    v, sc, pe = g.vector, g.scalar, g.tensor
    P = PLAN
    G = P["g"]
    ops = []
    ndma, nadd, shift, units, picked, stage = [0], [0], [0], [0, 0], [False], [0]
    plain = sorted({m[h].count("c") * UNIT // (CA, CB)[h] for m in MODES for h in range(2)} - {0})

    def op(alt, rd, wr, tok=None, inc=None, lat=0.0, after=()):
        ops.append({"alt": alt, "r": list(rd), "w": list(wr), "tok": tok, "inc": inc, "lat": lat, "after": list(after),
                    "rank": len(ops) + shift[0], "pick": picked[0], "line": stage[0]})
        picked[0] = False
        return len(ops) - 1

    def us(c):
        picked[0] = isinstance(c, float)
        return P["fix"] + max(64, c) * P["cyc"]

    def dma(e, out, in_, rd, wr, lat=3.0):
        q = {"s": sc, "y": g.sync}[e]
        op({e: (lambda: q.dma_start(out, in_), 0.1)}, rd, wr, ("d%d" % ndma[0], 16), 16, lat)
        ndma[0] += 1

    def f_ts(out, in0, s1, op0, s2=None, op1=None):
        if op1 is None:
            return lambda: v.tensor_scalar(out, in0, s1, None, op0)
        return lambda: v.tensor_scalar(out, in0, s1, s2, op0, op1)

    def f_act(out, in_, f, **kw):
        return lambda: sc.activation(out, in_, f, **kw)

    def ts(out, in0, s1, op0, rd, wr, s2=None, op1=None, c=64):
        op({"v": (f_ts(out, in0, s1, op0, s2, op1), us(c))}, rd, wr)

    def tt(out, in0, in1, o, rd, wr, c=96):
        op({"v": (lambda: v.tensor_tensor(out, in0, in1, o), us(c))}, rd, wr)

    def cp(out, in_, rd, wr, c=64, both=False):
        alt = {"v": (lambda: v.tensor_copy(out, in_), us(c))}
        if both:
            alt["s"] = (f_act(out, in_, Act.Copy), us(c))
        op(alt, rd, wr)

    def act(out, in_, f, rd, wr, c=64, **kw):
        op({"s": (f_act(out, in_, f, **kw), us(c))}, rd, wr)

    def either(fv, fs, rd, wr, cv, cs):
        op({"v": (fv, us(cv)), "s": (fs, us(cs))}, rd, wr)

    def scaled(out, in_, s, rd, wr, c=128):
        either(f_ts(out, in_, s, A.mult), f_act(out, in_, Act.Copy, scale=s), rd, wr, c, c)

    def lin(out, in_, a, b, rd, wr):
        either(f_ts(out, in_, a, A.mult, b, A.add), f_act(out, in_, Act.Identity, scale=a, bias=b), rd, wr, 64, 64)

    def mm(out, lhs, rhs, start, stop, rd, wr, c=64):
        op({"t": (lambda: pe.matmul(out, lhs, rhs, start, stop), c * P["pe"])}, rd, wr)

    def iota(out, pattern, base, cmul, wr, c, flag=True):
        if flag:
            fn = lambda: g.iota(out, pattern, base, cmul, allow_small_or_imprecise_dtypes=True)
        else:
            fn = lambda: g.iota(out, pattern, base, cmul)
        op({"g": (fn, 0.16 + 2 * c * P["cyc"])}, [], wr)

    def gcopy(out, in_, rd, wr, c):
        op({"g": (lambda: g.affine_select(out, in_, [[0, c]], A.is_gt, 0.0, 1, 0), 0.2 + 2 * c * P["cyc"])}, rd, wr)

    def keep(out, in_, pattern, base, cmul, rd, wr):
        op({"g": (lambda: g.affine_select(out, in_, pattern, A.is_gt, 0.0, base, cmul), 0.2 + 256 * P["cyc"])}, rd, wr)

    def ms(ap, val, wr, c=64):
        op({"v": (lambda: v.memset(ap, val), us(c))}, [], wr)

    def fill(ap, val, wr, c):
        either(lambda: v.memset(ap, val), f_act(ap, T.yj3[:, 0:c], Act.Identity, scale=0.0, bias=val), ["yj3"], wr, c // 2, c)

    def scan(out, data, init, rd, wr, c):
        op({"v": (lambda: v.tensor_tensor_scan(out, data, data, init, A.min, A.subtract), us(c))}, rd, wr)

    def remote(trs, local, n, rd, lat):
        return op({"g": (lambda: g.remote_dma_fused(trs, local_sem=T.sem[local]), P["call"])}, rd, [], (local, n), None, lat)

    def arrive(sem, n, wr, after):
        op({"x": (None, 0.0)}, [], wr, (sem, n), None, 0.0, after)

    others = [(r + d) % N for d in range(1, N)]
    hs = helpers_of(core, topo)
    off_e = topo.engines(core, T.cores[others[0]])
    on_e = topo.engines(core, hs[0])
    own = slice(r * S, (r + 1) * S)
    part, wid = [slice(0, CA), slice(CA, S)], [CA, CB]
    cP, rP = [T.c0[:, 0:CA], T.c1[:, 0:CB]], [T.r0[:, 0:CA], T.r1[:, 0:CB]]
    cK, rK = ["c0", "c1"], ["r0", "r1"]
    tl = [T.tl0, T.tl1]
    col = lambda i: T.pcf[:, i:i + 1]
    at = lambda h, k: (k * CA if h == 0 else 16 * CA + k * CB)
    blk = lambda b, h, k, n=1: b[:, at(h, k):at(h, k) + n * wid[h]]
    offs = lambda a, n, b=T.off: b[:, a // 16:(a + n) // 16]
    sent = {}

    def to_helpers(w, a, n, sem, local, key, rest):
        cw = n // len(hs)
        masks, ne = share(on_e, len(hs))
        trs = [transfer(topo, c, masks[j], T.sem[sem], w[:, a + j * cw:a + (j + 1) * cw], w[:, a + j * cw:a + (j + 1) * cw])
               for j, c in enumerate(hs)]
        i = remote(trs, local, ne * len(hs), key, P["hop"])
        return op({"q": (None, 2.0)}, [], [], None, None, rest + P["hop"] - 2.0, [i])

    def send_part(t, h):
        w = T["w%d" % t]
        key = "w%d.own%d" % (t, h)
        a = r * S + O + 1 + h * CA
        masks, ne = share(off_e, N - 1)
        if h == 0:
            sent[t] = to_helpers(w, a, CR, "ha%d" % t, "lb%d" % t, [key], P["relay"] - P["hop"])
            if CR < CA:
                ap = w[:, a + CR:a + CA]
                remote([transfer(topo, T.cores[d], masks[i], T.sem["a%d" % t], ap, ap) for i, d in enumerate(others)],
                       "lc%d" % t, ne * (N - 1), [key], P["direct"])
        else:
            trs = [transfer(topo, T.cores[d], masks[i], T.sem["a%d" % t], w[:, a:a + CB], w[:, a:a + CB]) for i, d in enumerate(others)]
            i = remote(trs, "la%d" % t, ne * (N - 1), [key], P["direct"] - 2.0)
            i = op({"q": (None, 3.0)}, [], [], None, None, P["direct"] - 3.0, [i])
            arrive("a%d" % t, ne * (N - 1) * (1 + (CR < CA) + len(hs)), ["w%d.%d" % (t, q) for q in others], [sent[t], i])

    def send_names(t):
        w, cl, nm = T.szl, T["cl%d" % t], T["nm%d" % t]
        masks, ne = share(off_e, N - 1)
        if t == 2:
            nh = len(hs)
            dma("y", nm[nh * r:nh * r + nh], w[0:128:8, own], ["szl%d" % r], ["nm2.own"], P["nm"])
            inner, ni = share([e for e in on_e if e not in off_e], nh)
            i = remote([transfer(topo, c, inner[j], T.sem.hp2, nm[nh * r + j], nm[nh * r + j]) for j, c in enumerate(hs)],
                       "lp2", ni * nh, ["nm2.own"], P["hop"])
            i = op({"x": (None, 0.0)}, [], [], None, None, P["nrel"], [i])
            arrive("p2", ne * (N - 1) * nh, ["nm2.far"], [i])
        else:
            dma("y", nm[r], w[0:128:8, own], ["szl%d" % r], ["nm%d.own" % t], P["nm"])
            i = remote([transfer(topo, T.cores[d], masks[j], T.sem["p%d" % t], nm[r], nm[r]) for j, d in enumerate(others)],
                       "lp%d" % t, ne * (N - 1), ["nm%d.own" % t], P["tot"])
            arrive("p%d" % t, ne * (N - 1), ["nm%d.far" % t], [i])
        for q in range(16):
            n = 48 if q < 15 else 47
            mm(T.r1[:, 320:320 + n], T.zw[:, 15 - q:143 - q], w[:, r * S + q + 1:(r + 1) * S:16], q == 0, q == 15,
               ["zw", "szl%d" % r], ["r1"])
        ts(cl[:, 0:47], T.r1[:, 320:367], float(-r * S), A.add, ["r1"], ["cl%da" % t])
        ts(cl[:, 47:48], T.r1[:, 367:368], col(14), A.add, ["r1", "pc14"], ["cl%db" % t])

    def wkeys(t):
        return ["w%d.%d" % (t, q) for q in others] + ["w%d.own0" % t, "w%d.own1" % t]

    def starts(tot, rd, sign=1.0):
        mm(T.c1[:, CB:CB + N], T.el[:], tot(0, N), True, False, rd + ["el"], ["c1"], 256)
        for s in range(1, N):
            mm(T.c1[:, CB + s:CB + N], T.ee[:], tot(0, N - s), False, s == N - 1, rd + ["ee"], ["c1"], 256)
        ts(T.base[:, 0:N], T.c1[:, CB:CB + N], T.c1[:, CB + r:CB + r + 1], A.subtract, ["c1"], ["base"], sign, A.mult)

    def bases(t):
        w = T["w%d" % t]
        starts(lambda a, b: w[:, (a + 1) * S + O:b * S + O + 1:S], wkeys(t))
        for q in others:
            ap, k, b = w[:, q * S + O + 1:(q + 1) * S + O], "w%d.%d" % (t, q), T.base[:, q:q + 1]
            either(f_ts(ap, ap, b, A.add), f_act(ap, ap, Act.Identity, bias=b), [k, "base"], [k], S, S)
        cp(w[:, O:W:S], T.base[:, 0:N], ["base"], ["w%d.col0" % t, "w%d.own1" % t, "w%d.z" % t])

    def fold(t):
        ju, k, dv = T["ju%d" % t], "ju%d" % t, T["dv%d" % t]
        win, wk = (T.rfi[:], ["rfi", "rfi.z"]) if t == 1 else (T.rw[:], ["rw0", "rw1", "rw.z"])
        tt(T.ne[:], win.indirect(T.cdu[:]), T.rr[:], A.not_equal, ["rr0", "rr1", "cdu"] + wk, ["ne"], S * G)
        mm(T.r1[:, CB:CB + 48], T.idf[:], T.cdf[:], True, False, ["idf", "cdf"], ["r1"], 256)
        for q in range(16):
            mm(T.r1[:, CB:CB + 48], T.zf[:, 15 - q:143 - q], T.ne[:, q:S:16], False, q == 15, ["zf", "ne"], ["r1"])
        tt(T.lt[:], T.r1[:, CB:CB + 48], T.nl[:], A.min, ["r1", "nl"], ["lt"], 64)
        cp(ju[:], T.lt[:], ["lt"], [k])
        if t == 1:
            cp(T.szl[:, own], T.yn[:].indirect(ju[:]), ["yn", k], ["szl%d" % r], S * G, True)
            send_names(2)
        if t == 2:
            cp(T.yj3[:], T.yn[:].indirect(ju[:]), ["yn", k], ["yj3"], S * G, True)
            cp(T.szl[:, own], T.yj3[:].indirect(T.ju1[:]), ["yj3", "ju1"], ["szl%d" % r], S * G, True)
            send_names(3)
        for h in range(2):
            mm(rP[h], T.b18[:], T.ne[:, part[h]], True, True, ["b18", "ne"], [rK[h]], wid[h])
            o = dv[:, part[h]]
            either(f_ts(o, rP[h], 0.0, A.is_equal, GONE, A.mult), f_act(o, rP[h], Act.Relu, bias=GONE, scale=-GONE),
                   [rK[h]], ["dv%d%d" % (t, h)], wid[h], wid[h])

    def sides(t, h):
        if t == 1:
            mm(rP[h], T.idf[:], T.rr[:, part[h]], True, True, ["idf", "rr%d" % h], [rK[h]], 4 * wid[h])
        tt(T.up[:, part[h]], rP[h], T.nf[:, part[h]], A.is_ge, [rK[h], "nf"], ["up%d" % h], wid[h])
        for d in range(3):
            k = ["tl%d.%d" % (h, d)]
            dma("y", tl[h][32 * d:32 * d + 32, :], T.up[:, part[h]], ["up%d" % h], k, 0.0)
            op({"q": (None, 0.4)}, ["up%d" % h], k, ops[-1]["tok"], None, P["tile"] - 0.4)

    def rename(t):
        for q in others:
            nm = T.nm2[len(hs) * q:len(hs) * (q + 1)] if t == 2 else T.nm3[q]
            dma("y", T.szl[0:128:8, q * S:(q + 1) * S], nm, ["nm%d.far" % t], ["szl%d" % q], P["nm"])
        wk = ["szl%d" % q for q in range(N)]
        for h in range(2):
            pu = PU[h]
            for a in range(at(h, 0), at(h, 16), pu):
                cp(T.gg[:, a:a + pu], T.szl[:].indirect(offs(a, pu)), wk + ["off"], ["gg%d" % a], pu * G, True)
            shift[0] = P["after"]
            for k in range(16):
                mm(rP[h], T.zw[:, 15 - k:143 - k], blk(T.gg, h, k), k == 0, k == 15,
                   ["zw", "gg%d" % (at(h, 0) + k * wid[h] // pu * pu)], [rK[h]], wid[h])
            sides(t, h)
            cp(T.rr[:, part[h]], rP[h], [rK[h]], ["rr%d" % h], wid[h], True)
            gcopy(T.rw[:, part[h]], T.rr[:, part[h]], ["rr%d" % h], ["rw%d" % h], wid[h])
            shift[0] = 0
        if t == RO:
            dma("y", T.yr[:], T.rr[:], ["rr0", "rr1"], [])

    def far(t, h):
        w = T["w%d" % t]
        wk = wkeys(t) + ["w%d.col0" % t, "w%d.z" % t, "ofa"]
        mine, mk = (T.ma, "ma") if h == 0 else (T.mb, "mb")
        nk, modes, first = UNIT // wid[h], MODES[t - 1][h], [True]

        def count(lhs, rhs, rd, last=False):
            mm(cP[h], lhs, rhs, first[0], last, rd, [cK[h]], wid[h])
            first[0] = False

        if t > 1:
            count(T.id2[:], T["f%d" % (t - 1)][:, part[h]], ["id2", "f%d%d" % (t - 1, h)])
        nc = modes.count("c")
        todo = {False: list(range(len(modes) - nc)), True: list(range(len(modes) - nc, len(modes)))}
        for n, mode in enumerate(modes):
            if nc and n == len(modes) - 2:
                j = plain.index(nc * nk)
                count(T.idc[:, 128 * j:128 * j + 128], T.up[:, part[h]], ["idc%d" % j, "up%d" % h])
            u = todo[mode == "c"].pop(0)
            xa, k0 = units[1] % 4 * UNIT, u * nk
            units[1] += 1
            d, x, dk = blk(T.dd, h, k0, nk), T.xx[:, xa:xa + UNIT], "dd%d.%d" % (h, u)
            xk = ["xx%d" % (xa + j * UNIT // 4) for j in range(4)]
            piece = lambda ap, a, j: ap[:, a + j * wid[h]:a + (j + 1) * wid[h]]
            if mode != "c":
                b = units[0] % 2
                units[0] += 1
                for j in range(nk):
                    k, o, tk = k0 + j, piece(T.tp, b * UNIT, j), "t%d" % b
                    if mode == "g":
                        mm(o, T.idm[:], T.hi[:, part[h]], True, False, ["idm", "hi%d" % h], [tk], wid[h])
                        mm(o, T.idh[:], T.lo[:, part[h]], False, False, ["idh", "lo%d" % h], [tk], wid[h])
                    mm(o, T.wk[0:120, 128 * k:128 * k + 128], tl[h][0:120, k % 4 * wid[h]:(k % 4 + 1) * wid[h]], mode != "g", True,
                       ["wk%d" % (k // 8), "tl%d.n" % h] + ["tl%d.%d" % (h, d) for d in range(3)], [tk], wid[h])
            win = w[:, 0:W + O].indirect(offs(at(h, k0), UNIT, T.ofa))
            mks = ["%s%d" % (mk, j) for j in range(nk)]
            if mode in "gd":
                act(d, win, Act.Copy, wk, [dk], UNIT * G)
            else:
                tt(d, win, mine[:], A.add, wk + mks, [dk], UNIT * G)
            if mode == "d":
                tok = ("e%d" % nadd[0], 16)
                op({"g": (lambda d=d: g.dma_start(d, mine[:], accum_op=A.add), P["gdma"])}, [dk] + mks, [dk], tok, 16)
                op({"q": (None, P["dq"])}, [dk] + mks, [dk], tok, None, P["add"] - P["dq"])
                nadd[0] += 1
            if mode == "c":
                act(d, d, Act.Abs, [dk], [dk], UNIT)
            else:
                tt(x, d, T.tp[:, b * UNIT:(b + 1) * UNIT], A.is_le, [dk, tk], xk, UNIT)
            for j in range(nk):
                k, xj = k0 + j, xk[j * 4 // nk:(j + 1) * 4 // nk]
                if mode == "c":
                    o, a = piece(T.xx, xa, j), blk(T.dd, h, k)
                    either(f_ts(o, a, T.rcn[:, k:k + 1], A.add, 0.0, A.max), f_act(o, a, Act.Relu, bias=T.rcn[:, k:k + 1]),
                           [dk, "rcn"], xj, wid[h], wid[h])
                count(T.zb[:, 15 - k:143 - k], piece(T.xx, xa, j), ["zb"] + xj, n == len(modes) - 1 and j == nk - 1)

    def own_forms(t, h, copy):
        m, mk = (T.ma, "ma") if h == 0 else (T.mb, "mb")
        rd = ["pp0", "pp.z"] + ["pp1"] * h
        for j in range(UNIT // wid[h]):
            copy(m[:, j * wid[h]:(j + 1) * wid[h]], T.pp[:, part[h]], rd, ["%s%d" % (mk, j)], wid[h])
        if "g" not in MODES[t - 1][h]:
            return
        copy(T.hi[:, part[h]], T.pp[:, part[h]], rd, ["hi%d" % h], wid[h])
        if t > 1:
            tt(T.lo[:, part[h]], T.pp[:, part[h]], T.hi[:, part[h]], A.subtract, rd + ["hi%d" % h], ["lo%d" % h], 2 * wid[h])
            return
        mm(T.c0[:, 0:wid[h]], T.idf[:], T.pp[:, part[h]], True, False, rd + ["idf"], ["c0"], 4 * wid[h])
        mm(T.c0[:, 0:wid[h]], T.idm[:], T.hi[:, part[h]], False, True, ["idm", "hi%d" % h], ["c0"], wid[h])
        cp(T.lo[:, part[h]], T.c0[:, 0:wid[h]], ["c0"], ["lo%d" % h], wid[h])

    def lengths(t, h):
        f, fk = T["f%d" % t][:, part[h]], "f%d%d" % (t, h)
        tt(f, cP[h], T.up[:, part[h]], A.not_equal, [cK[h], "up%d" % h], [fk], wid[h])
        b = units[0] % 2
        q, qk = (cP[0], "c0") if h == 0 else (T.tp[:, b * UNIT:b * UNIT + CB], "t%d" % b)
        mm(q, T.idn[:], T.szb[:, part[h]], True, False, ["idn", "szb"], [qk], wid[h])
        mm(q, T.idm[:], T["dv%d" % t][:, part[h]], False, False, ["idm", "dv%d%d" % (t, h)], [qk], wid[h])
        mm(q, T.b18[:], f, False, True, ["b18", fk], [qk], wid[h])
        o = T.ln[:, part[h]]
        if h == 0:
            either(f_ts(o, q, 0.0, A.max), f_act(o, q, Act.Relu), [qk], ["ln0"], CA, CA)
            scan(T.pp[:, 1:CA + 1], o, 0.0, ["ln0"], ["pp0"], CA)
        else:
            if t < RO:
                ts(o, q, 0.0, A.max, [qk], ["ln1"], c=CB)
            else:
                scaled(T.base[:, 4:5], T.pp[:, CA:CA + 1], -1.0, ["pp0"], ["sum0", "base"], 64)
                act(o, q, Act.Relu, [qk], ["ln1", "sum1"], CB, accum_out=T.base[:, 5:6])
            scan(T.pp[:, CA + 1:S + 1], o, T.pp[:, CA:CA + 1], ["ln1", "pp0"], ["pp1"], CB)
        if t < RO:
            w, lst, a = T["w%d" % (t + 1)], T["cl%d" % (t + 1)], r * S + O + 1
            la, lb = "cl%da" % (t + 1), "cl%db" % (t + 1)
            if h == 0:
                scaled(w[:, a:a + CA], T.pp[:, 0:CA + 1].indirect(lst[:, 0:CA // 16]), -1.0, ["pp0", "pp.z", la], ["w%d.own0" % (t + 1)], CA * G)
            else:
                ts(w[:, a + CA:a + S], T.pp[:, 0:S + 1].indirect(lst[:, CA // 16:48]), -1.0, A.mult, ["pp0", "pp1", "pp.z", la, lb],
                   ["w%d.own1" % (t + 1)], c=CB * G)
            send_part(t + 1, h)
            own_forms(t + 1, h, gcopy)

    def marks(h, rd):
        for u in range(1, RO + 1):
            mm(rP[h], T.id2[:], T["f%d" % u][:, part[h]], u == 1, False, ["id2", "f%d%d" % (u, h)] + rd, [rK[h]], wid[h])
        for u in range(1, RO):
            mm(rP[h], T.idm[:], T["dv%d" % u][:, part[h]], False, u == RO - 1, ["idm", "dv%d%d" % (u, h)], [rK[h]], wid[h])
        o = T.tt[:, S + h * CA:S + h * CA + wid[h]]
        ts(o, rP[h], GONE, A.is_ge, [rK[h]], ["tt.b%d" % h], c=wid[h])
        dma("y", T.yf[:, part[h]], o, ["tt.b%d" % h], [])

    dma("y", T.szi[:], T.sz[:], [], ["szi"], P["load"])
    dma("y", T.rfi[:, 0:S], T.rf[:], [], ["rfi"], P["load"] + 1.1)
    dma("s", T.cdi[:], T.cd[:], [], ["cdi"], P["load"] - 0.7)
    dma("s", T.rci[:], T.rch[:], [], ["rci"], P["load"])
    iota(T.pci[:, 0:1], [[0, 1]], 0, 1, ["pci0"], 1, False)
    iota(T.cc[:], [[1, 144]], 0, 0, ["cc"], 144)
    iota(T.nl[:], [[16, 48]], 0, 0, ["nl"], 48)
    iota(T.cg[:], [[16, 8], [0, 16]], 0, 0, ["cg"], 128)
    iota(T.cm[:], [[0, 8], [1, 16]], 0, 0, ["cm"], 128)
    iota(T.rfi[:, S:S + 16], [[0, 16]], -1, 0, ["rfi.z"], 16, False)
    iota(T.yj3[:], [[1, S // 64], [0, 64]], r * S // 64, 0, ["yj3"], S)
    cp(T.szb[:], T.szi[:], ["szi"], ["szb"], S)
    scan(T.pp[:, 1:S + 1], T.szb[:], 0.0, ["szb"], ["pp0", "pp1"], S)
    for d, q in enumerate(others):
        trz = [transfer(topo, T.cores[q], bits(off_e), T.sem["z%d" % (d + 1)], T.szb[:], T.szl[:, own])]
        i = remote(trz, "lz", len(off_e) * (N - 1), ["szb"], P["z0"] + d * (P["z"] - P["call"]))
        arrive("z%d" % (d + 1), len(off_e), ["szl%d" % ((r - d - 1) % N)], [i])
        if d == 0:
            masks, ne = share(off_e, N - 1)
            trs = [transfer(topo, T.cores[e], masks[j], T.sem.tt1, T.pp[:, S:S + 1], T.tot1[:, 4 * r:4 * r + 1]) for j, e in enumerate(others)]
            i = remote(trs, "lt1", ne * (N - 1), ["pp1"], P["z0"])
            arrive("tt1", ne * (N - 1), ["tot1"], [i])
    iota(T.pp[:, 0:1], [[0, 1]], 0, 0, ["pp.z"], 1)
    iota(T.hp[:], [[0, 2], [1, 64]], 0, 0, ["hp"], 128)
    iota(T.l0[:, 0:32], [[1, 16], [256, 2]], 0, 0, ["l0a"], 32)
    iota(T.l0[:, 32:48], [[1, 16]], CA, 0, ["l0b"], 16)
    iota(T.nf[:], [[1, S]], r * S, 0, ["nf"], S)
    iota(T.rw[:, S:S + 16], [[0, 16]], -1, 0, ["rw.z"], 16)
    for t in range(1, RO + 1):
        iota(T["w%d" % t][:, 0:O + 1], [[0, O + 1]], 0, 0, ["w%d.z" % t], 8)
    for i, m in enumerate((15, 112, 16, 14, 1, 8, 7, 124)):
        ts(T.pci[:, i + 1:i + 2], T.pci[:, 0:1], m, A.bitwise_and, ["pci0"], ["pci%d" % (i + 1)])
    cp(T.pcf[:, 0:9], T.pci[:, 0:9], ["pci%d" % i for i in range(9)], ["pcf"])
    ms(T.neg[:], -1.0, ["neg"], CA // 2)
    for j in range(4):
        fill(T.src[:, j * CA:(j + 1) * CA], 0.0, ["src"], CA)
    fill(T.f3[:], 1.0, ["f30", "f31"], S)
    dma("y", T.tl0[96:120, :], T.neg[0:96, 0:CA], ["neg"], ["tl0.n"], P["tile"])
    op({"g": (lambda: g.dma_start(T.tl1[96:120, :], T.neg[0:96, 0:CB]), P["gdma"])}, ["neg", "nf"], ["tl1.n"], ("e35", 16), 16, P["tile"])
    ts(col(9), col(5), 16.0, A.mult, ["pcf"], ["pc9"], col(3), A.not_equal)
    lin(col(10), col(4), 16.0, col(3), ["pcf"], ["pc10"])
    lin(col(11), col(3), -2.0, col(0), ["pcf"], ["pc11"])
    ts(col(12), col(7), 0.0, A.is_equal, ["pcf"], ["pc12"])
    ts(T.zb[:], T.cc[:], -15.0, A.add, ["cc", "pcf"], ["zb"], col(2), A.is_equal, 144)
    ts(T.sw[:], T.cc[:, 0:128], -16.0, A.add, ["cc", "pc11"], ["sw"], col(11), A.is_equal, 128)
    ts(T.idf[:], T.cc[:, 0:128], col(0), A.is_equal, ["cc", "pcf"], ["idf"], c=128)
    lin(col(13), col(9), float(S), col(10), ["pc9", "pc10"], ["pc13"])
    scaled(T.zw[:], T.zb[:], col(12), ["zb", "pc12"], ["zw"], 144)
    scaled(T.zf[:], T.zb[:], 1024.0, ["zb"], ["zf"], 144)
    scaled(T.zb[:], T.zb[:], 1 / 16, ["zb"], ["zb"], 144)
    scaled(T.idn[:], T.idf[:], 1.0, ["idf"], ["idn"])
    lin(T.nl[:], T.nl[:], 1.0, col(1), ["nl", "pcf"], ["nl"])
    cp(T.cdf[:], T.cdi[:], ["cdi", "szb"], ["cdf"])
    tt(T.lt[:], T.nl[:], T.cdi[:], A.is_equal, ["nl", "cdi", "szb"], ["lt"])
    lin(T.lt[:], T.lt[:], 1024.0, 0.0, ["lt"], ["lt"])
    tt(T.lt[:], T.lt[:], T.cdf[:], A.add, ["lt", "cdf"], ["lt"])
    ts(T.cdu[:], T.lt[:], float(S), A.min, ["lt"], ["cdu"])
    cp(T.rr[:], T.rfi[:, 0:S], ["rfi"], ["rr0", "rr1"], S)
    lin(col(15), col(6), 0.125, 0.0, ["pcf"], ["pc15"])
    lin(col(17), col(6), -8.0, 64.0, ["pcf"], ["pc17"])
    scaled(T.dg2[:, 0:128], T.idf[:], col(15), ["idf", "pc15"], ["dg2a"])
    scaled(T.dg2[:, 128:256], T.idf[:], col(17), ["idf", "pc17"], ["dg2b"])
    for h in range(2):
        mm(cP[h], T.dg2[:, 128:256], T.yj3[:, part[h]], True, False, ["dg2b", "yj3"], [cK[h]], wid[h])
        for a in range(0, wid[h], 128):
            mm((T.c0, T.c1)[h][:, a:a + 128], T.dg2[:, 0:128], T.hp[:], False, a + 128 == wid[h], ["dg2a", "hp"], [cK[h]], 128)
        cp(T.yn[:, part[h]], cP[h], [cK[h]], ["yn"], wid[h], True)
    ts(col(14), col(1), 15.0, A.is_equal, ["pcf"], ["pc14"], float(S + r * S), A.mult)
    lin(col(14), col(14), 1.0, float(-r * S), ["pc14"], ["pc14"])
    ts(T.b18[:], T.cg[:], col(2), A.is_equal, ["cg", "pcf"], ["b18"], float(GROW), A.mult, 128)
    op({"v": (lambda: v.transpose(T.tt[:, 0:S], T.rr[:]), us(S))}, ["rr0", "rr1"], ["tt.a"])
    for h in range(2):
        mm(rP[h], T.sw[:], T.tt[:, part[h]], True, True, ["sw", "tt.a"], [rK[h]], 4 * wid[h])
        cp(T.tt[:, S + h * CA:S + h * CA + wid[h]], rP[h], [rK[h]], ["tt.b%d" % h], wid[h], True)
    scaled(T.idm[:], T.idf[:], -1.0, ["idf"], ["idm"])
    scaled(T.w1[:, r * S + O + 1:(r + 1) * S + O + 1], T.pp[:, 1:S + 1], -1.0, ["pp0", "pp1"], ["w1.own0", "w1.own1", "w1.z"], S)
    own_forms(1, 0, lambda out, in_, rd, wr, c: cp(out, in_, rd, wr, c, True))
    fold(1)
    ts(T.l0u[:], T.l0[:], col(13), A.add, ["l0a", "l0b", "pc13"], ["l0u"])
    ts(T.ofa[:], T.tt[:].indirect(T.l0u[:]), float(O), A.add, ["tt.a", "tt.b0", "tt.b1", "l0u"], ["ofa"], c=S * G)
    lin(col(18), col(2), -SPAN / 16, float((8 * N - 8 * r) * SPAN), ["pcf"], ["pc18"])
    lin(col(19), col(2), SPAN / 16, float((8 * r + 1) * SPAN + 1), ["pcf"], ["pc19"])
    ts(T.ud[:, 0:16], T.rci[:], col(18), A.min, ["rci", "pc18", "szb"], ["ud0"])
    ts(T.ud[:, 16:32], T.rci[:], 1.0, A.add, ["rci", "pc19", "szb"], ["ud1"], col(19), A.min)
    tt(T.wd[:, 0:16], T.ud[:, 0:16], T.ud[:, 16:32], A.add, ["ud0", "ud1"], ["wd0"])
    cp(T.wd[:, 16:32], T.ud[:, 16:32], ["ud1"], ["wd1"])
    for d in range(3):
        ts(T.dg[:, 32 * d:32 * d + 32], T.wd[:], 255 << (8 * d), A.bitwise_and, ["wd0", "wd1"], ["dg%d" % d])
    lin(col(20), col(1), 128.0, 0.0, ["pcf"], ["pc20"])
    lin(col(21), col(8), 0.25, col(20), ["pcf", "pc20"], ["pc21"])
    lin(col(22), col(2), 1 / 16, col(20), ["pcf", "pc20"], ["pc22"])
    ts(T.sl[:, 0:6:2], T.cc[:, 0:96:32], col(21), A.add, ["cc", "pc21"], ["sl0"])
    ts(T.sl[:, 1:7:2], T.cc[:, 96:120:8], col(22), A.add, ["cc", "pc22"], ["sl1"])
    cp(T.src[:].indirect(T.sl[:, 0:6]), T.dg[:], ["sl0", "sl1", "dg0", "dg1", "dg2"], ["src"], 96 * 4)
    for b in range(2):
        for k in range(8 * b, 8 * b + 8):
            mm(T.tp[:, 128 * k:128 * k + 128], T.src[:, 128 * k:128 * k + 128], T.idn[:], True, True, ["src", "idn"], ["t%d" % b], 128)
        cp(T.wk[:, b * UNIT:(b + 1) * UNIT], T.tp[:, b * UNIT:(b + 1) * UNIT], ["t%d" % b], ["wk%d" % b], UNIT, True)
    for h in range(2):
        sides(1, h)
    ts(T.ee[:], T.cm[:], col(1), A.is_equal, ["cm", "pcf"], ["ee"], c=128)
    keep(T.el[:], T.ee[:], [[16, 8], [0, 16]], 0, -1, ["ee", "hp"], ["el"])
    scaled(T.id2[:], T.idf[:], GONE, ["idf"], ["id2"])
    ts(T.idh[:], T.idf[:], -1.0, A.mult, ["idf"], ["idh"], c=128)
    for j, n in enumerate(plain):
        keep(T.idc[:, 128 * j:128 * j + 128], T.idf[:], [[0, 8], [1, 16]], n - 15, 0, ["idf", "nf"], ["idc%d" % j])
    ts(T.rcn[:], T.rci[:], -1.0, A.mult, ["rci"], ["rcn"])
    cp(T.tot1[:, 4 * r:4 * r + 1], T.pp[:, S:S + 1], ["pp1"], ["tot1.own"], 64, True)
    starts(lambda a, b: T.tot1[:, 4 * a:4 * b:4], ["tot1", "tot1.own"], -1.0)
    cp(T.w1[:, O:W:S], T.base[:, 0:N], ["base"], ["w1.col0", "w1.z"])
    for d in range(1, N):
        q = (r - d) % N
        op({"v": (lambda q=q: v.tensor_tensor_scan(T.w1[:, q * S + O + 1:(q + 1) * S + O], T.szl[:, q * S:(q + 1) * S - 1], T.f3[:, 0:S - 1],
                                                   T.base[:, q:q + 1], A.add, A.mult), us(S))},
           ["szl%d" % q, "base", "f30", "f31"], ["w1.%d" % q])
    own_forms(1, 1, gcopy)
    ts(T.off[:], T.ofa[:], float(-O), A.add, ["ofa"], ["off"], c=S // 2)

    for t in range(1, RO + 1):
        far(t, 0)
        lengths(t, 0)
        far(t, 1)
        lengths(t, 1)
        if t < RO:
            bases(t + 1)
            rename(t + 1)
            shift[0] = P["after"]
            fold(t + 1)
            shift[0] = 0

    stage[0] = 1
    later = [q for q in range(N) if q > r]
    if later:
        masks, ne = share(off_e, len(later))
        trs = [transfer(topo, T.cores[d], masks[i], T.sem.tt4, T.base[:, 4:6], T.tot4[:, 2 * r:2 * r + 2]) for i, d in enumerate(later)]
        remote(trs, "lt4", ne * len(later), ["sum0", "sum1"], P["tot"])
    mm(T.c1[:, 0:2], T.el[:], T.base[:, 4:6], True, True, ["el", "sum0", "sum1"], ["c1", "own"], 256)
    if r > 0:
        i = op({"x": (None, 0.0)}, [], [], None, None, P["tot"], [len(ops) - 1])
        arrive("tt4", sum(share(off_e, N - 1 - q)[1] for q in range(r)), ["tot4"], [i])
    for h in range(2):
        marks(h, ["own"])
    cp(T.tt[:, 0:S], T.nf[:].indirect(T.ju3[:]), ["nf", "ju3"], ["tt.a"], S * G, True)
    dma("y", T.yj[:], T.tt[0:128:16, 0:S], ["tt.a"], [])
    if r > 0:
        mm(T.c1[:, 2:2 * r + 2], T.ee[:], T.tot4[:, 0:2 * r], True, True, ["ee", "tot4"], ["c1"], 256)
    op({"v": (lambda: v.tensor_reduce(T.base[:, 0:1], T.c1[:, 0:2 * r + 2], AxisListType.X, A.add), us(64))}, ["c1"], ["base"])
    for h in range(2):
        hf = slice(h * S // 2, (h + 1) * S // 2)
        rd, wr = ["pp0", "pp1", "pp.z", "base"], ["dd0.%d" % h]
        out = T.dd[:, h * UNIT:h * UNIT + S // 2]
        if h == 0:
            ts(out, T.pp[:, hf], -1.0, A.mult, rd, wr, T.base[:, 0:1], A.add, S // 2)
        else:
            act(out, T.pp[:, hf], Act.Identity, rd, wr, S // 2, bias=T.base[:, 0:1], scale=-1.0)
        dma("y" if h == 0 else "s", T.ya[:, hf], out, wr, [])
    emit(g, T, ops)
